import numpy as np
import ml_dtypes


def mxq(x, axis, fmt="e4m3"):
    dtype, down = {"e4m3": (ml_dtypes.float8_e4m3fn, 7), "e5m2": (ml_dtypes.float8_e5m2, 14)}[fmt]
    v = np.moveaxis(np.asarray(x, np.float32).astype(ml_dtypes.bfloat16).astype(np.float64), axis, -1)
    blocks = v.reshape(v.shape[:-1] + (-1, 32))
    amax = np.abs(blocks).max(-1, keepdims=True)
    byte = np.maximum(np.where(amax > 0, np.frexp(amax)[1] - 1 + 127, 0) - down, 1)
    scale = np.exp2(byte - 127.0)
    codes = (blocks / scale).astype(np.float32).astype(dtype).astype(np.float64)
    return np.moveaxis((codes * scale).reshape(v.shape), -1, axis)


WIDE = False


def mx_kscale(k):
    if not WIDE:
        return np.ones(k)
    levels = np.array([18, -18])
    if k % 512:
        return np.exp2(np.random.permutation(np.resize(levels, k // 32))).repeat(32)
    a = np.empty((k // 512, 16))
    for p in range(k // 512):
        a[p, :8] = np.random.permutation(np.resize(levels, 8))
        for g in range(8):
            far = levels[np.abs(levels - a[p, g]) >= 10]
            a[p, g + 8] = far[np.random.randint(len(far))]
    return np.exp2(a.ravel()).repeat(32)


def f64(x):
    return np.asarray(x).astype(np.float64)


def striped(idx):
    return np.tile(np.asarray(idx).reshape(-1, 16).T, (8, 1)).astype(np.uint16)


def unstriped(offs):
    return offs[:16].T.reshape(-1).astype(np.int64)


B, N, T, D, R = 2, 512, 2048, 512, 512


def setup_inputs():
    n = np.random.standard_normal
    idx = np.random.permutation(T)[:B * N]
    s = mx_kscale(D)[:, None]
    u = np.ones(T)
    u[idx] = mx_kscale(B * N)
    r = np.random.uniform(0.5, 2.0, T) * u
    x = n((B, D, R))
    return {
        "xT": (x * s).astype(np.float32),
        "wT": (n((D, T)) * (1.00 / np.sqrt(D)) / s / r).astype(np.float32),
        "y": np.random.randint(0, 2, (B, R, N)).astype(np.float32),
        "wt": (np.random.uniform(0.5, 1.5, (B, R, 1)) * 1.0 / np.sqrt(R)).astype(np.float32),
        "ts": np.tile(r, (128, 1)).astype(np.float32),
        "offs": striped(idx),
    }


def reference(xT, wT, y, wt, ts, offs):
    idx = unstriped(offs)
    pick = lambda x: x[:, idx].reshape(x.shape[0], B, N).transpose(1, 0, 2)
    w = pick(f64(wT))
    a = mxq(f64(xT), 1, "e4m3").transpose(0, 2, 1) @ mxq(w, 1, "e4m3")
    ts_ = pick(f64(ts))[:, :1, :]
    a = a * ts_
    p = 1.0 / (1.0 + np.exp(-a))
    g = f64(wt) * (p - f64(y)) * p * (1.0 - p)
    g = g * ts_
    gx = mxq(g, 2, "e5m2") @ mxq(w, 2, "e4m3").transpose(0, 2, 1)
    return gx

@@ -1,0 +1,307 @@
+from contextlib import ExitStack
+
+import concourse.mybir as mybir
+from concourse.masks import make_identity
+
+B, N, T, D, R = 2, 512, 2048, 512, 512
+FLOPS = 2 * 2 * B * R * N * D
+BYTES = 4 * (B * D * R + D * T + B * R * N + B * R + T + B * R * D) + 2 * 128 * B * N // 16
+
+F32 = mybir.dt.float32
+BF16 = mybir.dt.bfloat16
+U32 = mybir.dt.uint32
+U16 = mybir.dt.uint16
+U8 = mybir.dt.uint8
+E4M3 = mybir.dt.float8_e4m3fn_x4
+E5M2 = mybir.dt.float8_e5m2_x4
+ACT = mybir.ActivationFunctionType
+ALU = mybir.AluOpType
+
+P = 128
+PACK = 4
+ROWS = 256
+HALVES = R // ROWS
+TILES = ROWS // P
+LIST_COLS = N // 16
+
+
+def tile_attend_gsl2_x_ts_kernel(tc, xT, wT, y, wt, ts, offs, out):
+    nc = tc.nc
+    with ExitStack() as ctx:
+        keep = ctx.enter_context(tc.tile_pool(name="keep", bufs=1))
+        work = ctx.enter_context(tc.tile_pool(name="work", bufs=2))
+        psum = ctx.enter_context(tc.psum_pool(name="psum", bufs=2))
+        units = [(b, hf) for b in range(B) for hf in range(HALVES)]
+
+        offsets = keep.tile([P, B * LIST_COLS], U16, name="offsets")
+        nc.sync.dma_start(offsets[:], offs)
+        ts_table = keep.tile([P, T], F32, name="ts_table")
+        nc.vector.memset(ts_table[:], 0.0)
+        wt_rows = keep.tile([P, P], F32, name="wt_rows")
+        nc.vector.memset(wt_rows[:], 0.0)
+        planes, x_raw, y_raw = {}, {}, {}
+
+        def load_plane(t):
+            planes[t] = keep.tile([P, T], F32, name=f"plane{t}")
+            nc.sync.dma_start(planes[t][:], wT.rearrange("(p t) c -> p t c", t=PACK)[:, t, :])
+
+        def load_x(u):
+            b, hf = u
+            x_raw[u] = keep.tile([P, PACK, ROWS], F32, name=f"x_raw{b}{hf}")
+            nc.sync.dma_start(x_raw[u][:], xT[b].rearrange("(p t) r -> p t r", t=PACK)[:, :, hf * ROWS : (hf + 1) * ROWS])
+
+        def load_y(u):
+            b, hf = u
+            y_raw[u] = keep.tile([P, TILES, N], F32, name=f"y_raw{b}{hf}")
+            nc.sync.dma_start(y_raw[u][:], y[b, hf * ROWS : (hf + 1) * ROWS, :].rearrange("(j n) i -> n j i", n=P))
+
+        load_plane(0)
+        nc.scalar.dma_start(ts_table[0:1, :], ts[0:1, :])
+        nc.sync.dma_start(wt_rows[0 : B * R // P, :], wt.rearrange("b (j n) o -> (b j) (n o)", n=P))
+        load_x(units[0])
+        load_plane(1)
+        load_plane(2)
+        load_plane(3)
+        load_x(units[1])
+        load_y(units[0])
+        load_y(units[1])
+        for u in units[2:]:
+            load_x(u)
+            load_y(u)
+
+        ident = keep.tile([P, P], F32, name="ident")
+        nc.vector.memset(ident[:], 0.0)
+        make_identity(nc, ident[:], nomemset=True)
+        half = keep.tile([P, 1], F32, name="half")
+        nc.scalar.activation(half[:], ident[:, 0:1], ACT.Sigmoid, scale=0.0)
+
+        def group_list(b):
+            return offsets[:, b * LIST_COLS : (b + 1) * LIST_COLS]
+
+        wt_spread = []
+
+        def spread_weights():
+            turned = psum.tile([P, N], F32, name="turned", tag="misc")
+            nc.tensor.transpose(turned[:, 0:P], wt_rows[:], ident[:])
+            wt_cols = keep.tile([P, B * R // P], F32, name="wt_cols")
+            nc.scalar.copy(wt_cols[:], turned[:, 0 : B * R // P])
+            for b in range(B):
+                bank = psum.tile([P, R], F32, name="wt_spread", tag="wt_spread")
+                for j in range(R // P):
+                    col = b * (R // P) + j
+                    nc.tensor.transpose(bank[:, j * P : (j + 1) * P], wt_cols[:, col : col + 1].to_broadcast([P, P]), ident[:])
+                wt_spread.append(bank)
+
+        ts_cols = {}
+
+        def gather_scales(b, tag):
+            picked = keep.tile([P, N], F32, name="ts_picked", tag=tag, align_bytes=64)
+            nc.vector.tensor_copy(picked[:], ts_table[:].indirect(group_list(b)))
+            turned = psum.tile([P, N], F32, name="turned", tag="misc")
+            for t in range(PACK):
+                nc.tensor.transpose(turned[:, t * P : (t + 1) * P], picked[:, t:N:PACK], ident[:])
+            cols = keep.tile([P, PACK], F32, name=f"ts_cols{b}")
+            nc.scalar.copy(cols[:], turned[:, 0:N:P])
+            ts_cols[b] = cols
+
+        picked_w = {}
+        w_slots = [keep.tile([P, PACK * D], BF16, name=f"w_slots{b}", align_bytes=64) for b in range(B)]
+
+        def gather(b, t):
+            a, e = divmod(t, 2)
+            if e == 0:
+                tag = "picked_late" if a == 1 else f"picked_early{b}"
+                picked_w[b, a] = keep.tile([P, 2 * N], BF16, name="picked_w", tag=tag, align_bytes=64)
+            nc.vector.tensor_copy(picked_w[b, a][:, e * N : (e + 1) * N], planes[t][:].indirect(group_list(b)))
+
+        def turn(b, a, tag="misc"):
+            words = picked_w[b, a][:].bitcast(F32)
+            turned = psum.tile([P, N], F32, name="turned", tag=tag)
+            for e in range(2):
+                for v in range(2):
+                    nc.tensor.transpose(
+                        turned[:, (2 * e + v) * P : (2 * e + v + 1) * P],
+                        words[:, e * N // 2 + v : (e + 1) * N // 2 : 2],
+                        ident[:],
+                    )
+            nc.scalar.copy(
+                w_slots[b][:].bitcast(F32).rearrange("s (p t v) -> s p t v", t=PACK, v=2)[:, :, 2 * a : 2 * a + 2, :],
+                turned[:].rearrange("s (e v p) -> s p e v", e=2, v=2),
+            )
+
+        def quantise(src, cols, fmt, name):
+            codes = keep.tile([P, cols], U32, name=name + "_codes", align_bytes=64)
+            scales = keep.tile([P, cols], U8, name=name + "_scales", align_bytes=64)
+            nc.vector.quantize_mx(out=codes[:].bitcast(fmt), scales=scales[:], in_=src)
+            return codes, scales
+
+        w_feat_q, w_slot_q, x_q = {}, {}, {}
+
+        w_feats = [keep.tile([P, PACK * N], BF16, name="w_feats", tag=f"w_feats{b}", align_bytes=64) for b in range(B)]
+
+        def weave(b, a, copy):
+            copy(
+                w_feats[b][:].rearrange("p (r s t) -> p s t r", r=PACK, t=PACK)[:, :, 2 * a : 2 * a + 2, :],
+                picked_w[b, a][:].rearrange("p (e s r) -> p s e r", e=2, r=PACK),
+            )
+
+        def prepare_features(b):
+            w_feat_q[b] = quantise(w_feats[b][:], N, E4M3, f"w_feat{b}")
+
+        def prepare_slots(b):
+            w_slot_q[b] = quantise(w_slots[b][:], D, E4M3, f"w_slot{b}")
+
+        def prepare_x(u):
+            woven = work.tile([P, PACK * ROWS], BF16, name="x_woven", align_bytes=64)
+            nc.scalar.copy(
+                woven[:].rearrange("p (c i t) -> p c t i", i=4, t=PACK),
+                x_raw[u][:].rearrange("p t (c i) -> p c t i", i=4),
+            )
+            x_q[u] = quantise(woven[:], ROWS, E4M3, f"x{u[0]}{u[1]}")
+
+        score_banks, y_banks, probs, grads = {}, {}, {}, {}
+
+        def scores(u):
+            b = u[0]
+            w_codes, w_scales = w_feat_q[b]
+            x_codes, x_scales = x_q[u]
+            score_banks[u] = []
+            for a in range(2):
+                bank = psum.tile([P, 2 * ROWS], F32, name="score", tag="score")
+                for e in range(2):
+                    cols = slice((2 * a + e) * P, (2 * a + e + 1) * P)
+                    nc.tensor.matmul_mx(
+                        out=bank[:, e * ROWS : (e + 1) * ROWS],
+                        lhsT=w_codes[:, cols].bitcast(E4M3),
+                        lhsT_scale=w_scales[:, cols],
+                        rhs=x_codes[:].bitcast(E4M3),
+                        rhs_scale=x_scales[:],
+                        start=True,
+                        stop=True,
+                    )
+                score_banks[u].append(bank)
+
+        def turn_y(u):
+            y_banks[u] = []
+            for a in range(2):
+                bank = psum.tile([P, 2 * ROWS], F32, name="y_turned", tag="y_turned")
+                for e in range(2):
+                    for j in range(TILES):
+                        at = e * ROWS + j * P
+                        nc.tensor.transpose(bank[:, at : at + P], y_raw[u][:, j, 2 * a + e : N : PACK], ident[:])
+                y_banks[u].append(bank)
+
+        def weigh(u):
+            b, hf = u
+            prob = work.tile([P, PACK * ROWS], F32, name="prob")
+            square = work.tile([P, PACK * ROWS], F32, name="square")
+            for t in range(PACK):
+                nc.scalar.activation(
+                    prob[:, t * ROWS : (t + 1) * ROWS],
+                    score_banks[u][t // 2][:, (t % 2) * ROWS : (t % 2 + 1) * ROWS],
+                    ACT.Sigmoid,
+                    scale=ts_cols[b][:, t : t + 1],
+                )
+            nc.scalar.activation(
+                square[:].rearrange("p (c i t) -> p c t i", i=4, t=PACK),
+                prob[:].rearrange("p (t c i) -> p c t i", i=4, t=PACK),
+                ACT.Square,
+                bias=half[:],
+                scale=-1.0,
+            )
+            probs[u] = (prob, square)
+
+        def scale_miss(u):
+            b, hf = u
+            prob, square = probs[u]
+            miss = work.tile([P, PACK * ROWS], F32, name="miss")
+            scaled = work.tile([P, PACK * ROWS], F32, name="scaled")
+            for a in range(2):
+                cols = slice(2 * a * ROWS, 2 * (a + 1) * ROWS)
+                nc.vector.tensor_tensor(miss[:, cols], y_banks[u][a][:], prob[:, cols], ALU.subtract)
+            for t in range(PACK):
+                cols = slice(t * ROWS, (t + 1) * ROWS)
+                nc.vector.scalar_tensor_tensor(
+                    scaled[:, cols], miss[:, cols], ts_cols[b][:, t : t + 1],
+                    wt_spread[b][:, hf * ROWS : (hf + 1) * ROWS], ALU.mult, ALU.mult,
+                )
+            grads[u] = (square, scaled)
+
+        def finish(u, pieces):
+            b, hf = u
+            square, scaled = grads[u]
+            w_codes, w_scales = w_slot_q[b]
+            rows = ROWS // pieces
+            quantised = []
+            for k in range(pieces):
+                h = work.tile([P, PACK * rows], BF16, name="h", align_bytes=64)
+                nc.vector.scalar_tensor_tensor(
+                    h[:].rearrange("p (r t) -> p r t", t=PACK),
+                    square[:].rearrange("p (r t) -> p r t", t=PACK)[:, k * rows : (k + 1) * rows, :],
+                    -0.25,
+                    scaled[:].rearrange("p (t r) -> p r t", t=PACK)[:, k * rows : (k + 1) * rows, :],
+                    ALU.add,
+                    ALU.mult,
+                )
+                quantised.append(quantise(h[:], rows, E5M2, f"h{b}{hf}{k}"))
+            for j in range(TILES):
+                h_codes, h_scales = quantised[j * P // rows]
+                cols = slice(j * P % rows, j * P % rows + P)
+                bank = psum.tile([P, D], F32, name="result", tag="misc")
+                nc.tensor.matmul_mx(
+                    out=bank[:],
+                    lhsT=h_codes[:, cols].bitcast(E5M2),
+                    lhsT_scale=h_scales[:, cols],
+                    rhs=w_codes[:].bitcast(E4M3),
+                    rhs_scale=w_scales[:],
+                    start=True,
+                    stop=True,
+                )
+                staged = work.tile([P, D], F32, name="staged", bufs=4)
+                nc.scalar.copy(staged[:], bank[:])
+                first = hf * ROWS + j * P
+                nc.sync.dma_start(out[b, first : first + P, :], staged[:])
+
+        gather_scales(0, "ts_picked0")
+        gather(0, 0)
+        prepare_x(units[0])
+        spread_weights()
+        gather_scales(1, "ts_picked1")
+        gather(1, 0)
+        gather(0, 1)
+        weave(0, 0, nc.scalar.copy)
+        gather(1, 1)
+        turn(0, 0)
+        turn(1, 0)
+        weave(1, 0, nc.scalar.copy)
+        gather(0, 2)
+        gather(0, 3)
+        weave(0, 1, nc.vector.tensor_copy)
+        prepare_features(0)
+        scores(units[0])
+        turn_y(units[0])
+        turn(0, 1)
+        gather(1, 2)
+        gather(1, 3)
+        prepare_x(units[1])
+        prepare_slots(0)
+        weigh(units[0])
+        scores(units[1])
+        scale_miss(units[0])
+        turn(1, 1, "y_turned")
+        turn_y(units[1])
+        weave(1, 1, nc.vector.tensor_copy)
+        prepare_features(1)
+        prepare_x(units[2])
+        prepare_slots(1)
+        for k in range(1, len(units)):
+            weigh(units[k])
+            if k + 1 < len(units):
+                scores(units[k + 1])
+            finish(units[k - 1], 1)
+            scale_miss(units[k])
+            if k + 1 < len(units):
+                turn_y(units[k + 1])
+            if k + 2 < len(units):
+                prepare_x(units[k + 2])
+        finish(units[-1], TILES)

@@ -22,6 +22,7 @@ PACK = 4
 ROWS = 256
 HALVES = R // ROWS
 TILES = ROWS // P
+LINE = 4
 LIST_COLS = N // 16
 
 
@@ -36,7 +37,8 @@ def tile_attend_gsl2_x_ts_kernel(tc, xT, wT, y, wt, ts, offs, out):
         offsets = keep.tile([P, B * LIST_COLS], U16, name="offsets")
         nc.sync.dma_start(offsets[:], offs)
         ts_table = keep.tile([P, T], F32, name="ts_table")
-        nc.vector.memset(ts_table[:], 0.0)
+        nc.gpsimd.memset(ts_table[:, T // 2 :], 0.0)
+        nc.vector.memset(ts_table[:, : T // 2], 0.0)
         wt_rows = keep.tile([P, P], F32, name="wt_rows")
         nc.vector.memset(wt_rows[:], 0.0)
         planes, x_raw, y_raw = {}, {}, {}
@@ -104,24 +106,25 @@ def tile_attend_gsl2_x_ts_kernel(tc, xT, wT, y, wt, ts, offs, out):
             nc.scalar.copy(cols[:], turned[:, 0:N:P])
             ts_cols[b] = cols
 
-        picked_w = {}
+        picked_w = keep.tile([P, 7 * N], BF16, name="picked_w", align_bytes=64)
+
+        def place(b, t):
+            return 2 * t + (b if t < PACK - 1 else 0)
         w_slots = [keep.tile([P, PACK * D], BF16, name=f"w_slots{b}", align_bytes=64) for b in range(B)]
 
         def gather(b, t):
-            a, e = divmod(t, 2)
-            if e == 0:
-                tag = "picked_late" if a == 1 else f"picked_early{b}"
-                picked_w[b, a] = keep.tile([P, 2 * N], BF16, name="picked_w", tag=tag, align_bytes=64)
-            nc.vector.tensor_copy(picked_w[b, a][:, e * N : (e + 1) * N], planes[t][:].indirect(group_list(b)))
+            at = place(b, t) * N
+            nc.vector.tensor_copy(picked_w[:, at : at + N], planes[t][:].indirect(group_list(b)))
 
         def turn(b, a, tag="misc"):
-            words = picked_w[b, a][:].bitcast(F32)
+            words = picked_w[:].bitcast(F32)
             turned = psum.tile([P, N], F32, name="turned", tag=tag)
             for e in range(2):
+                at = place(b, 2 * a + e) * N // 2
                 for v in range(2):
                     nc.tensor.transpose(
                         turned[:, (2 * e + v) * P : (2 * e + v + 1) * P],
-                        words[:, e * N // 2 + v : (e + 1) * N // 2 : 2],
+                        words[:, at + v : at + N // 2 : 2],
                         ident[:],
                     )
             nc.scalar.copy(
@@ -140,9 +143,10 @@ def tile_attend_gsl2_x_ts_kernel(tc, xT, wT, y, wt, ts, offs, out):
         w_feats = [keep.tile([P, PACK * N], BF16, name="w_feats", tag=f"w_feats{b}", align_bytes=64) for b in range(B)]
 
         def weave(b, a, copy):
+            first, second = place(b, 2 * a), place(b, 2 * a + 1)
             copy(
                 w_feats[b][:].rearrange("p (r s t) -> p s t r", r=PACK, t=PACK)[:, :, 2 * a : 2 * a + 2, :],
-                picked_w[b, a][:].rearrange("p (e s r) -> p s e r", e=2, r=PACK),
+                picked_w[:].rearrange("p (e s r) -> p s e r", s=P, r=PACK)[:, :, first : second + 1 : second - first, :],
             )
 
         def prepare_features(b):
@@ -191,24 +195,24 @@ def tile_attend_gsl2_x_ts_kernel(tc, xT, wT, y, wt, ts, offs, out):
                         nc.tensor.transpose(bank[:, at : at + P], y_raw[u][:, j, 2 * a + e : N : PACK], ident[:])
                 y_banks[u].append(bank)
 
+        def lines(tile):
+            return tile[:].rearrange("p (c t i) -> p c t i", t=PACK, i=LINE)
+
+        def dealt(bank_cols):
+            return bank_cols.rearrange("p (i c) -> p c i", i=LINE)
+
         def weigh(u):
             b, hf = u
             prob = work.tile([P, PACK * ROWS], F32, name="prob")
             square = work.tile([P, PACK * ROWS], F32, name="square")
             for t in range(PACK):
                 nc.scalar.activation(
-                    prob[:, t * ROWS : (t + 1) * ROWS],
-                    score_banks[u][t // 2][:, (t % 2) * ROWS : (t % 2 + 1) * ROWS],
+                    lines(prob)[:, :, t, :],
+                    dealt(score_banks[u][t // 2][:, (t % 2) * ROWS : (t % 2 + 1) * ROWS]),
                     ACT.Sigmoid,
                     scale=ts_cols[b][:, t : t + 1],
                 )
-            nc.scalar.activation(
-                square[:].rearrange("p (c i t) -> p c t i", i=4, t=PACK),
-                prob[:].rearrange("p (t c i) -> p c t i", i=4, t=PACK),
-                ACT.Square,
-                bias=half[:],
-                scale=-1.0,
-            )
+            nc.scalar.activation(square[:], prob[:], ACT.Square, bias=half[:], scale=-1.0)
             probs[u] = (prob, square)
 
         def scale_miss(u):
@@ -217,13 +221,16 @@ def tile_attend_gsl2_x_ts_kernel(tc, xT, wT, y, wt, ts, offs, out):
             miss = work.tile([P, PACK * ROWS], F32, name="miss")
             scaled = work.tile([P, PACK * ROWS], F32, name="scaled")
             for a in range(2):
-                cols = slice(2 * a * ROWS, 2 * (a + 1) * ROWS)
-                nc.vector.tensor_tensor(miss[:, cols], y_banks[u][a][:], prob[:, cols], ALU.subtract)
+                nc.vector.tensor_tensor(
+                    lines(miss)[:, :, 2 * a : 2 * a + 2, :],
+                    y_banks[u][a][:].rearrange("p (e i c) -> p c e i", e=2, i=LINE),
+                    lines(prob)[:, :, 2 * a : 2 * a + 2, :],
+                    ALU.subtract,
+                )
             for t in range(PACK):
-                cols = slice(t * ROWS, (t + 1) * ROWS)
                 nc.vector.scalar_tensor_tensor(
-                    scaled[:, cols], miss[:, cols], ts_cols[b][:, t : t + 1],
-                    wt_spread[b][:, hf * ROWS : (hf + 1) * ROWS], ALU.mult, ALU.mult,
+                    lines(scaled)[:, :, t, :], lines(miss)[:, :, t, :], ts_cols[b][:, t : t + 1],
+                    dealt(wt_spread[b][:, hf * ROWS : (hf + 1) * ROWS]), ALU.mult, ALU.mult,
                 )
             grads[u] = (square, scaled)
 
@@ -232,14 +239,15 @@ def tile_attend_gsl2_x_ts_kernel(tc, xT, wT, y, wt, ts, offs, out):
             square, scaled = grads[u]
             w_codes, w_scales = w_slot_q[b]
             rows = ROWS // pieces
+            runs = LINE // pieces
             quantised = []
             for k in range(pieces):
                 h = work.tile([P, PACK * rows], BF16, name="h", align_bytes=64)
                 nc.vector.scalar_tensor_tensor(
-                    h[:].rearrange("p (r t) -> p r t", t=PACK),
-                    square[:].rearrange("p (r t) -> p r t", t=PACK)[:, k * rows : (k + 1) * rows, :],
+                    h[:].rearrange("p (i m) -> p m i", i=runs),
+                    square[:].rearrange("p (m i) -> p m i", i=LINE)[:, :, k * runs : (k + 1) * runs],
                     -0.25,
-                    scaled[:].rearrange("p (t r) -> p r t", t=PACK)[:, k * rows : (k + 1) * rows, :],
+                    scaled[:].rearrange("p (m i) -> p m i", i=LINE)[:, :, k * runs : (k + 1) * runs],
                     ALU.add,
                     ALU.mult,
                 )
@@ -275,13 +283,13 @@ def tile_attend_gsl2_x_ts_kernel(tc, xT, wT, y, wt, ts, offs, out):
         turn(1, 0)
         weave(1, 0, nc.scalar.copy)
         gather(0, 2)
+        gather(1, 2)
         gather(0, 3)
         weave(0, 1, nc.vector.tensor_copy)
         prepare_features(0)
         scores(units[0])
         turn_y(units[0])
         turn(0, 1)
-        gather(1, 2)
         gather(1, 3)
         prepare_x(units[1])
         prepare_slots(0)
@@ -290,7 +298,7 @@ def tile_attend_gsl2_x_ts_kernel(tc, xT, wT, y, wt, ts, offs, out):
         scale_miss(units[0])
         turn(1, 1, "y_turned")
         turn_y(units[1])
-        weave(1, 1, nc.vector.tensor_copy)
+        weave(1, 1, nc.scalar.copy)
         prepare_features(1)
         prepare_x(units[2])
         prepare_slots(1)

@@ -36,7 +36,7 @@ def tile_attend_gsl2_x_ts_kernel(tc, xT, wT, y, wt, ts, offs, out):
 
         offsets = keep.tile([P, B * LIST_COLS], U16, name="offsets")
         nc.sync.dma_start(offsets[:], offs)
-        ts_table = keep.tile([P, T], F32, name="ts_table")
+        ts_table = keep.tile([P, T], F32, name="ts_table", align_bytes=64)
         nc.gpsimd.memset(ts_table[:, T // 2 :], 0.0)
         nc.vector.memset(ts_table[:, : T // 2], 0.0)
         wt_rows = keep.tile([P, P], F32, name="wt_rows")
@@ -64,8 +64,8 @@ def tile_attend_gsl2_x_ts_kernel(tc, xT, wT, y, wt, ts, offs, out):
         load_plane(1)
         load_plane(2)
         load_plane(3)
-        load_x(units[1])
         load_y(units[0])
+        load_x(units[1])
         load_y(units[1])
         for u in units[2:]:
             load_x(u)
@@ -106,7 +106,7 @@ def tile_attend_gsl2_x_ts_kernel(tc, xT, wT, y, wt, ts, offs, out):
             nc.scalar.copy(cols[:], turned[:, 0:N:P])
             ts_cols[b] = cols
 
-        picked_w = keep.tile([P, 7 * N], BF16, name="picked_w", align_bytes=64)
+        picked_w = keep.tile([P, 7 * N], BF16, name="picked_w", tag="ts_table", align_bytes=64)
 
         def place(b, t):
             return 2 * t + (b if t < PACK - 1 else 0)
@@ -212,7 +212,14 @@ def tile_attend_gsl2_x_ts_kernel(tc, xT, wT, y, wt, ts, offs, out):
                     ACT.Sigmoid,
                     scale=ts_cols[b][:, t : t + 1],
                 )
-            nc.scalar.activation(square[:], prob[:], ACT.Square, bias=half[:], scale=-1.0)
+            for a in range(2):
+                nc.scalar.activation(
+                    lines(square)[:, :, 2 * a : 2 * a + 2, :],
+                    lines(prob)[:, :, 2 * a : 2 * a + 2, :],
+                    ACT.Square,
+                    bias=half[:],
+                    scale=-1.0,
+                )
             probs[u] = (prob, square)
 
         def scale_miss(u):
@@ -266,16 +273,17 @@ def tile_attend_gsl2_x_ts_kernel(tc, xT, wT, y, wt, ts, offs, out):
                     stop=True,
                 )
                 staged = work.tile([P, D], F32, name="staged", bufs=4)
-                nc.scalar.copy(staged[:], bank[:])
+                last = u == units[-1] and j == TILES - 1
+                (nc.vector.tensor_copy if last else nc.scalar.copy)(staged[:], bank[:])
                 first = hf * ROWS + j * P
                 nc.sync.dma_start(out[b, first : first + P, :], staged[:])
 
         gather_scales(0, "ts_picked0")
         gather(0, 0)
-        prepare_x(units[0])
         spread_weights()
         gather_scales(1, "ts_picked1")
         gather(1, 0)
+        prepare_x(units[0])
         gather(0, 1)
         weave(0, 0, nc.scalar.copy)
         gather(1, 1)
@@ -296,9 +304,9 @@ def tile_attend_gsl2_x_ts_kernel(tc, xT, wT, y, wt, ts, offs, out):
         weigh(units[0])
         scores(units[1])
         scale_miss(units[0])
-        turn(1, 1, "y_turned")
+        turn(1, 1)
         turn_y(units[1])
-        weave(1, 1, nc.scalar.copy)
+        weave(1, 1, nc.vector.tensor_copy)
         prepare_features(1)
         prepare_x(units[2])
         prepare_slots(1)

@@ -23,6 +23,7 @@ ROWS = 256
 HALVES = R // ROWS
 TILES = ROWS // P
 LINE = 4
+SCALAR_PLANE = 0
 LIST_COLS = N // 16
 
 
@@ -36,7 +37,7 @@ def tile_attend_gsl2_x_ts_kernel(tc, xT, wT, y, wt, ts, offs, out):
 
         offsets = keep.tile([P, B * LIST_COLS], U16, name="offsets")
         nc.sync.dma_start(offsets[:], offs)
-        ts_table = keep.tile([P, T], F32, name="ts_table", align_bytes=64)
+        ts_table = keep.tile([P, T], F32, name="ts_table")
         nc.gpsimd.memset(ts_table[:, T // 2 :], 0.0)
         nc.vector.memset(ts_table[:, : T // 2], 0.0)
         wt_rows = keep.tile([P, P], F32, name="wt_rows")
@@ -58,12 +59,12 @@ def tile_attend_gsl2_x_ts_kernel(tc, xT, wT, y, wt, ts, offs, out):
             nc.sync.dma_start(y_raw[u][:], y[b, hf * ROWS : (hf + 1) * ROWS, :].rearrange("(j n) i -> n j i", n=P))
 
         load_plane(0)
-        nc.scalar.dma_start(ts_table[0:1, :], ts[0:1, :])
+        nc.sync.dma_start(ts_table[0:1, :], ts[0:1, :])
         nc.sync.dma_start(wt_rows[0 : B * R // P, :], wt.rearrange("b (j n) o -> (b j) (n o)", n=P))
-        load_x(units[0])
         load_plane(1)
         load_plane(2)
         load_plane(3)
+        load_x(units[0])
         load_y(units[0])
         load_x(units[1])
         load_y(units[1])
@@ -77,48 +78,56 @@ def tile_attend_gsl2_x_ts_kernel(tc, xT, wT, y, wt, ts, offs, out):
         half = keep.tile([P, 1], F32, name="half")
         nc.scalar.activation(half[:], ident[:, 0:1], ACT.Sigmoid, scale=0.0)
 
-        def group_list(b):
-            return offsets[:, b * LIST_COLS : (b + 1) * LIST_COLS]
-
         wt_spread = []
 
         def spread_weights():
-            turned = psum.tile([P, N], F32, name="turned", tag="misc")
+            turned = psum.tile([P, N], F32, name="turned", tag="misc", bufs=2)
             nc.tensor.transpose(turned[:, 0:P], wt_rows[:], ident[:])
             wt_cols = keep.tile([P, B * R // P], F32, name="wt_cols")
             nc.scalar.copy(wt_cols[:], turned[:, 0 : B * R // P])
             for b in range(B):
-                bank = psum.tile([P, R], F32, name="wt_spread", tag="wt_spread")
+                bank = psum.tile([P, R], F32, name="wt_spread", tag="misc", bufs=2)
                 for j in range(R // P):
                     col = b * (R // P) + j
                     nc.tensor.transpose(bank[:, j * P : (j + 1) * P], wt_cols[:, col : col + 1].to_broadcast([P, P]), ident[:])
-                wt_spread.append(bank)
+                spread = keep.tile([P, R], F32, name=f"wt_spread{b}")
+                nc.scalar.copy(
+                    spread[:].rearrange("p (h c i) -> p h c i", h=HALVES, i=LINE),
+                    bank[:].rearrange("p (h i c) -> p h c i", h=HALVES, i=LINE),
+                )
+                wt_spread.append(spread)
 
         ts_cols = {}
 
-        def gather_scales(b, tag):
-            picked = keep.tile([P, N], F32, name="ts_picked", tag=tag, align_bytes=64)
-            nc.vector.tensor_copy(picked[:], ts_table[:].indirect(group_list(b)))
-            turned = psum.tile([P, N], F32, name="turned", tag="misc")
+        ts_picked = keep.tile([P, B * N], F32, name="ts_picked")
+
+        def turn_scales(b):
+            picked = ts_picked[:, b * N : (b + 1) * N]
+            turned = psum.tile([P, N], F32, name="turned", tag="misc", bufs=2)
             for t in range(PACK):
                 nc.tensor.transpose(turned[:, t * P : (t + 1) * P], picked[:, t:N:PACK], ident[:])
             cols = keep.tile([P, PACK], F32, name=f"ts_cols{b}")
             nc.scalar.copy(cols[:], turned[:, 0:N:P])
             ts_cols[b] = cols
 
-        picked_w = keep.tile([P, 7 * N], BF16, name="picked_w", tag="ts_table", align_bytes=64)
+        picked_w = keep.tile([P, 8 * N], BF16, name="picked_w", align_bytes=64)
 
         def place(b, t):
-            return 2 * t + (b if t < PACK - 1 else 0)
+            return B * t + b
         w_slots = [keep.tile([P, PACK * D], BF16, name=f"w_slots{b}", align_bytes=64) for b in range(B)]
 
-        def gather(b, t):
-            at = place(b, t) * N
-            nc.vector.tensor_copy(picked_w[:, at : at + N], planes[t][:].indirect(group_list(b)))
+        def gather(t):
+            picked = picked_w[:, t * B * N : (t + 1) * B * N]
+            if t == SCALAR_PLANE:
+                narrow = keep.tile([P, T], BF16, name="narrow")
+                nc.scalar.activation(narrow[:], planes[t][:], ACT.Copy)
+                nc.scalar.activation(picked, narrow[:].indirect(offsets[:]), ACT.Copy)
+            else:
+                nc.vector.tensor_copy(picked, planes[t][:].indirect(offsets[:]))
 
-        def turn(b, a, tag="misc"):
+        def turn(b, a):
             words = picked_w[:].bitcast(F32)
-            turned = psum.tile([P, N], F32, name="turned", tag=tag)
+            turned = psum.tile([P, N], F32, name="turned", tag="misc", bufs=2)
             for e in range(2):
                 at = place(b, 2 * a + e) * N // 2
                 for v in range(2):
@@ -142,11 +151,10 @@ def tile_attend_gsl2_x_ts_kernel(tc, xT, wT, y, wt, ts, offs, out):
 
         w_feats = [keep.tile([P, PACK * N], BF16, name="w_feats", tag=f"w_feats{b}", align_bytes=64) for b in range(B)]
 
-        def weave(b, a, copy):
-            first, second = place(b, 2 * a), place(b, 2 * a + 1)
+        def weave(b, copy, part=slice(0, P)):
             copy(
-                w_feats[b][:].rearrange("p (r s t) -> p s t r", r=PACK, t=PACK)[:, :, 2 * a : 2 * a + 2, :],
-                picked_w[:].rearrange("p (e s r) -> p s e r", s=P, r=PACK)[:, :, first : second + 1 : second - first, :],
+                w_feats[b][:].rearrange("p (r s t) -> p s t r", r=PACK, t=PACK)[:, part, :, :],
+                picked_w[:].rearrange("p (e s r) -> p s e r", s=P, r=PACK)[:, part, place(b, 0) : place(b, PACK - 1) + 1 : place(b, 1) - place(b, 0), :],
             )
 
         def prepare_features(b):
@@ -171,7 +179,7 @@ def tile_attend_gsl2_x_ts_kernel(tc, xT, wT, y, wt, ts, offs, out):
             x_codes, x_scales = x_q[u]
             score_banks[u] = []
             for a in range(2):
-                bank = psum.tile([P, 2 * ROWS], F32, name="score", tag="score")
+                bank = psum.tile([P, 2 * ROWS], F32, name="score", tag="score", bufs=2)
                 for e in range(2):
                     cols = slice((2 * a + e) * P, (2 * a + e + 1) * P)
                     nc.tensor.matmul_mx(
@@ -188,7 +196,7 @@ def tile_attend_gsl2_x_ts_kernel(tc, xT, wT, y, wt, ts, offs, out):
         def turn_y(u):
             y_banks[u] = []
             for a in range(2):
-                bank = psum.tile([P, 2 * ROWS], F32, name="y_turned", tag="y_turned")
+                bank = psum.tile([P, 2 * ROWS], F32, name="y_turned", tag="y_turned", bufs=4)
                 for e in range(2):
                     for j in range(TILES):
                         at = e * ROWS + j * P
@@ -237,7 +245,7 @@ def tile_attend_gsl2_x_ts_kernel(tc, xT, wT, y, wt, ts, offs, out):
             for t in range(PACK):
                 nc.vector.scalar_tensor_tensor(
                     lines(scaled)[:, :, t, :], lines(miss)[:, :, t, :], ts_cols[b][:, t : t + 1],
-                    dealt(wt_spread[b][:, hf * ROWS : (hf + 1) * ROWS]), ALU.mult, ALU.mult,
+                    wt_spread[b][:, hf * ROWS : (hf + 1) * ROWS].rearrange("p (c i) -> p c i", i=LINE), ALU.mult, ALU.mult,
                 )
             grads[u] = (square, scaled)
 
@@ -262,7 +270,7 @@ def tile_attend_gsl2_x_ts_kernel(tc, xT, wT, y, wt, ts, offs, out):
             for j in range(TILES):
                 h_codes, h_scales = quantised[j * P // rows]
                 cols = slice(j * P % rows, j * P % rows + P)
-                bank = psum.tile([P, D], F32, name="result", tag="misc")
+                bank = psum.tile([P, D], F32, name="result", tag="misc", bufs=2)
                 nc.tensor.matmul_mx(
                     out=bank[:],
                     lhsT=h_codes[:, cols].bitcast(E5M2),
@@ -278,27 +286,23 @@ def tile_attend_gsl2_x_ts_kernel(tc, xT, wT, y, wt, ts, offs, out):
                 first = hf * ROWS + j * P
                 nc.sync.dma_start(out[b, first : first + P, :], staged[:])
 
-        gather_scales(0, "ts_picked0")
-        gather(0, 0)
-        spread_weights()
-        gather_scales(1, "ts_picked1")
-        gather(1, 0)
+        gather(0)
+        nc.vector.tensor_copy(ts_picked[:], ts_table[:].indirect(offsets[:]))
+        turn_scales(0)
+        turn_scales(1)
         prepare_x(units[0])
-        gather(0, 1)
-        weave(0, 0, nc.scalar.copy)
-        gather(1, 1)
+        spread_weights()
+        gather(1)
         turn(0, 0)
         turn(1, 0)
-        weave(1, 0, nc.scalar.copy)
-        gather(0, 2)
-        gather(1, 2)
-        gather(0, 3)
-        weave(0, 1, nc.vector.tensor_copy)
+        gather(2)
+        gather(3)
+        weave(0, nc.vector.tensor_copy, slice(0, 96))
+        weave(0, nc.scalar.copy, slice(96, P))
         prepare_features(0)
         scores(units[0])
         turn_y(units[0])
         turn(0, 1)
-        gather(1, 3)
         prepare_x(units[1])
         prepare_slots(0)
         weigh(units[0])
@@ -306,7 +310,7 @@ def tile_attend_gsl2_x_ts_kernel(tc, xT, wT, y, wt, ts, offs, out):
         scale_miss(units[0])
         turn(1, 1)
         turn_y(units[1])
-        weave(1, 1, nc.vector.tensor_copy)
+        weave(1, nc.vector.tensor_copy)
         prepare_features(1)
         prepare_x(units[2])
         prepare_slots(1)

@@ -19,127 +19,62 @@ ALU = mybir.AluOpType
 
 P = 128
 PACK = 4
+PAIRS = PACK // 2
+BANK = 512
 ROWS = 256
-HALVES = R // ROWS
 TILES = ROWS // P
+UNITS = B * R // ROWS
 LINE = 4
+WT_COLS = B * R // P
 SCALAR_PLANE = 0
-LIST_COLS = N // 16
+VECTOR_SHARE = 80
 
 
 def tile_attend_gsl2_x_ts_kernel(tc, xT, wT, y, wt, ts, offs, out):
     nc = tc.nc
     with ExitStack() as ctx:
         keep = ctx.enter_context(tc.tile_pool(name="keep", bufs=1))
-        work = ctx.enter_context(tc.tile_pool(name="work", bufs=2))
-        psum = ctx.enter_context(tc.psum_pool(name="psum", bufs=2))
-        units = [(b, hf) for b in range(B) for hf in range(HALVES)]
+        work = ctx.enter_context(tc.tile_pool(name="work", bufs=3))
+        score_banks = ctx.enter_context(tc.psum_pool(name="score_banks", bufs=3))
+        y_banks = ctx.enter_context(tc.psum_pool(name="y_banks", bufs=3))
+        other_banks = ctx.enter_context(tc.psum_pool(name="other_banks", bufs=2))
 
-        offsets = keep.tile([P, B * LIST_COLS], U16, name="offsets")
+        def group(u):
+            return u * ROWS // R
+
+        def rows_of(u):
+            return slice(u * ROWS % R, u * ROWS % R + ROWS)
+
+        offsets = keep.tile([P, B * N // 16], U16, name="offsets")
         nc.sync.dma_start(offsets[:], offs)
         ts_table = keep.tile([P, T], F32, name="ts_table")
         nc.gpsimd.memset(ts_table[:, T // 2 :], 0.0)
         nc.vector.memset(ts_table[:, : T // 2], 0.0)
-        wt_rows = keep.tile([P, P], F32, name="wt_rows")
-        nc.vector.memset(wt_rows[:], 0.0)
-        planes, x_raw, y_raw = {}, {}, {}
-
-        def load_plane(t):
-            planes[t] = keep.tile([P, T], F32, name=f"plane{t}")
-            nc.sync.dma_start(planes[t][:], wT.rearrange("(p t) c -> p t c", t=PACK)[:, t, :])
-
-        def load_x(u):
-            b, hf = u
-            x_raw[u] = keep.tile([P, PACK, ROWS], F32, name=f"x_raw{b}{hf}")
-            nc.sync.dma_start(x_raw[u][:], xT[b].rearrange("(p t) r -> p t r", t=PACK)[:, :, hf * ROWS : (hf + 1) * ROWS])
-
-        def load_y(u):
-            b, hf = u
-            y_raw[u] = keep.tile([P, TILES, N], F32, name=f"y_raw{b}{hf}")
-            nc.sync.dma_start(y_raw[u][:], y[b, hf * ROWS : (hf + 1) * ROWS, :].rearrange("(j n) i -> n j i", n=P))
-
-        load_plane(0)
-        nc.sync.dma_start(ts_table[0:1, :], ts[0:1, :])
-        nc.sync.dma_start(wt_rows[0 : B * R // P, :], wt.rearrange("b (j n) o -> (b j) (n o)", n=P))
-        load_plane(1)
-        load_plane(2)
-        load_plane(3)
-        load_x(units[0])
-        load_y(units[0])
-        load_x(units[1])
-        load_y(units[1])
-        for u in units[2:]:
-            load_x(u)
-            load_y(u)
+        wt_cols = keep.tile([P, WT_COLS], F32, name="wt_cols")
+        nc.sync.dma_start(wt_cols[:], wt.rearrange("b (n j) o -> (b n) (j o)", j=WT_COLS))
+        planes = []
+        for t in range(PACK):
+            plane = keep.tile([P, T], F32, name=f"plane{t}")
+            nc.sync.dma_start(plane[:], wT.rearrange("(p t) c -> p t c", t=PACK)[:, t, :])
+            planes.append(plane)
+            if t == SCALAR_PLANE:
+                nc.sync.dma_start(ts_table[0:1, :], ts[0:1, :])
+        x_raw, y_raw = [], []
+        for u in range(UNITS):
+            x_unit = keep.tile([P, PACK, ROWS], F32, name=f"x_raw{u}")
+            nc.sync.dma_start(x_unit[:], xT[group(u)].rearrange("(p t) r -> p t r", t=PACK)[:, :, rows_of(u)])
+            x_raw.append(x_unit)
+            y_unit = keep.tile([P, TILES, N], F32, name=f"y_raw{u}")
+            nc.sync.dma_start(y_unit[:], y[group(u), rows_of(u), :].rearrange("(j n) i -> n j i", n=P))
+            y_raw.append(y_unit)
 
         ident = keep.tile([P, P], F32, name="ident")
-        nc.vector.memset(ident[:], 0.0)
-        make_identity(nc, ident[:], nomemset=True)
+        make_identity(nc, ident[:])
         half = keep.tile([P, 1], F32, name="half")
         nc.scalar.activation(half[:], ident[:, 0:1], ACT.Sigmoid, scale=0.0)
 
-        wt_spread = []
-
-        def spread_weights():
-            turned = psum.tile([P, N], F32, name="turned", tag="misc", bufs=2)
-            nc.tensor.transpose(turned[:, 0:P], wt_rows[:], ident[:])
-            wt_cols = keep.tile([P, B * R // P], F32, name="wt_cols")
-            nc.scalar.copy(wt_cols[:], turned[:, 0 : B * R // P])
-            for b in range(B):
-                bank = psum.tile([P, R], F32, name="wt_spread", tag="misc", bufs=2)
-                for j in range(R // P):
-                    col = b * (R // P) + j
-                    nc.tensor.transpose(bank[:, j * P : (j + 1) * P], wt_cols[:, col : col + 1].to_broadcast([P, P]), ident[:])
-                spread = keep.tile([P, R], F32, name=f"wt_spread{b}")
-                nc.scalar.copy(
-                    spread[:].rearrange("p (h c i) -> p h c i", h=HALVES, i=LINE),
-                    bank[:].rearrange("p (h i c) -> p h c i", h=HALVES, i=LINE),
-                )
-                wt_spread.append(spread)
-
-        ts_cols = {}
-
-        ts_picked = keep.tile([P, B * N], F32, name="ts_picked")
-
-        def turn_scales(b):
-            picked = ts_picked[:, b * N : (b + 1) * N]
-            turned = psum.tile([P, N], F32, name="turned", tag="misc", bufs=2)
-            for t in range(PACK):
-                nc.tensor.transpose(turned[:, t * P : (t + 1) * P], picked[:, t:N:PACK], ident[:])
-            cols = keep.tile([P, PACK], F32, name=f"ts_cols{b}")
-            nc.scalar.copy(cols[:], turned[:, 0:N:P])
-            ts_cols[b] = cols
-
-        picked_w = keep.tile([P, 8 * N], BF16, name="picked_w", align_bytes=64)
-
-        def place(b, t):
-            return B * t + b
-        w_slots = [keep.tile([P, PACK * D], BF16, name=f"w_slots{b}", align_bytes=64) for b in range(B)]
-
-        def gather(t):
-            picked = picked_w[:, t * B * N : (t + 1) * B * N]
-            if t == SCALAR_PLANE:
-                narrow = keep.tile([P, T], BF16, name="narrow")
-                nc.scalar.activation(narrow[:], planes[t][:], ACT.Copy)
-                nc.scalar.activation(picked, narrow[:].indirect(offsets[:]), ACT.Copy)
-            else:
-                nc.vector.tensor_copy(picked, planes[t][:].indirect(offsets[:]))
-
-        def turn(b, a):
-            words = picked_w[:].bitcast(F32)
-            turned = psum.tile([P, N], F32, name="turned", tag="misc", bufs=2)
-            for e in range(2):
-                at = place(b, 2 * a + e) * N // 2
-                for v in range(2):
-                    nc.tensor.transpose(
-                        turned[:, (2 * e + v) * P : (2 * e + v + 1) * P],
-                        words[:, at + v : at + N // 2 : 2],
-                        ident[:],
-                    )
-            nc.scalar.copy(
-                w_slots[b][:].bitcast(F32).rearrange("s (p t v) -> s p t v", t=PACK, v=2)[:, :, 2 * a : 2 * a + 2, :],
-                turned[:].rearrange("s (e v p) -> s p e v", e=2, v=2),
-            )
+        def lines(tile):
+            return tile[:].rearrange("p (c t i) -> p c t i", t=PACK, i=LINE)
 
         def quantise(src, cols, fmt, name):
             codes = keep.tile([P, cols], U32, name=name + "_codes", align_bytes=64)
@@ -147,39 +82,91 @@ def tile_attend_gsl2_x_ts_kernel(tc, xT, wT, y, wt, ts, offs, out):
             nc.vector.quantize_mx(out=codes[:].bitcast(fmt), scales=scales[:], in_=src)
             return codes, scales
 
-        w_feat_q, w_slot_q, x_q = {}, {}, {}
-
-        w_feats = [keep.tile([P, PACK * N], BF16, name="w_feats", tag=f"w_feats{b}", align_bytes=64) for b in range(B)]
-
-        def weave(b, copy, part=slice(0, P)):
-            copy(
-                w_feats[b][:].rearrange("p (r s t) -> p s t r", r=PACK, t=PACK)[:, part, :, :],
-                picked_w[:].rearrange("p (e s r) -> p s e r", s=P, r=PACK)[:, part, place(b, 0) : place(b, PACK - 1) + 1 : place(b, 1) - place(b, 0), :],
-            )
-
-        def prepare_features(b):
-            w_feat_q[b] = quantise(w_feats[b][:], N, E4M3, f"w_feat{b}")
-
-        def prepare_slots(b):
-            w_slot_q[b] = quantise(w_slots[b][:], D, E4M3, f"w_slot{b}")
-
-        def prepare_x(u):
-            woven = work.tile([P, PACK * ROWS], BF16, name="x_woven", align_bytes=64)
+        wt_spread = keep.tile([P, B * R], F32, name="wt_spread")
+        cols_a_bank = BANK // P
+        for first in range(0, WT_COLS, cols_a_bank):
+            bank = other_banks.tile([P, BANK], F32, name="bank")
+            for j in range(cols_a_bank):
+                column = wt_cols[:, first + j : first + j + 1].to_broadcast([P, P])
+                nc.tensor.transpose(bank[:, j * P : (j + 1) * P], column, ident[:])
+            spread = wt_spread[:].rearrange("p (u m j i) -> p u m j i", u=UNITS, j=WT_COLS, i=LINE)
             nc.scalar.copy(
-                woven[:].rearrange("p (c i t) -> p c t i", i=4, t=PACK),
-                x_raw[u][:].rearrange("p t (c i) -> p c t i", i=4),
+                spread[:, :, :, first : first + cols_a_bank, :],
+                bank[:].rearrange("p (j u i m) -> p u m j i", j=cols_a_bank, u=UNITS, i=LINE),
             )
-            x_q[u] = quantise(woven[:], ROWS, E4M3, f"x{u[0]}{u[1]}")
 
-        score_banks, y_banks, probs, grads = {}, {}, {}, {}
+        picked = keep.tile([P, PACK * B * N], BF16, name="picked", align_bytes=64)
 
-        def scores(u):
-            b = u[0]
-            w_codes, w_scales = w_feat_q[b]
-            x_codes, x_scales = x_q[u]
-            score_banks[u] = []
-            for a in range(2):
-                bank = psum.tile([P, 2 * ROWS], F32, name="score", tag="score", bufs=2)
+        def gather(t):
+            dst = picked[:, t * B * N : (t + 1) * B * N]
+            if t == SCALAR_PLANE:
+                narrow = keep.tile([P, T], BF16, name="narrow")
+                nc.scalar.activation(narrow[:], planes[t][:], ACT.Copy)
+                nc.scalar.activation(dst, narrow[:].indirect(offsets[:]), ACT.Copy)
+            else:
+                nc.vector.tensor_copy(dst, planes[t][:].indirect(offsets[:]))
+
+        ts_cols = []
+
+        def gather_scales():
+            ts_picked = keep.tile([P, B * N], F32, name="ts_picked")
+            nc.vector.tensor_copy(ts_picked[:], ts_table[:].indirect(offsets[:]))
+            for b in range(B):
+                bank = score_banks.tile([P, BANK], F32, name="score")
+                for t in range(PACK):
+                    nc.tensor.transpose(bank[:, t * P : (t + 1) * P], ts_picked[:, b * N + t : (b + 1) * N : PACK], ident[:])
+                cols = keep.tile([P, PACK], F32, name=f"ts_cols{b}")
+                nc.scalar.copy(cols[:], bank[:, 0:BANK:P])
+                ts_cols.append(cols)
+
+        by_slot = [keep.tile([P, D * PACK], BF16, name=f"by_slot{b}", align_bytes=64) for b in range(B)]
+
+        def turn_planes(b, a):
+            words = picked[:].bitcast(F32)
+            bank = other_banks.tile([P, BANK], F32, name="bank")
+            for e in range(2):
+                start = ((2 * a + e) * B + b) * N // 2
+                for v in range(2):
+                    quarter = 2 * e + v
+                    nc.tensor.transpose(
+                        bank[:, quarter * P : (quarter + 1) * P], words[:, start + v : start + N // 2 : 2], ident[:]
+                    )
+            nc.scalar.copy(
+                by_slot[b][:].bitcast(F32).rearrange("s (p t v) -> s p t v", t=PACK, v=2)[:, :, 2 * a : 2 * a + 2, :],
+                bank[:].rearrange("s (e v p) -> s p e v", e=2, v=2),
+            )
+
+        by_feature = [keep.tile([P, N * PACK], BF16, name=f"by_feature{b}", align_bytes=64) for b in range(B)]
+
+        def weave(b, copy, quads):
+            copy(
+                by_feature[b][:].rearrange("p (r s t) -> p s t r", r=PACK, t=PACK)[:, quads, :, :],
+                picked[:].rearrange("p (t b s r) -> p b s t r", t=PACK, b=B, r=PACK)[:, b, quads, :, :],
+            )
+
+        w_feature_mx, w_slot_mx, x_mx, h_mx = {}, {}, {}, {}
+        scores, y_turned, probs, squares, scaled, results = {}, {}, {}, {}, {}, {}
+
+        def quantise_by_feature(b):
+            w_feature_mx[b] = quantise(by_feature[b][:], N, E4M3, f"w_feature{b}")
+
+        def quantise_by_slot(b):
+            w_slot_mx[b] = quantise(by_slot[b][:], D, E4M3, f"w_slot{b}")
+
+        def quantise_x(u):
+            woven = keep.tile([P, ROWS * PACK], BF16, name=f"x_woven{u}", align_bytes=64)
+            nc.scalar.copy(
+                woven[:].rearrange("p (q n t) -> p q t n", n=LINE, t=PACK),
+                x_raw[u][:].rearrange("p t (q n) -> p q t n", n=LINE),
+            )
+            x_mx[u] = quantise(woven[:], ROWS, E4M3, f"x{u}")
+
+        def score(u):
+            w_codes, w_scales = w_feature_mx[group(u)]
+            x_codes, x_scales = x_mx[u]
+            scores[u] = []
+            for a in range(PAIRS):
+                bank = score_banks.tile([P, BANK], F32, name="score")
                 for e in range(2):
                     cols = slice((2 * a + e) * P, (2 * a + e + 1) * P)
                     nc.tensor.matmul_mx(
@@ -191,137 +178,135 @@ def tile_attend_gsl2_x_ts_kernel(tc, xT, wT, y, wt, ts, offs, out):
                         start=True,
                         stop=True,
                     )
-                score_banks[u].append(bank)
+                scores[u].append(bank)
 
         def turn_y(u):
-            y_banks[u] = []
-            for a in range(2):
-                bank = psum.tile([P, 2 * ROWS], F32, name="y_turned", tag="y_turned", bufs=4)
+            y_turned[u] = []
+            for a in range(PAIRS):
+                bank = y_banks.tile([P, BANK], F32, name="y_turned")
                 for e in range(2):
                     for j in range(TILES):
                         at = e * ROWS + j * P
                         nc.tensor.transpose(bank[:, at : at + P], y_raw[u][:, j, 2 * a + e : N : PACK], ident[:])
-                y_banks[u].append(bank)
+                y_turned[u].append(bank)
 
-        def lines(tile):
-            return tile[:].rearrange("p (c t i) -> p c t i", t=PACK, i=LINE)
-
-        def dealt(bank_cols):
-            return bank_cols.rearrange("p (i c) -> p c i", i=LINE)
-
-        def weigh(u):
-            b, hf = u
-            prob = work.tile([P, PACK * ROWS], F32, name="prob")
-            square = work.tile([P, PACK * ROWS], F32, name="square")
+        def sigmoids(u):
+            probs[u] = work.tile([P, PACK * ROWS], F32, name="prob")
+            squares[u] = work.tile([P, PACK * ROWS], F32, name="square")
             for t in range(PACK):
+                a, e = divmod(t, 2)
                 nc.scalar.activation(
-                    lines(prob)[:, :, t, :],
-                    dealt(score_banks[u][t // 2][:, (t % 2) * ROWS : (t % 2 + 1) * ROWS]),
+                    lines(probs[u])[:, :, t, :],
+                    scores[u][a][:, e * ROWS : (e + 1) * ROWS].rearrange("p (i c) -> p c i", i=LINE),
                     ACT.Sigmoid,
-                    scale=ts_cols[b][:, t : t + 1],
+                    scale=ts_cols[group(u)][:, t : t + 1],
                 )
-            for a in range(2):
+            for a in range(PAIRS):
                 nc.scalar.activation(
-                    lines(square)[:, :, 2 * a : 2 * a + 2, :],
-                    lines(prob)[:, :, 2 * a : 2 * a + 2, :],
+                    lines(squares[u])[:, :, 2 * a : 2 * a + 2, :],
+                    lines(probs[u])[:, :, 2 * a : 2 * a + 2, :],
                     ACT.Square,
                     bias=half[:],
                     scale=-1.0,
                 )
-            probs[u] = (prob, square)
 
-        def scale_miss(u):
-            b, hf = u
-            prob, square = probs[u]
+        def scale_misses(u):
             miss = work.tile([P, PACK * ROWS], F32, name="miss")
-            scaled = work.tile([P, PACK * ROWS], F32, name="scaled")
-            for a in range(2):
+            scaled[u] = work.tile([P, PACK * ROWS], F32, name="scaled")
+            for a in range(PAIRS):
                 nc.vector.tensor_tensor(
                     lines(miss)[:, :, 2 * a : 2 * a + 2, :],
-                    y_banks[u][a][:].rearrange("p (e i c) -> p c e i", e=2, i=LINE),
-                    lines(prob)[:, :, 2 * a : 2 * a + 2, :],
+                    y_turned[u][a][:].rearrange("p (e i c) -> p c e i", e=2, i=LINE),
+                    lines(probs[u])[:, :, 2 * a : 2 * a + 2, :],
                     ALU.subtract,
                 )
             for t in range(PACK):
                 nc.vector.scalar_tensor_tensor(
-                    lines(scaled)[:, :, t, :], lines(miss)[:, :, t, :], ts_cols[b][:, t : t + 1],
-                    wt_spread[b][:, hf * ROWS : (hf + 1) * ROWS].rearrange("p (c i) -> p c i", i=LINE), ALU.mult, ALU.mult,
+                    lines(scaled[u])[:, :, t, :],
+                    lines(miss)[:, :, t, :],
+                    ts_cols[group(u)][:, t : t + 1],
+                    wt_spread[:, u * ROWS : (u + 1) * ROWS].rearrange("p (c i) -> p c i", i=LINE),
+                    ALU.mult,
+                    ALU.mult,
                 )
-            grads[u] = (square, scaled)
 
-        def finish(u, pieces):
-            b, hf = u
-            square, scaled = grads[u]
-            w_codes, w_scales = w_slot_q[b]
-            rows = ROWS // pieces
-            runs = LINE // pieces
-            quantised = []
+        def multiply(u, pieces):
+            w_codes, w_scales = w_slot_mx[group(u)]
+            rows, runs = ROWS // pieces, LINE // pieces
             for k in range(pieces):
-                h = work.tile([P, PACK * rows], BF16, name="h", align_bytes=64)
+                h = work.tile([P, rows * PACK], BF16, name="h", align_bytes=64)
                 nc.vector.scalar_tensor_tensor(
                     h[:].rearrange("p (i m) -> p m i", i=runs),
-                    square[:].rearrange("p (m i) -> p m i", i=LINE)[:, :, k * runs : (k + 1) * runs],
+                    squares[u][:].rearrange("p (m i) -> p m i", i=LINE)[:, :, k * runs : (k + 1) * runs],
                     -0.25,
-                    scaled[:].rearrange("p (m i) -> p m i", i=LINE)[:, :, k * runs : (k + 1) * runs],
+                    scaled[u][:].rearrange("p (m i) -> p m i", i=LINE)[:, :, k * runs : (k + 1) * runs],
                     ALU.add,
                     ALU.mult,
                 )
-                quantised.append(quantise(h[:], rows, E5M2, f"h{b}{hf}{k}"))
+                h_mx[u, k] = quantise(h[:], rows, E5M2, f"h{u}{k}")
+            results[u] = []
             for j in range(TILES):
-                h_codes, h_scales = quantised[j * P // rows]
-                cols = slice(j * P % rows, j * P % rows + P)
-                bank = psum.tile([P, D], F32, name="result", tag="misc", bufs=2)
+                k, first = divmod(j * P, rows)
+                h_codes, h_scales = h_mx[u, k]
+                bank = other_banks.tile([P, BANK], F32, name="bank")
                 nc.tensor.matmul_mx(
                     out=bank[:],
-                    lhsT=h_codes[:, cols].bitcast(E5M2),
-                    lhsT_scale=h_scales[:, cols],
+                    lhsT=h_codes[:, first : first + P].bitcast(E5M2),
+                    lhsT_scale=h_scales[:, first : first + P],
                     rhs=w_codes[:].bitcast(E4M3),
                     rhs_scale=w_scales[:],
                     start=True,
                     stop=True,
                 )
-                staged = work.tile([P, D], F32, name="staged", bufs=4)
-                last = u == units[-1] and j == TILES - 1
-                (nc.vector.tensor_copy if last else nc.scalar.copy)(staged[:], bank[:])
-                first = hf * ROWS + j * P
-                nc.sync.dma_start(out[b, first : first + P, :], staged[:])
+                results[u].append(bank)
+
+        def store(u, copies):
+            for j, copy in enumerate(copies):
+                staged = work.tile([P, D], F32, name="staged", bufs=2 * TILES)
+                copy(staged[:], results[u][j][:])
+                first = rows_of(u).start + j * P
+                nc.sync.dma_start(out[group(u), first : first + P, :], staged[:])
 
         gather(0)
-        nc.vector.tensor_copy(ts_picked[:], ts_table[:].indirect(offsets[:]))
-        turn_scales(0)
-        turn_scales(1)
-        prepare_x(units[0])
-        spread_weights()
+        gather_scales()
         gather(1)
-        turn(0, 0)
-        turn(1, 0)
+        turn_planes(0, 0)
+        turn_planes(1, 0)
         gather(2)
         gather(3)
-        weave(0, nc.vector.tensor_copy, slice(0, 96))
-        weave(0, nc.scalar.copy, slice(96, P))
-        prepare_features(0)
-        scores(units[0])
-        turn_y(units[0])
-        turn(0, 1)
-        prepare_x(units[1])
-        prepare_slots(0)
-        weigh(units[0])
-        scores(units[1])
-        scale_miss(units[0])
-        turn(1, 1)
-        turn_y(units[1])
-        weave(1, nc.vector.tensor_copy)
-        prepare_features(1)
-        prepare_x(units[2])
-        prepare_slots(1)
-        for k in range(1, len(units)):
-            weigh(units[k])
-            if k + 1 < len(units):
-                scores(units[k + 1])
-            finish(units[k - 1], 1)
-            scale_miss(units[k])
-            if k + 1 < len(units):
-                turn_y(units[k + 1])
-            if k + 2 < len(units):
-                prepare_x(units[k + 2])
-        finish(units[-1], TILES)
+
+        weave(0, nc.vector.tensor_copy, slice(0, VECTOR_SHARE))
+        weave(0, nc.scalar.copy, slice(VECTOR_SHARE, P))
+        quantise_by_feature(0)
+        quantise_x(0)
+        score(0)
+        turn_y(0)
+        sigmoids(0)
+        quantise_x(1)
+        score(1)
+        turn_planes(0, 1)
+        weave(1, nc.vector.tensor_copy, slice(0, P))
+        quantise_by_feature(1)
+        quantise_x(2)
+        quantise_by_slot(0)
+        scale_misses(0)
+        turn_y(1)
+        sigmoids(1)
+        turn_planes(1, 1)
+        quantise_by_slot(1)
+
+        last = UNITS - 1
+        for u in range(1, UNITS):
+            if u < last:
+                score(u + 1)
+            multiply(u - 1, 1)
+            scale_misses(u)
+            if u + 1 < last:
+                quantise_x(u + 2)
+            if u < last:
+                sigmoids(u + 1)
+            store(u - 1, [nc.scalar.copy] * TILES)
+            if u < last:
+                turn_y(u + 1)
+        multiply(last, TILES)
+        store(last, [nc.scalar.copy, nc.vector.tensor_copy])

@@ -19,25 +19,26 @@ ALU = mybir.AluOpType
 
 P = 128
 PACK = 4
-PAIRS = PACK // 2
 BANK = 512
 ROWS = 256
 TILES = ROWS // P
 UNITS = B * R // ROWS
+ROW_TILES = B * R // P
 LINE = 4
-WT_COLS = B * R // P
-SCALAR_PLANE = 0
-VECTOR_SHARE = 80
+AT_TS, AT_PLANE, AT_X, AT_WOVEN = 0, 4 * T, 8 * T, 8 * T + 4 * PACK * ROWS
+COLS = N // 16
 
 
 def tile_attend_gsl2_x_ts_kernel(tc, xT, wT, y, wt, ts, offs, out):
     nc = tc.nc
     with ExitStack() as ctx:
         keep = ctx.enter_context(tc.tile_pool(name="keep", bufs=1))
-        work = ctx.enter_context(tc.tile_pool(name="work", bufs=3))
-        score_banks = ctx.enter_context(tc.psum_pool(name="score_banks", bufs=3))
-        y_banks = ctx.enter_context(tc.psum_pool(name="y_banks", bufs=3))
-        other_banks = ctx.enter_context(tc.psum_pool(name="other_banks", bufs=2))
+        work = ctx.enter_context(tc.tile_pool(name="work", bufs=2))
+        shared = ctx.enter_context(tc.tile_pool(name="shared", bufs=1))
+        score_banks = ctx.enter_context(tc.psum_pool(name="score_banks", bufs=2))
+        prob_banks = ctx.enter_context(tc.psum_pool(name="prob_banks", bufs=2))
+        miss_banks = ctx.enter_context(tc.psum_pool(name="miss_banks", bufs=2))
+        out_banks = ctx.enter_context(tc.psum_pool(name="out_banks", bufs=2))
 
         def group(u):
             return u * ROWS // R
@@ -45,25 +46,39 @@ def tile_attend_gsl2_x_ts_kernel(tc, xT, wT, y, wt, ts, offs, out):
         def rows_of(u):
             return slice(u * ROWS % R, u * ROWS % R + ROWS)
 
-        offsets = keep.tile([P, B * N // 16], U16, name="offsets")
+        offsets = keep.tile([P, B * COLS], U16, name="offsets")
         nc.sync.dma_start(offsets[:], offs)
-        ts_table = keep.tile([P, T], F32, name="ts_table")
-        nc.gpsimd.memset(ts_table[:, T // 2 :], 0.0)
-        nc.vector.memset(ts_table[:, : T // 2], 0.0)
-        wt_cols = keep.tile([P, WT_COLS], F32, name="wt_cols")
-        nc.sync.dma_start(wt_cols[:], wt.rearrange("b (n j) o -> (b n) (j o)", j=WT_COLS))
+        zero = keep.tile([P, 1], F32, name="zero")
+        nc.vector.memset(zero[:], 0.0)
+        ts_table = shared.tile([P, T], F32, name="ts_table", offset=AT_TS, align_bytes=64)
+        nc.vector.memset(ts_table[:], 0.0)
+        wt_rows = keep.tile([P, P], F32, name="wt_rows")
+        nc.vector.memset(wt_rows[:], 0.0)
         planes = []
         for t in range(PACK):
-            plane = keep.tile([P, T], F32, name=f"plane{t}")
+            if t == PACK - 1:
+                plane = shared.tile([P, T], F32, name=f"plane{t}", offset=AT_PLANE, align_bytes=64)
+            else:
+                plane = keep.tile([P, T], F32, name=f"plane{t}")
             nc.sync.dma_start(plane[:], wT.rearrange("(p t) c -> p t c", t=PACK)[:, t, :])
             planes.append(plane)
-            if t == SCALAR_PLANE:
+            if t == 0:
                 nc.sync.dma_start(ts_table[0:1, :], ts[0:1, :])
+                nc.sync.dma_start(wt_rows[0:ROW_TILES, :], wt.rearrange("b (j n) o -> (b j) (n o)", n=P))
         x_raw, y_raw = [], []
-        for u in range(UNITS):
-            x_unit = keep.tile([P, PACK, ROWS], F32, name=f"x_raw{u}")
+
+        def load_x(u):
+            if u == 0:
+                x_unit = shared.tile([P, PACK, ROWS], F32, name=f"x_raw{u}", offset=AT_X, align_bytes=64)
+            else:
+                x_unit = keep.tile([P, PACK, ROWS], F32, name=f"x_raw{u}")
             nc.sync.dma_start(x_unit[:], xT[group(u)].rearrange("(p t) r -> p t r", t=PACK)[:, :, rows_of(u)])
             x_raw.append(x_unit)
+
+        load_x(0)
+        for u in range(UNITS):
+            if u + 1 < UNITS:
+                load_x(u + 1)
             y_unit = keep.tile([P, TILES, N], F32, name=f"y_raw{u}")
             nc.sync.dma_start(y_unit[:], y[group(u), rows_of(u), :].rearrange("(j n) i -> n j i", n=P))
             y_raw.append(y_unit)
@@ -71,101 +86,126 @@ def tile_attend_gsl2_x_ts_kernel(tc, xT, wT, y, wt, ts, offs, out):
         ident = keep.tile([P, P], F32, name="ident")
         make_identity(nc, ident[:])
         half = keep.tile([P, 1], F32, name="half")
-        nc.scalar.activation(half[:], ident[:, 0:1], ACT.Sigmoid, scale=0.0)
+        nc.scalar.activation(half[:], zero[:], ACT.Sigmoid)
 
-        def lines(tile):
-            return tile[:].rearrange("p (c t i) -> p c t i", t=PACK, i=LINE)
+        def quantise(src, codes, scales, fmt):
+            nc.vector.quantize_mx(out=codes.bitcast(fmt), scales=scales, in_=src)
 
-        def quantise(src, cols, fmt, name):
+        def mx_tiles(cols, name):
             codes = keep.tile([P, cols], U32, name=name + "_codes", align_bytes=64)
             scales = keep.tile([P, cols], U8, name=name + "_scales", align_bytes=64)
-            nc.vector.quantize_mx(out=codes[:].bitcast(fmt), scales=scales[:], in_=src)
             return codes, scales
 
-        wt_spread = keep.tile([P, B * R], F32, name="wt_spread")
-        cols_a_bank = BANK // P
-        for first in range(0, WT_COLS, cols_a_bank):
-            bank = other_banks.tile([P, BANK], F32, name="bank")
-            for j in range(cols_a_bank):
-                column = wt_cols[:, first + j : first + j + 1].to_broadcast([P, P])
-                nc.tensor.transpose(bank[:, j * P : (j + 1) * P], column, ident[:])
-            spread = wt_spread[:].rearrange("p (u m j i) -> p u m j i", u=UNITS, j=WT_COLS, i=LINE)
-            nc.scalar.copy(
-                spread[:, :, :, first : first + cols_a_bank, :],
-                bank[:].rearrange("p (j u i m) -> p u m j i", j=cols_a_bank, u=UNITS, i=LINE),
+        wt_bank = miss_banks.tile([P, BANK], F32, name="turned_miss")
+        nc.tensor.transpose(wt_bank[:, :P], wt_rows[:], ident[:])
+
+        ts_picked = keep.tile([P, B * N], F32, name="ts_picked")
+        for b in range(B):
+            nc.scalar.activation(
+                ts_picked[:, b * N : (b + 1) * N], ts_table[:].indirect(offsets[:, b * COLS : (b + 1) * COLS]), ACT.Copy
             )
+        ts_cols = {}
+
+        def small(cols, name, place):
+            return shared.tile([P, cols], F32, name=name, offset=AT_PLANE + B * 5 * D + 64 * place, align_bytes=64)
+
+        def turn_scales(b):
+            bank = miss_banks.tile([P, BANK], F32, name="turned_miss")
+            for t in range(PACK):
+                nc.tensor.transpose(bank[:, t * P : (t + 1) * P], ts_picked[:, b * N + t : (b + 1) * N : PACK], ident[:])
+            return bank
+
+        def scale_columns(b, bank):
+            ts_cols[b] = small(PACK, f"ts_cols{b}", b)
+            nc.scalar.copy(ts_cols[b][:], bank[:, 0:BANK:P])
 
         picked = keep.tile([P, PACK * B * N], BF16, name="picked", align_bytes=64)
+        by_slot, w_slot_mx = {}, {}
 
         def gather(t):
-            dst = picked[:, t * B * N : (t + 1) * B * N]
-            if t == SCALAR_PLANE:
-                narrow = keep.tile([P, T], BF16, name="narrow")
-                nc.scalar.activation(narrow[:], planes[t][:], ACT.Copy)
-                nc.scalar.activation(dst, narrow[:].indirect(offsets[:]), ACT.Copy)
-            else:
-                nc.vector.tensor_copy(dst, planes[t][:].indirect(offsets[:]))
+            first = t * B * N
+            cut = B * N if t < PACK - 1 else N
+            nc.vector.tensor_copy(picked[:, first : first + cut], planes[t][:].indirect(offsets[:, : cut // 16]))
+            if cut < B * N:
+                nc.scalar.activation(
+                    picked[:, first + cut : first + B * N], planes[t][:].indirect(offsets[:, cut // 16 :]), ACT.Copy
+                )
 
-        ts_cols = []
-
-        def gather_scales():
-            ts_picked = keep.tile([P, B * N], F32, name="ts_picked")
-            nc.vector.tensor_copy(ts_picked[:], ts_table[:].indirect(offsets[:]))
+        def turn_plane(t):
+            a, e = divmod(t, 2)
+            if e == 0:
+                by_slot[a] = shared.tile([P, B * 2 * P * PACK], BF16, name=f"by_slot{a}", offset=[AT_TS, AT_X][a], align_bytes=64)
+            bank = out_banks.tile([P, BANK], F32, name="result")
             for b in range(B):
-                bank = score_banks.tile([P, BANK], F32, name="score")
-                for t in range(PACK):
-                    nc.tensor.transpose(bank[:, t * P : (t + 1) * P], ts_picked[:, b * N + t : (b + 1) * N : PACK], ident[:])
-                cols = keep.tile([P, PACK], F32, name=f"ts_cols{b}")
-                nc.scalar.copy(cols[:], bank[:, 0:BANK:P])
-                ts_cols.append(cols)
-
-        by_slot = [keep.tile([P, D * PACK], BF16, name=f"by_slot{b}", align_bytes=64) for b in range(B)]
-
-        def turn_planes(b, a):
-            words = picked[:].bitcast(F32)
-            bank = other_banks.tile([P, BANK], F32, name="bank")
-            for e in range(2):
-                start = ((2 * a + e) * B + b) * N // 2
+                words = picked[:].bitcast(F32)
+                first = (t * B + b) * N // 2
                 for v in range(2):
-                    quarter = 2 * e + v
+                    quarter = 2 * b + v
                     nc.tensor.transpose(
-                        bank[:, quarter * P : (quarter + 1) * P], words[:, start + v : start + N // 2 : 2], ident[:]
+                        bank[:, quarter * P : (quarter + 1) * P], words[:, first + v : first + N // 2 : 2], ident[:]
                     )
             nc.scalar.copy(
-                by_slot[b][:].bitcast(F32).rearrange("s (p t v) -> s p t v", t=PACK, v=2)[:, :, 2 * a : 2 * a + 2, :],
-                bank[:].rearrange("s (e v p) -> s p e v", e=2, v=2),
+                by_slot[a][:].bitcast(F32).rearrange("s (b e p v) -> s b e p v", b=B, e=2, v=2)[:, :, e, :, :],
+                bank[:].rearrange("s (b v p) -> s b p v", b=B, v=2),
             )
 
-        by_feature = [keep.tile([P, N * PACK], BF16, name=f"by_feature{b}", align_bytes=64) for b in range(B)]
+        def quantise_by_slot(a, b):
+            if a == 0:
+                codes = shared.tile([P, D], U32, name=f"w_slot{b}_codes", offset=AT_PLANE + b * 4 * D, align_bytes=64)
+                scales = shared.tile([P, D], U8, name=f"w_slot{b}_scales", offset=AT_PLANE + B * 4 * D + b * D, align_bytes=64)
+                w_slot_mx[b] = codes, scales
+            codes, scales = w_slot_mx[b]
+            cols = slice(a * D // 2, (a + 1) * D // 2)
+            quantise(by_slot[a][:, b * 2 * D : (b + 1) * 2 * D], codes[:, cols], scales[:, cols], E4M3)
 
-        def weave(b, copy, quads):
-            copy(
-                by_feature[b][:].rearrange("p (r s t) -> p s t r", r=PACK, t=PACK)[:, quads, :, :],
-                picked[:].rearrange("p (t b s r) -> p b s t r", t=PACK, b=B, r=PACK)[:, b, quads, :, :],
-            )
+        w_feature_mx, x_mx = {}, {}
 
-        w_feature_mx, w_slot_mx, x_mx, h_mx = {}, {}, {}, {}
-        scores, y_turned, probs, squares, scaled, results = {}, {}, {}, {}, {}, {}
+        def weave(b):
+            if b == 0:
+                by_feature = keep.tile([P, N * PACK], BF16, name="by_feature0", align_bytes=64)
+            else:
+                by_feature = shared.tile([P, N * PACK], BF16, name="by_feature1", offset=AT_WOVEN, align_bytes=64)
+            for a in range(2):
+                nc.vector.tensor_copy(
+                    by_feature[:].rearrange("p (r q e t) -> p q r e t", r=PACK, e=2, t=PACK)[:, :, 2 * a : 2 * a + 2],
+                    picked[:].rearrange("p (t b q e r) -> p b q r e t", t=PACK, b=B, e=2, r=PACK)[:, b, :, 2 * a : 2 * a + 2],
+                )
+            codes, scales = w_feature_mx[b] = mx_tiles(N, f"w_feature{b}")
+            for a in range(2):
+                cols = slice(a * N // 2, (a + 1) * N // 2)
+                quantise(by_feature[:, a * N * 2 : (a + 1) * N * 2], codes[:, cols], scales[:, cols], E4M3)
 
-        def quantise_by_feature(b):
-            w_feature_mx[b] = quantise(by_feature[b][:], N, E4M3, f"w_feature{b}")
+        x_woven = {}
 
-        def quantise_by_slot(b):
-            w_slot_mx[b] = quantise(by_slot[b][:], D, E4M3, f"w_slot{b}")
-
-        def quantise_x(u):
-            woven = keep.tile([P, ROWS * PACK], BF16, name=f"x_woven{u}", align_bytes=64)
+        def weave_x(u):
+            if u == 0:
+                woven = shared.tile([P, ROWS * PACK], BF16, name=f"x_woven{u}", offset=AT_WOVEN, align_bytes=64)
+            else:
+                woven = keep.tile([P, ROWS * PACK], BF16, name=f"x_woven{u}", align_bytes=64)
+            x_woven[u] = woven
             nc.scalar.copy(
                 woven[:].rearrange("p (q n t) -> p q t n", n=LINE, t=PACK),
                 x_raw[u][:].rearrange("p t (q n) -> p q t n", n=LINE),
             )
-            x_mx[u] = quantise(woven[:], ROWS, E4M3, f"x{u}")
 
-        def score(u):
+        def quantise_x(u):
+            x_mx[u] = mx_tiles(ROWS, f"x{u}")
+            quantise(x_woven[u][:], x_mx[u][0][:], x_mx[u][1][:], E4M3)
+
+        probs, squares, slopes, targets, misses, hs, h_mx = {}, {}, {}, {}, {}, {}, {}
+
+        def weigh_targets(k):
+            u, j = divmod(k, TILES)
+            targets[k] = work.tile([P, N], F32, name="target", bufs=2)
+            nc.vector.tensor_scalar(targets[k][:], y_raw[u][:, j, :], wt_cols[:, k : k + 1], None, ALU.mult)
+
+        def front(u):
             w_codes, w_scales = w_feature_mx[group(u)]
             x_codes, x_scales = x_mx[u]
-            scores[u] = []
-            for a in range(PAIRS):
+            probs[u] = work.tile([P, PACK, ROWS], F32, name="prob", bufs=UNITS)
+            square = work.tile([P, PACK, ROWS], F32, name="square", bufs=UNITS)
+            squares[u] = square
+            for a in range(2):
                 bank = score_banks.tile([P, BANK], F32, name="score")
                 for e in range(2):
                     cols = slice((2 * a + e) * P, (2 * a + e + 1) * P)
@@ -178,135 +218,123 @@ def tile_attend_gsl2_x_ts_kernel(tc, xT, wT, y, wt, ts, offs, out):
                         start=True,
                         stop=True,
                     )
-                scores[u].append(bank)
-
-        def turn_y(u):
-            y_turned[u] = []
-            for a in range(PAIRS):
-                bank = y_banks.tile([P, BANK], F32, name="y_turned")
                 for e in range(2):
-                    for j in range(TILES):
-                        at = e * ROWS + j * P
-                        nc.tensor.transpose(bank[:, at : at + P], y_raw[u][:, j, 2 * a + e : N : PACK], ident[:])
-                y_turned[u].append(bank)
-
-        def sigmoids(u):
-            probs[u] = work.tile([P, PACK * ROWS], F32, name="prob")
-            squares[u] = work.tile([P, PACK * ROWS], F32, name="square")
-            for t in range(PACK):
-                a, e = divmod(t, 2)
+                    t = 2 * a + e
+                    nc.scalar.activation(
+                        probs[u][:, t, :], bank[:, e * ROWS : (e + 1) * ROWS], ACT.Sigmoid, scale=ts_cols[group(u)][:, t : t + 1]
+                    )
+            for a in range(2):
                 nc.scalar.activation(
-                    lines(probs[u])[:, :, t, :],
-                    scores[u][a][:, e * ROWS : (e + 1) * ROWS].rearrange("p (i c) -> p c i", i=LINE),
-                    ACT.Sigmoid,
-                    scale=ts_cols[group(u)][:, t : t + 1],
-                )
-            for a in range(PAIRS):
-                nc.scalar.activation(
-                    lines(squares[u])[:, :, 2 * a : 2 * a + 2, :],
-                    lines(probs[u])[:, :, 2 * a : 2 * a + 2, :],
-                    ACT.Square,
-                    bias=half[:],
-                    scale=-1.0,
+                    square[:, 2 * a : 2 * a + 2, :], probs[u][:, 2 * a : 2 * a + 2, :], ACT.Square, bias=half[:], scale=-1.0
                 )
 
-        def scale_misses(u):
-            miss = work.tile([P, PACK * ROWS], F32, name="miss")
-            scaled[u] = work.tile([P, PACK * ROWS], F32, name="scaled")
-            for a in range(PAIRS):
-                nc.vector.tensor_tensor(
-                    lines(miss)[:, :, 2 * a : 2 * a + 2, :],
-                    y_turned[u][a][:].rearrange("p (e i c) -> p c e i", e=2, i=LINE),
-                    lines(probs[u])[:, :, 2 * a : 2 * a + 2, :],
-                    ALU.subtract,
-                )
+        def slope(u):
+            square = squares[u]
+            slopes[u] = work.tile([P, PACK * ROWS], F32, name="slope")
             for t in range(PACK):
-                nc.vector.scalar_tensor_tensor(
-                    lines(scaled[u])[:, :, t, :],
-                    lines(miss)[:, :, t, :],
-                    ts_cols[group(u)][:, t : t + 1],
-                    wt_spread[:, u * ROWS : (u + 1) * ROWS].rearrange("p (c i) -> p c i", i=LINE),
-                    ALU.mult,
-                    ALU.mult,
-                )
-
-        def multiply(u, pieces):
-            w_codes, w_scales = w_slot_mx[group(u)]
-            rows, runs = ROWS // pieces, LINE // pieces
-            for k in range(pieces):
-                h = work.tile([P, rows * PACK], BF16, name="h", align_bytes=64)
-                nc.vector.scalar_tensor_tensor(
-                    h[:].rearrange("p (i m) -> p m i", i=runs),
-                    squares[u][:].rearrange("p (m i) -> p m i", i=LINE)[:, :, k * runs : (k + 1) * runs],
+                nc.vector.tensor_scalar(
+                    slopes[u][:].rearrange("p (c t i) -> p c t i", t=PACK, i=LINE)[:, :, t, :],
+                    square[:, t, :].rearrange("p (c i) -> p c i", i=LINE),
                     -0.25,
-                    scaled[u][:].rearrange("p (m i) -> p m i", i=LINE)[:, :, k * runs : (k + 1) * runs],
+                    ts_cols[group(u)][:, t : t + 1],
                     ALU.add,
                     ALU.mult,
                 )
-                h_mx[u, k] = quantise(h[:], rows, E5M2, f"h{u}{k}")
-            results[u] = []
-            for j in range(TILES):
-                k, first = divmod(j * P, rows)
-                h_codes, h_scales = h_mx[u, k]
-                bank = other_banks.tile([P, BANK], F32, name="bank")
-                nc.tensor.matmul_mx(
-                    out=bank[:],
-                    lhsT=h_codes[:, first : first + P].bitcast(E5M2),
-                    lhsT_scale=h_scales[:, first : first + P],
-                    rhs=w_codes[:].bitcast(E4M3),
-                    rhs_scale=w_scales[:],
-                    start=True,
-                    stop=True,
-                )
-                results[u].append(bank)
 
-        def store(u, copies):
-            for j, copy in enumerate(copies):
-                staged = work.tile([P, D], F32, name="staged", bufs=2 * TILES)
-                copy(staged[:], results[u][j][:])
-                first = rows_of(u).start + j * P
-                nc.sync.dma_start(out[group(u), first : first + P, :], staged[:])
+        def miss(k):
+            u, j = divmod(k, TILES)
+            turned = prob_banks.tile([P, BANK], F32, name="turned_prob")
+            for t in range(PACK):
+                nc.tensor.transpose(turned[:, t * P : (t + 1) * P], probs[u][:, t, j * P : (j + 1) * P], ident[:])
+            weighted = work.tile([P, N], F32, name="weighted", bufs=3)
+            nc.vector.scalar_tensor_tensor(
+                weighted[:].rearrange("p (t s) -> p s t", t=PACK),
+                turned[:].rearrange("p (t s) -> p s t", t=PACK),
+                wt_minus[:, k : k + 1],
+                targets[k][:].rearrange("p (s t) -> p s t", t=PACK),
+                ALU.mult,
+                ALU.add,
+            )
+            misses[k] = miss_banks.tile([P, BANK], F32, name="turned_miss")
+            for t in range(PACK):
+                nc.tensor.transpose(misses[k][:, t * P : (t + 1) * P], weighted[:, t * P : (t + 1) * P], ident[:])
+
+        def gradient(k):
+            u, j = divmod(k, TILES)
+            h = work.tile([P, P * PACK], BF16, name="h", align_bytes=64, bufs=3)
+            nc.vector.tensor_tensor(
+                h[:].rearrange("p (c i t) -> p c t i", t=PACK, i=LINE),
+                misses[k][:].rearrange("p (t c i) -> p c t i", t=PACK, i=LINE),
+                slopes[u][:, j * BANK : (j + 1) * BANK].rearrange("p (c t i) -> p c t i", t=PACK, i=LINE),
+                ALU.mult,
+            )
+            hs[k] = h
+
+        def quantise_h(k):
+            h_mx[k] = mx_tiles(P, f"h{k}")
+            quantise(hs[k][:], h_mx[k][0][:], h_mx[k][1][:], E5M2)
+
+        def finish(k, copy):
+            u, j = divmod(k, TILES)
+            w_codes, w_scales = w_slot_mx[group(u)]
+            h_codes, h_scales = h_mx[k]
+            bank = out_banks.tile([P, BANK], F32, name="result")
+            nc.tensor.matmul_mx(
+                out=bank[:],
+                lhsT=h_codes[:].bitcast(E5M2),
+                lhsT_scale=h_scales[:],
+                rhs=w_codes[:].bitcast(E4M3),
+                rhs_scale=w_scales[:],
+                start=True,
+                stop=True,
+            )
+            staged = work.tile([P, D], F32, name="staged", bufs=4)
+            copy(staged[:].rearrange("n (p t) -> n p t", t=PACK), bank[:].rearrange("n (t p) -> n p t", t=PACK))
+            first = rows_of(u).start + j * P
+            nc.sync.dma_start(out[group(u), first : first + P, :], staged[:])
 
         gather(0)
-        gather_scales()
+        turn_plane(0)
+        ts_bank = turn_scales(0)
         gather(1)
-        turn_planes(0, 0)
-        turn_planes(1, 0)
+        turn_plane(1)
         gather(2)
         gather(3)
-
-        weave(0, nc.vector.tensor_copy, slice(0, VECTOR_SHARE))
-        weave(0, nc.scalar.copy, slice(VECTOR_SHARE, P))
-        quantise_by_feature(0)
+        wt_cols = small(ROW_TILES, "wt_cols", B)
+        wt_minus = small(ROW_TILES, "wt_minus", B + 1)
+        weave_x(0)
+        weave(0)
         quantise_x(0)
-        score(0)
-        turn_y(0)
-        sigmoids(0)
+        scale_columns(0, ts_bank)
+        nc.scalar.copy(wt_cols[:], wt_bank[:, :ROW_TILES])
+        nc.scalar.activation(wt_minus[:], wt_bank[:, :ROW_TILES], ACT.Copy, scale=-1.0)
+        weave_x(1)
+        turn_plane(2)
+        turn_plane(3)
+        scale_columns(1, turn_scales(1))
+        front(0)
         quantise_x(1)
-        score(1)
-        turn_planes(0, 1)
-        weave(1, nc.vector.tensor_copy, slice(0, P))
-        quantise_by_feature(1)
-        quantise_x(2)
-        quantise_by_slot(0)
-        scale_misses(0)
-        turn_y(1)
-        sigmoids(1)
-        turn_planes(1, 1)
-        quantise_by_slot(1)
-
-        last = UNITS - 1
-        for u in range(1, UNITS):
-            if u < last:
-                score(u + 1)
-            multiply(u - 1, 1)
-            scale_misses(u)
-            if u + 1 < last:
+        weave(1)
+        for b in range(B):
+            quantise_by_slot(0, b)
+        for u in range(UNITS):
+            first = u * TILES
+            weigh_targets(first)
+            weigh_targets(first + 1)
+            if u + 2 < UNITS:
+                weave_x(u + 2)
+            if u + 1 < UNITS:
+                front(u + 1)
+            miss(first)
+            slope(u)
+            miss(first + 1)
+            if u + 2 < UNITS:
                 quantise_x(u + 2)
-            if u < last:
-                sigmoids(u + 1)
-            store(u - 1, [nc.scalar.copy] * TILES)
-            if u < last:
-                turn_y(u + 1)
-        multiply(last, TILES)
-        store(last, [nc.scalar.copy, nc.vector.tensor_copy])
+            gradient(first)
+            if u < B:
+                quantise_by_slot(1, u)
+            gradient(first + 1)
+            quantise_h(first)
+            quantise_h(first + 1)
+        for k in range(ROW_TILES):
+            finish(k, nc.scalar.copy if k < ROW_TILES - 1 else nc.vector.tensor_copy)

@@ -25,20 +25,27 @@ TILES = ROWS // P
 UNITS = B * R // ROWS
 ROW_TILES = B * R // P
 LINE = 4
-AT_TS, AT_PLANE, AT_X, AT_WOVEN = 0, 4 * T, 8 * T, 8 * T + 4 * PACK * ROWS
 COLS = N // 16
+VECTOR_SLOPES = 3
+SLOT = 4 * PACK * ROWS
+AT = {"ts": 0, "x0": 2 * SLOT, "y": 4 * SLOT, "woven0": 6 * SLOT, "square": 7 * SLOT, "h": 11 * SLOT}
 
 
 def tile_attend_gsl2_x_ts_kernel(tc, xT, wT, y, wt, ts, offs, out):
     nc = tc.nc
     with ExitStack() as ctx:
         keep = ctx.enter_context(tc.tile_pool(name="keep", bufs=1))
-        work = ctx.enter_context(tc.tile_pool(name="work", bufs=2))
         shared = ctx.enter_context(tc.tile_pool(name="shared", bufs=1))
+        work = ctx.enter_context(tc.tile_pool(name="work", bufs=2))
         score_banks = ctx.enter_context(tc.psum_pool(name="score_banks", bufs=2))
         prob_banks = ctx.enter_context(tc.psum_pool(name="prob_banks", bufs=2))
         miss_banks = ctx.enter_context(tc.psum_pool(name="miss_banks", bufs=2))
         out_banks = ctx.enter_context(tc.psum_pool(name="out_banks", bufs=2))
+
+        def placed(shape, dtype, name, at=None):
+            if at is None:
+                return keep.tile(shape, dtype, name=name, align_bytes=64)
+            return shared.tile(shape, dtype, name=name, offset=at, align_bytes=64)
 
         def group(u):
             return u * ROWS // R
@@ -50,77 +57,64 @@ def tile_attend_gsl2_x_ts_kernel(tc, xT, wT, y, wt, ts, offs, out):
         nc.sync.dma_start(offsets[:], offs)
         zero = keep.tile([P, 1], F32, name="zero")
         nc.vector.memset(zero[:], 0.0)
-        ts_table = shared.tile([P, T], F32, name="ts_table", offset=AT_TS, align_bytes=64)
-        nc.vector.memset(ts_table[:], 0.0)
         wt_rows = keep.tile([P, P], F32, name="wt_rows")
         nc.vector.memset(wt_rows[:], 0.0)
+        ts_table = placed([P, T], F32, "ts_table", AT["ts"])
+        nc.vector.memset(ts_table[:], 0.0)
         planes = []
         for t in range(PACK):
-            if t == PACK - 1:
-                plane = shared.tile([P, T], F32, name=f"plane{t}", offset=AT_PLANE, align_bytes=64)
-            else:
-                plane = keep.tile([P, T], F32, name=f"plane{t}")
+            plane = placed([P, T], F32, f"plane{t}")
             nc.sync.dma_start(plane[:], wT.rearrange("(p t) c -> p t c", t=PACK)[:, t, :])
             planes.append(plane)
             if t == 0:
                 nc.sync.dma_start(ts_table[0:1, :], ts[0:1, :])
                 nc.sync.dma_start(wt_rows[0:ROW_TILES, :], wt.rearrange("b (j n) o -> (b j) (n o)", n=P))
-        x_raw, y_raw = [], []
+        x_raw, y_raw = {}, {}
 
         def load_x(u):
-            if u == 0:
-                x_unit = shared.tile([P, PACK, ROWS], F32, name=f"x_raw{u}", offset=AT_X, align_bytes=64)
-            else:
-                x_unit = keep.tile([P, PACK, ROWS], F32, name=f"x_raw{u}")
-            nc.sync.dma_start(x_unit[:], xT[group(u)].rearrange("(p t) r -> p t r", t=PACK)[:, :, rows_of(u)])
-            x_raw.append(x_unit)
+            x_raw[u] = placed([P, PACK, ROWS], F32, f"x_raw{u}", AT.get(f"x{u}"))
+            nc.sync.dma_start(x_raw[u][:], xT[group(u)].rearrange("(p t) r -> p t r", t=PACK)[:, :, rows_of(u)])
 
         load_x(0)
         for u in range(UNITS):
             if u + 1 < UNITS:
                 load_x(u + 1)
-            y_unit = keep.tile([P, TILES, N], F32, name=f"y_raw{u}")
-            nc.sync.dma_start(y_unit[:], y[group(u), rows_of(u), :].rearrange("(j n) i -> n j i", n=P))
-            y_raw.append(y_unit)
+            y_raw[u] = placed([P, TILES, N], F32, f"y_raw{u}", AT["y"] if u == 0 else None)
+            nc.sync.dma_start(y_raw[u][:], y[group(u), rows_of(u), :].rearrange("(j n) i -> n j i", n=P))
 
         ident = keep.tile([P, P], F32, name="ident")
         make_identity(nc, ident[:])
         half = keep.tile([P, 1], F32, name="half")
         nc.scalar.activation(half[:], zero[:], ACT.Sigmoid)
 
-        def quantise(src, codes, scales, fmt):
-            nc.vector.quantize_mx(out=codes.bitcast(fmt), scales=scales, in_=src)
-
-        def mx_tiles(cols, name):
-            codes = keep.tile([P, cols], U32, name=name + "_codes", align_bytes=64)
-            scales = keep.tile([P, cols], U8, name=name + "_scales", align_bytes=64)
+        def quantise(src, cols, fmt, name, at=None):
+            codes = placed([P, cols], U32, name + "_codes", at)
+            scales = placed([P, cols], U8, name + "_scales", None if at is None else at + 4 * cols)
+            nc.vector.quantize_mx(out=codes[:].bitcast(fmt), scales=scales[:], in_=src)
             return codes, scales
-
-        wt_bank = miss_banks.tile([P, BANK], F32, name="turned_miss")
-        nc.tensor.transpose(wt_bank[:, :P], wt_rows[:], ident[:])
 
         ts_picked = keep.tile([P, B * N], F32, name="ts_picked")
         for b in range(B):
             nc.scalar.activation(
                 ts_picked[:, b * N : (b + 1) * N], ts_table[:].indirect(offsets[:, b * COLS : (b + 1) * COLS]), ACT.Copy
             )
-        ts_cols = {}
+        column_bank = prob_banks.tile([P, BANK], F32, name="turned_prob")
+        nc.tensor.transpose(column_bank[:, BANK - P :], wt_rows[:], ident[:])
+        for k in range(B * PACK):
+            b, t = divmod(k, PACK)
+            nc.tensor.transpose(column_bank[:, 2 * k : 2 * k + P], ts_picked[:, b * N + t : (b + 1) * N : PACK], ident[:])
 
-        def small(cols, name, place):
-            return shared.tile([P, cols], F32, name=name, offset=AT_PLANE + B * 5 * D + 64 * place, align_bytes=64)
+        def columns(name, src, scale):
+            tile = keep.tile([P, ROW_TILES], F32, name=name)
+            nc.scalar.activation(tile[:], src, ACT.Copy, scale=scale)
+            return tile
 
-        def turn_scales(b):
-            bank = miss_banks.tile([P, BANK], F32, name="turned_miss")
-            for t in range(PACK):
-                nc.tensor.transpose(bank[:, t * P : (t + 1) * P], ts_picked[:, b * N + t : (b + 1) * N : PACK], ident[:])
-            return bank
-
-        def scale_columns(b, bank):
-            ts_cols[b] = small(PACK, f"ts_cols{b}", b)
-            nc.scalar.copy(ts_cols[b][:], bank[:, 0:BANK:P])
+        ts_turned, wt_turned = column_bank[:, 0 : 2 * B * PACK : 2], column_bank[:, BANK - P : BANK - P + ROW_TILES]
+        ts_cols, ts_quarter = columns("ts_cols", ts_turned, 1.0), columns("ts_quarter", ts_turned, -0.25)
+        wt_cols, wt_minus = columns("wt_cols", wt_turned, 1.0), columns("wt_minus", wt_turned, -1.0)
 
         picked = keep.tile([P, PACK * B * N], BF16, name="picked", align_bytes=64)
-        by_slot, w_slot_mx = {}, {}
+        by_slot, w_slot_mx, w_feature_mx, x_woven, x_mx = {}, {}, {}, {}, {}
 
         def gather(t):
             first = t * B * N
@@ -134,10 +128,10 @@ def tile_attend_gsl2_x_ts_kernel(tc, xT, wT, y, wt, ts, offs, out):
         def turn_plane(t):
             a, e = divmod(t, 2)
             if e == 0:
-                by_slot[a] = shared.tile([P, B * 2 * P * PACK], BF16, name=f"by_slot{a}", offset=[AT_TS, AT_X][a], align_bytes=64)
+                by_slot[a] = placed([P, B * 2 * P * PACK], BF16, f"by_slot{a}", AT["x0"] if a else AT["ts"])
             bank = out_banks.tile([P, BANK], F32, name="result")
+            words = picked[:].bitcast(F32)
             for b in range(B):
-                words = picked[:].bitcast(F32)
                 first = (t * B + b) * N // 2
                 for v in range(2):
                     quarter = 2 * b + v
@@ -149,70 +143,59 @@ def tile_attend_gsl2_x_ts_kernel(tc, xT, wT, y, wt, ts, offs, out):
                 bank[:].rearrange("s (b v p) -> s b p v", b=B, v=2),
             )
 
-        def quantise_by_slot(a, b):
-            if a == 0:
-                codes = shared.tile([P, D], U32, name=f"w_slot{b}_codes", offset=AT_PLANE + b * 4 * D, align_bytes=64)
-                scales = shared.tile([P, D], U8, name=f"w_slot{b}_scales", offset=AT_PLANE + B * 4 * D + b * D, align_bytes=64)
-                w_slot_mx[b] = codes, scales
-            codes, scales = w_slot_mx[b]
-            cols = slice(a * D // 2, (a + 1) * D // 2)
-            quantise(by_slot[a][:, b * 2 * D : (b + 1) * 2 * D], codes[:, cols], scales[:, cols], E4M3)
+        def quantise_by_slot(a):
+            w_slot_mx[a] = quantise(by_slot[a][:], D, E4M3, f"w_slot{a}", None if a else AT["woven0"])
 
-        w_feature_mx, x_mx = {}, {}
+        def quantise_by_feature(b, pieces):
+            by_feature = placed([P, N * PACK], BF16, f"by_feature{b}", AT["woven0"] - SLOT if b else None)
+            woven = by_feature[:].rearrange("p (r q e t) -> p q r e t", r=PACK, e=2, t=PACK)
+            planar = picked[:].rearrange("p (t b q e r) -> p b q r e t", t=PACK, b=B, e=2, r=PACK)[:, b]
+            tiles = PACK // pieces
+            for a in range(pieces):
+                nc.vector.tensor_copy(woven[:, :, a * tiles : (a + 1) * tiles], planar[:, :, a * tiles : (a + 1) * tiles])
+            for a in range(pieces):
+                part = by_feature[:, a * tiles * P * PACK : (a + 1) * tiles * P * PACK]
+                codes, scales = quantise(part, tiles * P, E4M3, f"w_feature{b}{a}")
+                for r in range(tiles):
+                    w_feature_mx[b, a * tiles + r] = codes[:, r * P : (r + 1) * P], scales[:, r * P : (r + 1) * P]
 
-        def weave(b):
-            if b == 0:
-                by_feature = keep.tile([P, N * PACK], BF16, name="by_feature0", align_bytes=64)
-            else:
-                by_feature = shared.tile([P, N * PACK], BF16, name="by_feature1", offset=AT_WOVEN, align_bytes=64)
-            for a in range(2):
-                nc.vector.tensor_copy(
-                    by_feature[:].rearrange("p (r q e t) -> p q r e t", r=PACK, e=2, t=PACK)[:, :, 2 * a : 2 * a + 2],
-                    picked[:].rearrange("p (t b q e r) -> p b q r e t", t=PACK, b=B, e=2, r=PACK)[:, b, :, 2 * a : 2 * a + 2],
+        def weave_x(u, at=None):
+            x_woven[u] = placed([P, ROWS * PACK], BF16, f"x_woven{u}", at)
+            if u < 3:
+                nc.scalar.copy(
+                    x_woven[u][:].rearrange("p (q n t) -> p q t n", n=LINE, t=PACK),
+                    x_raw[u][:].rearrange("p t (q n) -> p q t n", n=LINE),
                 )
-            codes, scales = w_feature_mx[b] = mx_tiles(N, f"w_feature{b}")
-            for a in range(2):
-                cols = slice(a * N // 2, (a + 1) * N // 2)
-                quantise(by_feature[:, a * N * 2 : (a + 1) * N * 2], codes[:, cols], scales[:, cols], E4M3)
-
-        x_woven = {}
-
-        def weave_x(u):
-            if u == 0:
-                woven = shared.tile([P, ROWS * PACK], BF16, name=f"x_woven{u}", offset=AT_WOVEN, align_bytes=64)
             else:
-                woven = keep.tile([P, ROWS * PACK], BF16, name=f"x_woven{u}", align_bytes=64)
-            x_woven[u] = woven
-            nc.scalar.copy(
-                woven[:].rearrange("p (q n t) -> p q t n", n=LINE, t=PACK),
-                x_raw[u][:].rearrange("p t (q n) -> p q t n", n=LINE),
-            )
+                nc.gpsimd.tensor_scalar(
+                    x_woven[u][:].rearrange("p (r t) -> p r t", t=PACK),
+                    x_raw[u][:].rearrange("p t r -> p r t"),
+                    1.0,
+                    0.0,
+                    ALU.mult,
+                    ALU.add,
+                )
 
         def quantise_x(u):
-            x_mx[u] = mx_tiles(ROWS, f"x{u}")
-            quantise(x_woven[u][:], x_mx[u][0][:], x_mx[u][1][:], E4M3)
+            x_mx[u] = quantise(x_woven[u][:], ROWS, E4M3, f"x{u}")
 
         probs, squares, slopes, targets, misses, hs, h_mx = {}, {}, {}, {}, {}, {}, {}
 
-        def weigh_targets(k):
-            u, j = divmod(k, TILES)
-            targets[k] = work.tile([P, N], F32, name="target", bufs=2)
-            nc.vector.tensor_scalar(targets[k][:], y_raw[u][:, j, :], wt_cols[:, k : k + 1], None, ALU.mult)
+        def scale_of(u, t, cols=ts_cols):
+            k = group(u) * PACK + t
+            return cols[:, k : k + 1]
 
-        def front(u):
-            w_codes, w_scales = w_feature_mx[group(u)]
+        def sigmoids(u):
             x_codes, x_scales = x_mx[u]
-            probs[u] = work.tile([P, PACK, ROWS], F32, name="prob", bufs=UNITS)
-            square = work.tile([P, PACK, ROWS], F32, name="square", bufs=UNITS)
-            squares[u] = square
+            probs[u] = placed([P, PACK, ROWS], F32, f"prob{u}", None)
             for a in range(2):
                 bank = score_banks.tile([P, BANK], F32, name="score")
                 for e in range(2):
-                    cols = slice((2 * a + e) * P, (2 * a + e + 1) * P)
+                    w_codes, w_scales = w_feature_mx[group(u), 2 * a + e]
                     nc.tensor.matmul_mx(
                         out=bank[:, e * ROWS : (e + 1) * ROWS],
-                        lhsT=w_codes[:, cols].bitcast(E4M3),
-                        lhsT_scale=w_scales[:, cols],
+                        lhsT=w_codes.bitcast(E4M3),
+                        lhsT_scale=w_scales,
                         rhs=x_codes[:].bitcast(E4M3),
                         rhs_scale=x_scales[:],
                         start=True,
@@ -220,33 +203,33 @@ def tile_attend_gsl2_x_ts_kernel(tc, xT, wT, y, wt, ts, offs, out):
                     )
                 for e in range(2):
                     t = 2 * a + e
-                    nc.scalar.activation(
-                        probs[u][:, t, :], bank[:, e * ROWS : (e + 1) * ROWS], ACT.Sigmoid, scale=ts_cols[group(u)][:, t : t + 1]
-                    )
-            for a in range(2):
-                nc.scalar.activation(
-                    square[:, 2 * a : 2 * a + 2, :], probs[u][:, 2 * a : 2 * a + 2, :], ACT.Square, bias=half[:], scale=-1.0
-                )
+                    nc.scalar.activation(probs[u][:, t, :], bank[:, e * ROWS : (e + 1) * ROWS], ACT.Sigmoid, scale=scale_of(u, t))
+
+        def square(u):
+            squares[u] = placed([P, PACK, ROWS], F32, f"square{u}", AT["square"] + u * SLOT)
+            nc.scalar.activation(squares[u][:], probs[u][:], ACT.Square, bias=half[:], scale=-1.0)
 
         def slope(u):
-            square = squares[u]
-            slopes[u] = work.tile([P, PACK * ROWS], F32, name="slope")
+            slopes[u] = work.tile([P, PACK * ROWS], F32, name="slope", bufs=1 if u < VECTOR_SLOPES else 2, tag="slope" if u < VECTOR_SLOPES else "late_slope")
             for t in range(PACK):
-                nc.vector.tensor_scalar(
-                    slopes[u][:].rearrange("p (c t i) -> p c t i", t=PACK, i=LINE)[:, :, t, :],
-                    square[:, t, :].rearrange("p (c i) -> p c i", i=LINE),
-                    -0.25,
-                    ts_cols[group(u)][:, t : t + 1],
-                    ALU.add,
-                    ALU.mult,
-                )
+                dst = slopes[u][:].rearrange("p (c t i) -> p c t i", t=PACK, i=LINE)[:, :, t, :]
+                src = squares[u][:, t, :].rearrange("p (c i) -> p c i", i=LINE)
+                if u < VECTOR_SLOPES:
+                    nc.vector.tensor_scalar(dst, src, -0.25, scale_of(u, t), ALU.add, ALU.mult)
+                else:
+                    nc.scalar.activation(dst, src, ACT.Identity, bias=scale_of(u, t, ts_quarter), scale=scale_of(u, t))
+
+        def weigh_targets(k, engine, at=None):
+            u, j = divmod(k, TILES)
+            targets[k] = placed([P, N], F32, f"target{k}", at)
+            engine.tensor_scalar(targets[k][:], y_raw[u][:, j, :], wt_cols[:, k : k + 1], 0.0, ALU.mult, ALU.add)
 
         def miss(k):
             u, j = divmod(k, TILES)
             turned = prob_banks.tile([P, BANK], F32, name="turned_prob")
-            for t in range(PACK):
+            for t in reversed(range(PACK)):
                 nc.tensor.transpose(turned[:, t * P : (t + 1) * P], probs[u][:, t, j * P : (j + 1) * P], ident[:])
-            weighted = work.tile([P, N], F32, name="weighted", bufs=3)
+            weighted = work.tile([P, N], F32, name="weighted")
             nc.vector.scalar_tensor_tensor(
                 weighted[:].rearrange("p (t s) -> p s t", t=PACK),
                 turned[:].rearrange("p (t s) -> p s t", t=PACK),
@@ -261,80 +244,97 @@ def tile_attend_gsl2_x_ts_kernel(tc, xT, wT, y, wt, ts, offs, out):
 
         def gradient(k):
             u, j = divmod(k, TILES)
-            h = work.tile([P, P * PACK], BF16, name="h", align_bytes=64, bufs=3)
+            if j == 0:
+                hs[u] = placed([P, ROWS * PACK], BF16, f"h{u}", AT["h"] + u * SLOT + SLOT // 4)
             nc.vector.tensor_tensor(
-                h[:].rearrange("p (c i t) -> p c t i", t=PACK, i=LINE),
+                hs[u][:, j * BANK : (j + 1) * BANK].rearrange("p (c i t) -> p c t i", t=PACK, i=LINE),
                 misses[k][:].rearrange("p (t c i) -> p c t i", t=PACK, i=LINE),
                 slopes[u][:, j * BANK : (j + 1) * BANK].rearrange("p (c t i) -> p c t i", t=PACK, i=LINE),
                 ALU.mult,
             )
-            hs[k] = h
 
-        def quantise_h(k):
-            h_mx[k] = mx_tiles(P, f"h{k}")
-            quantise(hs[k][:], h_mx[k][0][:], h_mx[k][1][:], E5M2)
+        def quantise_h(first, tiles):
+            u, j = divmod(first, TILES)
+            codes, scales = quantise(hs[u][:, j * BANK : (j + tiles) * BANK], tiles * P, E5M2, f"h{first}")
+            for k in range(tiles):
+                h_mx[first + k] = codes[:, k * P : (k + 1) * P], scales[:, k * P : (k + 1) * P]
 
         def finish(k, copy):
             u, j = divmod(k, TILES)
-            w_codes, w_scales = w_slot_mx[group(u)]
             h_codes, h_scales = h_mx[k]
-            bank = out_banks.tile([P, BANK], F32, name="result")
-            nc.tensor.matmul_mx(
-                out=bank[:],
-                lhsT=h_codes[:].bitcast(E5M2),
-                lhsT_scale=h_scales[:],
-                rhs=w_codes[:].bitcast(E4M3),
-                rhs_scale=w_scales[:],
-                start=True,
-                stop=True,
-            )
+            if u + 1 < UNITS:
+                bank = out_banks.tile([P, BANK], F32, name="result")
+            else:
+                bank = score_banks.tile([P, BANK], F32, name="score")
+            for a in range(2):
+                w_codes, w_scales = w_slot_mx[a]
+                cols = slice(group(u) * D // 2, (group(u) + 1) * D // 2)
+                nc.tensor.matmul_mx(
+                    out=bank[:, a * D // 2 : (a + 1) * D // 2],
+                    lhsT=h_codes.bitcast(E5M2),
+                    lhsT_scale=h_scales,
+                    rhs=w_codes[:, cols].bitcast(E4M3),
+                    rhs_scale=w_scales[:, cols],
+                    start=True,
+                    stop=True,
+                )
             staged = work.tile([P, D], F32, name="staged", bufs=4)
             copy(staged[:].rearrange("n (p t) -> n p t", t=PACK), bank[:].rearrange("n (t p) -> n p t", t=PACK))
             first = rows_of(u).start + j * P
             nc.sync.dma_start(out[group(u), first : first + P, :], staged[:])
 
-        gather(0)
-        turn_plane(0)
-        ts_bank = turn_scales(0)
-        gather(1)
-        turn_plane(1)
-        gather(2)
-        gather(3)
-        wt_cols = small(ROW_TILES, "wt_cols", B)
-        wt_minus = small(ROW_TILES, "wt_minus", B + 1)
-        weave_x(0)
-        weave(0)
+        for t in range(PACK):
+            gather(t)
+            if t < 2:
+                turn_plane(t)
+        weave_x(0, AT["woven0"] - SLOT // 4)
+        quantise_by_feature(0, 2)
         quantise_x(0)
-        scale_columns(0, ts_bank)
-        nc.scalar.copy(wt_cols[:], wt_bank[:, :ROW_TILES])
-        nc.scalar.activation(wt_minus[:], wt_bank[:, :ROW_TILES], ACT.Copy, scale=-1.0)
-        weave_x(1)
         turn_plane(2)
         turn_plane(3)
-        scale_columns(1, turn_scales(1))
-        front(0)
+        weave_x(1)
+        sigmoids(0)
+        weave_x(2)
+        square(0)
         quantise_x(1)
-        weave(1)
-        for b in range(B):
-            quantise_by_slot(0, b)
+        quantise_by_feature(1, 1)
+        quantise_by_slot(0)
+        for k in range(TILES):
+            weigh_targets(k, nc.vector)
+        weigh_targets(TILES, nc.gpsimd, AT["y"])
+        miss(0)
+        miss(1)
+        sigmoids(1)
         for u in range(UNITS):
             first = u * TILES
-            weigh_targets(first)
-            weigh_targets(first + 1)
-            if u + 2 < UNITS:
-                weave_x(u + 2)
-            if u + 1 < UNITS:
-                front(u + 1)
-            miss(first)
-            slope(u)
-            miss(first + 1)
             if u + 2 < UNITS:
                 quantise_x(u + 2)
+            if u < VECTOR_SLOPES:
+                slope(u)
+            at = AT["h"] + (u - 1) * SLOT if u else AT["square"]
+            if u == 0:
+                quantise_by_slot(1)
+                weigh_targets(first + TILES + 1, nc.gpsimd, at)
+                weave_x(3, at + SLOT // 2)
+            else:
+                quantise_h(first - TILES, TILES)
+                if u + 1 < UNITS:
+                    weigh_targets(first + TILES, nc.gpsimd, at)
+                    weigh_targets(first + TILES + 1, nc.gpsimd, at + SLOT // 2)
             gradient(first)
-            if u < B:
-                quantise_by_slot(1, u)
             gradient(first + 1)
-            quantise_h(first)
-            quantise_h(first + 1)
-        for k in range(ROW_TILES):
-            finish(k, nc.scalar.copy if k < ROW_TILES - 1 else nc.vector.tensor_copy)
+            if u + 1 < UNITS:
+                square(u + 1)
+                if u + 1 >= VECTOR_SLOPES:
+                    slope(u + 1)
+                miss(first + TILES)
+                miss(first + TILES + 1)
+            if u + 2 < UNITS:
+                sigmoids(u + 2)
+            if u:
+                finish(first - 2, nc.scalar.copy)
+                finish(first - 1, nc.scalar.copy)
+        quantise_h(ROW_TILES - 2, 1)
+        quantise_h(ROW_TILES - 1, 1)
+        finish(ROW_TILES - 2, nc.scalar.copy)
+        finish(ROW_TILES - 1, nc.vector.tensor_copy)

@@ -28,7 +28,8 @@ LINE = 4
 COLS = N // 16
 VECTOR_SLOPES = 3
 SLOT = 4 * PACK * ROWS
-AT = {"ts": 0, "x0": 2 * SLOT, "y": 4 * SLOT, "woven0": 6 * SLOT, "square": 7 * SLOT, "h": 11 * SLOT}
+AT = {"ts": 0, "x0": 2 * SLOT, "y": 4 * SLOT, "woven0": 6 * SLOT, "step": 7 * SLOT, "planes": 14 * SLOT}
+STEP = 3 * SLOT // 2
 
 
 def tile_attend_gsl2_x_ts_kernel(tc, xT, wT, y, wt, ts, offs, out):
@@ -57,13 +58,13 @@ def tile_attend_gsl2_x_ts_kernel(tc, xT, wT, y, wt, ts, offs, out):
         nc.sync.dma_start(offsets[:], offs)
         zero = keep.tile([P, 1], F32, name="zero")
         nc.vector.memset(zero[:], 0.0)
-        wt_rows = keep.tile([P, P], F32, name="wt_rows")
-        nc.vector.memset(wt_rows[:], 0.0)
         ts_table = placed([P, T], F32, "ts_table", AT["ts"])
         nc.vector.memset(ts_table[:], 0.0)
+        wt_rows = keep.tile([P, P], F32, name="wt_rows")
+        nc.vector.memset(wt_rows[:], 0.0)
         planes = []
         for t in range(PACK):
-            plane = placed([P, T], F32, f"plane{t}")
+            plane = placed([P, T], F32, f"plane{t}", AT["planes"] + 4 * T * t)
             nc.sync.dma_start(plane[:], wT.rearrange("(p t) c -> p t c", t=PACK)[:, t, :])
             planes.append(plane)
             if t == 0:
@@ -75,10 +76,10 @@ def tile_attend_gsl2_x_ts_kernel(tc, xT, wT, y, wt, ts, offs, out):
             x_raw[u] = placed([P, PACK, ROWS], F32, f"x_raw{u}", AT.get(f"x{u}"))
             nc.sync.dma_start(x_raw[u][:], xT[group(u)].rearrange("(p t) r -> p t r", t=PACK)[:, :, rows_of(u)])
 
-        load_x(0)
         for u in range(UNITS):
-            if u + 1 < UNITS:
-                load_x(u + 1)
+            if u < B:
+                load_x(2 * u)
+                load_x(2 * u + 1)
             y_raw[u] = placed([P, TILES, N], F32, f"y_raw{u}", AT["y"] if u == 0 else None)
             nc.sync.dma_start(y_raw[u][:], y[group(u), rows_of(u), :].rearrange("(j n) i -> n j i", n=P))
 
@@ -161,20 +162,10 @@ def tile_attend_gsl2_x_ts_kernel(tc, xT, wT, y, wt, ts, offs, out):
 
         def weave_x(u, at=None):
             x_woven[u] = placed([P, ROWS * PACK], BF16, f"x_woven{u}", at)
-            if u < 3:
-                nc.scalar.copy(
-                    x_woven[u][:].rearrange("p (q n t) -> p q t n", n=LINE, t=PACK),
-                    x_raw[u][:].rearrange("p t (q n) -> p q t n", n=LINE),
-                )
-            else:
-                nc.gpsimd.tensor_scalar(
-                    x_woven[u][:].rearrange("p (r t) -> p r t", t=PACK),
-                    x_raw[u][:].rearrange("p t r -> p r t"),
-                    1.0,
-                    0.0,
-                    ALU.mult,
-                    ALU.add,
-                )
+            nc.scalar.copy(
+                x_woven[u][:].rearrange("p (q n t) -> p q t n", n=LINE, t=PACK),
+                x_raw[u][:].rearrange("p t (q n) -> p q t n", n=LINE),
+            )
 
         def quantise_x(u):
             x_mx[u] = quantise(x_woven[u][:], ROWS, E4M3, f"x{u}")
@@ -206,8 +197,10 @@ def tile_attend_gsl2_x_ts_kernel(tc, xT, wT, y, wt, ts, offs, out):
                     nc.scalar.activation(probs[u][:, t, :], bank[:, e * ROWS : (e + 1) * ROWS], ACT.Sigmoid, scale=scale_of(u, t))
 
         def square(u):
-            squares[u] = placed([P, PACK, ROWS], F32, f"square{u}", AT["square"] + u * SLOT)
-            nc.scalar.activation(squares[u][:], probs[u][:], ACT.Square, bias=half[:], scale=-1.0)
+            squares[u] = placed([P, PACK, ROWS], F32, f"square{u}", AT["step"] + u * STEP + SLOT // 2)
+            for a in range(2):
+                pair = slice(2 * a, 2 * a + 2)
+                nc.scalar.activation(squares[u][:, pair, :], probs[u][:, pair, :], ACT.Square, bias=half[:], scale=-1.0)
 
         def slope(u):
             slopes[u] = work.tile([P, PACK * ROWS], F32, name="slope", bufs=1 if u < VECTOR_SLOPES else 2, tag="slope" if u < VECTOR_SLOPES else "late_slope")
@@ -219,10 +212,12 @@ def tile_attend_gsl2_x_ts_kernel(tc, xT, wT, y, wt, ts, offs, out):
                 else:
                     nc.scalar.activation(dst, src, ACT.Identity, bias=scale_of(u, t, ts_quarter), scale=scale_of(u, t))
 
-        def weigh_targets(k, engine, at=None):
-            u, j = divmod(k, TILES)
-            targets[k] = placed([P, N], F32, f"target{k}", at)
-            engine.tensor_scalar(targets[k][:], y_raw[u][:, j, :], wt_cols[:, k : k + 1], 0.0, ALU.mult, ALU.add)
+        def weigh_targets(tiles, engine, at=None):
+            held = placed([P, len(tiles), N], F32, f"target{tiles[0]}", at)
+            for place, k in enumerate(tiles):
+                u, j = divmod(k, TILES)
+                targets[k] = held[:, place, :]
+                engine.tensor_scalar(targets[k], y_raw[u][:, j, :], wt_cols[:, k : k + 1], 0.0, ALU.mult, ALU.add)
 
         def miss(k):
             u, j = divmod(k, TILES)
@@ -234,7 +229,7 @@ def tile_attend_gsl2_x_ts_kernel(tc, xT, wT, y, wt, ts, offs, out):
                 weighted[:].rearrange("p (t s) -> p s t", t=PACK),
                 turned[:].rearrange("p (t s) -> p s t", t=PACK),
                 wt_minus[:, k : k + 1],
-                targets[k][:].rearrange("p (s t) -> p s t", t=PACK),
+                targets[k].rearrange("p (s t) -> p s t", t=PACK),
                 ALU.mult,
                 ALU.add,
             )
@@ -245,7 +240,7 @@ def tile_attend_gsl2_x_ts_kernel(tc, xT, wT, y, wt, ts, offs, out):
         def gradient(k):
             u, j = divmod(k, TILES)
             if j == 0:
-                hs[u] = placed([P, ROWS * PACK], BF16, f"h{u}", AT["h"] + u * SLOT + SLOT // 4)
+                hs[u] = placed([P, ROWS * PACK], BF16, f"h{u}", AT["step"] + (u + 1) * STEP)
             nc.vector.tensor_tensor(
                 hs[u][:, j * BANK : (j + 1) * BANK].rearrange("p (c i t) -> p c t i", t=PACK, i=LINE),
                 misses[k][:].rearrange("p (t c i) -> p c t i", t=PACK, i=LINE),
@@ -259,26 +254,27 @@ def tile_attend_gsl2_x_ts_kernel(tc, xT, wT, y, wt, ts, offs, out):
             for k in range(tiles):
                 h_mx[first + k] = codes[:, k * P : (k + 1) * P], scales[:, k * P : (k + 1) * P]
 
-        def finish(k, copy):
-            u, j = divmod(k, TILES)
+        def product(k, a, bank):
             h_codes, h_scales = h_mx[k]
-            if u + 1 < UNITS:
-                bank = out_banks.tile([P, BANK], F32, name="result")
-            else:
-                bank = score_banks.tile([P, BANK], F32, name="score")
+            w_codes, w_scales = w_slot_mx[a]
+            b = group(k // TILES)
+            cols = slice(b * D // 2, (b + 1) * D // 2)
+            nc.tensor.matmul_mx(
+                out=bank,
+                lhsT=h_codes.bitcast(E5M2),
+                lhsT_scale=h_scales,
+                rhs=w_codes[:, cols].bitcast(E4M3),
+                rhs_scale=w_scales[:, cols],
+                start=True,
+                stop=True,
+            )
+
+        def finish(k, copy, pool, name):
+            u, j = divmod(k, TILES)
+            bank = pool.tile([P, BANK], F32, name=name)
             for a in range(2):
-                w_codes, w_scales = w_slot_mx[a]
-                cols = slice(group(u) * D // 2, (group(u) + 1) * D // 2)
-                nc.tensor.matmul_mx(
-                    out=bank[:, a * D // 2 : (a + 1) * D // 2],
-                    lhsT=h_codes.bitcast(E5M2),
-                    lhsT_scale=h_scales,
-                    rhs=w_codes[:, cols].bitcast(E4M3),
-                    rhs_scale=w_scales[:, cols],
-                    start=True,
-                    stop=True,
-                )
-            staged = work.tile([P, D], F32, name="staged", bufs=4)
+                product(k, a, bank[:, a * D // 2 : (a + 1) * D // 2])
+            staged = placed([P, D], F32, f"staged{k}", AT["planes"] + 4 * D * k)
             copy(staged[:].rearrange("n (p t) -> n p t", t=PACK), bank[:].rearrange("n (t p) -> n p t", t=PACK))
             first = rows_of(u).start + j * P
             nc.sync.dma_start(out[group(u), first : first + P, :], staged[:])
@@ -299,28 +295,25 @@ def tile_attend_gsl2_x_ts_kernel(tc, xT, wT, y, wt, ts, offs, out):
         quantise_x(1)
         quantise_by_feature(1, 1)
         quantise_by_slot(0)
-        for k in range(TILES):
-            weigh_targets(k, nc.vector)
-        weigh_targets(TILES, nc.gpsimd, AT["y"])
+        weigh_targets(range(TILES), nc.vector)
+        weigh_targets([TILES], nc.gpsimd, AT["y"])
         miss(0)
         miss(1)
         sigmoids(1)
+        weave_x(3)
         for u in range(UNITS):
             first = u * TILES
             if u + 2 < UNITS:
                 quantise_x(u + 2)
             if u < VECTOR_SLOPES:
                 slope(u)
-            at = AT["h"] + (u - 1) * SLOT if u else AT["square"]
             if u == 0:
                 quantise_by_slot(1)
-                weigh_targets(first + TILES + 1, nc.gpsimd, at)
-                weave_x(3, at + SLOT // 2)
-            else:
+            if u:
                 quantise_h(first - TILES, TILES)
-                if u + 1 < UNITS:
-                    weigh_targets(first + TILES, nc.gpsimd, at)
-                    weigh_targets(first + TILES + 1, nc.gpsimd, at + SLOT // 2)
+            if u + 1 < UNITS:
+                ahead = range(first + TILES + 1, min(first + 2 * TILES + 1, ROW_TILES))
+                weigh_targets(ahead, nc.gpsimd, AT["step"] + u * STEP + SLOT // 4)
             gradient(first)
             gradient(first + 1)
             if u + 1 < UNITS:
@@ -332,9 +325,10 @@ def tile_attend_gsl2_x_ts_kernel(tc, xT, wT, y, wt, ts, offs, out):
             if u + 2 < UNITS:
                 sigmoids(u + 2)
             if u:
-                finish(first - 2, nc.scalar.copy)
-                finish(first - 1, nc.scalar.copy)
+                banks = (out_banks, "result") if u + 1 < UNITS else (score_banks, "score")
+                finish(first - 2, nc.scalar.copy, *banks)
+                finish(first - 1, nc.scalar.copy, *banks)
         quantise_h(ROW_TILES - 2, 1)
         quantise_h(ROW_TILES - 1, 1)
-        finish(ROW_TILES - 2, nc.scalar.copy)
-        finish(ROW_TILES - 1, nc.vector.tensor_copy)
+        finish(ROW_TILES - 2, nc.scalar.copy, prob_banks, "turned_prob")
+        finish(ROW_TILES - 1, nc.vector.tensor_copy, prob_banks, "turned_prob")

@@ -26,10 +26,11 @@ UNITS = B * R // ROWS
 ROW_TILES = B * R // P
 LINE = 4
 COLS = N // 16
-VECTOR_SLOPES = 3
+X_LOADS = ((0, 1, 2), (3,), (), ())
 SLOT = 4 * PACK * ROWS
-AT = {"ts": 0, "x0": 2 * SLOT, "y": 4 * SLOT, "woven0": 6 * SLOT, "step": 7 * SLOT, "planes": 14 * SLOT}
-STEP = 3 * SLOT // 2
+K = 1024
+AT = {"ts": 0, "x3": 8 * K, "x2": 12 * K, "woven0": 24 * K, "square": 28 * K, "step": 36 * K, "planes": 76 * K}
+STEP = 8 * K
 
 
 def tile_attend_gsl2_x_ts_kernel(tc, xT, wT, y, wt, ts, offs, out):
@@ -38,15 +39,20 @@ def tile_attend_gsl2_x_ts_kernel(tc, xT, wT, y, wt, ts, offs, out):
         keep = ctx.enter_context(tc.tile_pool(name="keep", bufs=1))
         shared = ctx.enter_context(tc.tile_pool(name="shared", bufs=1))
         work = ctx.enter_context(tc.tile_pool(name="work", bufs=2))
-        score_banks = ctx.enter_context(tc.psum_pool(name="score_banks", bufs=2))
+        product_banks = [ctx.enter_context(tc.psum_pool(name=f"product_banks{k}", bufs=2)) for k in range(2)]
         prob_banks = ctx.enter_context(tc.psum_pool(name="prob_banks", bufs=2))
         miss_banks = ctx.enter_context(tc.psum_pool(name="miss_banks", bufs=2))
-        out_banks = ctx.enter_context(tc.psum_pool(name="out_banks", bufs=2))
 
         def placed(shape, dtype, name, at=None):
             if at is None:
                 return keep.tile(shape, dtype, name=name, align_bytes=64)
             return shared.tile(shape, dtype, name=name, offset=at, align_bytes=64)
+
+        def product_bank(pair):
+            return product_banks[pair % 2].tile([P, BANK], F32, name="product")
+
+        def step(u, at):
+            return AT["step"] + u * STEP + at
 
         def group(u):
             return u * ROWS // R
@@ -55,7 +61,6 @@ def tile_attend_gsl2_x_ts_kernel(tc, xT, wT, y, wt, ts, offs, out):
             return slice(u * ROWS % R, u * ROWS % R + ROWS)
 
         offsets = keep.tile([P, B * COLS], U16, name="offsets")
-        nc.sync.dma_start(offsets[:], offs)
         zero = keep.tile([P, 1], F32, name="zero")
         nc.vector.memset(zero[:], 0.0)
         ts_table = placed([P, T], F32, "ts_table", AT["ts"])
@@ -68,6 +73,7 @@ def tile_attend_gsl2_x_ts_kernel(tc, xT, wT, y, wt, ts, offs, out):
             nc.sync.dma_start(plane[:], wT.rearrange("(p t) c -> p t c", t=PACK)[:, t, :])
             planes.append(plane)
             if t == 0:
+                nc.sync.dma_start(offsets[:], offs)
                 nc.sync.dma_start(ts_table[0:1, :], ts[0:1, :])
                 nc.sync.dma_start(wt_rows[0:ROW_TILES, :], wt.rearrange("b (j n) o -> (b j) (n o)", n=P))
         x_raw, y_raw = {}, {}
@@ -77,10 +83,9 @@ def tile_attend_gsl2_x_ts_kernel(tc, xT, wT, y, wt, ts, offs, out):
             nc.sync.dma_start(x_raw[u][:], xT[group(u)].rearrange("(p t) r -> p t r", t=PACK)[:, :, rows_of(u)])
 
         for u in range(UNITS):
-            if u < B:
-                load_x(2 * u)
-                load_x(2 * u + 1)
-            y_raw[u] = placed([P, TILES, N], F32, f"y_raw{u}", AT["y"] if u == 0 else None)
+            for k in X_LOADS[u]:
+                load_x(k)
+            y_raw[u] = placed([P, TILES, N], F32, f"y_raw{u}", step(1, 5 * K) if u == 0 else None)
             nc.sync.dma_start(y_raw[u][:], y[group(u), rows_of(u), :].rearrange("(j n) i -> n j i", n=P))
 
         ident = keep.tile([P, P], F32, name="ident")
@@ -89,8 +94,8 @@ def tile_attend_gsl2_x_ts_kernel(tc, xT, wT, y, wt, ts, offs, out):
         nc.scalar.activation(half[:], zero[:], ACT.Sigmoid)
 
         def quantise(src, cols, fmt, name, at=None):
-            codes = placed([P, cols], U32, name + "_codes", at)
-            scales = placed([P, cols], U8, name + "_scales", None if at is None else at + 4 * cols)
+            codes = placed([P, cols], U32, name + "_codes")
+            scales = placed([P, cols], U8, name + "_scales", at)
             nc.vector.quantize_mx(out=codes[:].bitcast(fmt), scales=scales[:], in_=src)
             return codes, scales
 
@@ -129,8 +134,8 @@ def tile_attend_gsl2_x_ts_kernel(tc, xT, wT, y, wt, ts, offs, out):
         def turn_plane(t):
             a, e = divmod(t, 2)
             if e == 0:
-                by_slot[a] = placed([P, B * 2 * P * PACK], BF16, f"by_slot{a}", AT["x0"] if a else AT["ts"])
-            bank = out_banks.tile([P, BANK], F32, name="result")
+                by_slot[a] = placed([P, B * 2 * P * PACK], BF16, f"by_slot{a}", AT["x3"] if a else AT["ts"])
+            bank = product_bank(1)
             words = picked[:].bitcast(F32)
             for b in range(B):
                 first = (t * B + b) * N // 2
@@ -145,7 +150,7 @@ def tile_attend_gsl2_x_ts_kernel(tc, xT, wT, y, wt, ts, offs, out):
             )
 
         def quantise_by_slot(a):
-            w_slot_mx[a] = quantise(by_slot[a][:], D, E4M3, f"w_slot{a}", None if a else AT["woven0"])
+            w_slot_mx[a] = quantise(by_slot[a][:], D, E4M3, f"w_slot{a}", step(2, 4 * K) if a else AT["woven0"])
 
         def quantise_by_feature(b, pieces):
             by_feature = placed([P, N * PACK], BF16, f"by_feature{b}", AT["woven0"] - SLOT if b else None)
@@ -168,7 +173,7 @@ def tile_attend_gsl2_x_ts_kernel(tc, xT, wT, y, wt, ts, offs, out):
             )
 
         def quantise_x(u):
-            x_mx[u] = quantise(x_woven[u][:], ROWS, E4M3, f"x{u}")
+            x_mx[u] = quantise(x_woven[u][:], ROWS, E4M3, f"x{u}", step(1, 4 * K) if u + 1 == UNITS else None)
 
         probs, squares, slopes, targets, misses, hs, h_mx = {}, {}, {}, {}, {}, {}, {}
 
@@ -178,9 +183,9 @@ def tile_attend_gsl2_x_ts_kernel(tc, xT, wT, y, wt, ts, offs, out):
 
         def sigmoids(u):
             x_codes, x_scales = x_mx[u]
-            probs[u] = placed([P, PACK, ROWS], F32, f"prob{u}", None)
+            probs[u] = placed([P, PACK, ROWS], F32, f"prob{u}", None if u else AT["x2"])
             for a in range(2):
-                bank = score_banks.tile([P, BANK], F32, name="score")
+                bank = product_bank(0)
                 for e in range(2):
                     w_codes, w_scales = w_feature_mx[group(u), 2 * a + e]
                     nc.tensor.matmul_mx(
@@ -197,27 +202,27 @@ def tile_attend_gsl2_x_ts_kernel(tc, xT, wT, y, wt, ts, offs, out):
                     nc.scalar.activation(probs[u][:, t, :], bank[:, e * ROWS : (e + 1) * ROWS], ACT.Sigmoid, scale=scale_of(u, t))
 
         def square(u):
-            squares[u] = placed([P, PACK, ROWS], F32, f"square{u}", AT["step"] + u * STEP + SLOT // 2)
             for a in range(2):
-                pair = slice(2 * a, 2 * a + 2)
-                nc.scalar.activation(squares[u][:, pair, :], probs[u][:, pair, :], ACT.Square, bias=half[:], scale=-1.0)
+                at = AT["square"] + 2 * K * u if a == 0 else (None if u else step(2, 5 * K))
+                squares[u, a] = placed([P, 2, ROWS], F32, f"square{u}{a}", at)
+                nc.scalar.activation(squares[u, a][:], probs[u][:, 2 * a : 2 * a + 2, :], ACT.Square, bias=half[:], scale=-1.0)
 
         def slope(u):
-            slopes[u] = work.tile([P, PACK * ROWS], F32, name="slope", bufs=1 if u < VECTOR_SLOPES else 2, tag="slope" if u < VECTOR_SLOPES else "late_slope")
+            on_vector = u + 1 < UNITS
+            slopes[u] = placed([P, PACK * ROWS], F32, f"slope{u}", step(u, 0) if on_vector else None)
             for t in range(PACK):
                 dst = slopes[u][:].rearrange("p (c t i) -> p c t i", t=PACK, i=LINE)[:, :, t, :]
-                src = squares[u][:, t, :].rearrange("p (c i) -> p c i", i=LINE)
-                if u < VECTOR_SLOPES:
+                src = squares[u, t // 2][:, t % 2, :].rearrange("p (c i) -> p c i", i=LINE)
+                if on_vector:
                     nc.vector.tensor_scalar(dst, src, -0.25, scale_of(u, t), ALU.add, ALU.mult)
                 else:
                     nc.scalar.activation(dst, src, ACT.Identity, bias=scale_of(u, t, ts_quarter), scale=scale_of(u, t))
 
-        def weigh_targets(tiles, engine, at=None):
-            held = placed([P, len(tiles), N], F32, f"target{tiles[0]}", at)
-            for place, k in enumerate(tiles):
-                u, j = divmod(k, TILES)
-                targets[k] = held[:, place, :]
-                engine.tensor_scalar(targets[k], y_raw[u][:, j, :], wt_cols[:, k : k + 1], 0.0, ALU.mult, ALU.add)
+        def weigh_targets(k, engine):
+            u, j = divmod(k, TILES)
+            at = step(u, 4 * K - 64) if j == 0 else (step(u + 1, 6 * K) if u else None)
+            targets[k] = placed([P, N], F32, f"target{k}", at)
+            engine.tensor_scalar(targets[k][:], y_raw[u][:, j, :], wt_cols[:, k : k + 1], 0.0, ALU.mult, ALU.add)
 
         def miss(k):
             u, j = divmod(k, TILES)
@@ -229,7 +234,7 @@ def tile_attend_gsl2_x_ts_kernel(tc, xT, wT, y, wt, ts, offs, out):
                 weighted[:].rearrange("p (t s) -> p s t", t=PACK),
                 turned[:].rearrange("p (t s) -> p s t", t=PACK),
                 wt_minus[:, k : k + 1],
-                targets[k].rearrange("p (s t) -> p s t", t=PACK),
+                targets[k][:].rearrange("p (s t) -> p s t", t=PACK),
                 ALU.mult,
                 ALU.add,
             )
@@ -240,7 +245,7 @@ def tile_attend_gsl2_x_ts_kernel(tc, xT, wT, y, wt, ts, offs, out):
         def gradient(k):
             u, j = divmod(k, TILES)
             if j == 0:
-                hs[u] = placed([P, ROWS * PACK], BF16, f"h{u}", AT["step"] + (u + 1) * STEP)
+                hs[u] = placed([P, ROWS * PACK], BF16, f"h{u}", step(u + 3, 5 * K) if u + 2 < UNITS else None)
             nc.vector.tensor_tensor(
                 hs[u][:, j * BANK : (j + 1) * BANK].rearrange("p (c i t) -> p c t i", t=PACK, i=LINE),
                 misses[k][:].rearrange("p (t c i) -> p c t i", t=PACK, i=LINE),
@@ -250,34 +255,40 @@ def tile_attend_gsl2_x_ts_kernel(tc, xT, wT, y, wt, ts, offs, out):
 
         def quantise_h(first, tiles):
             u, j = divmod(first, TILES)
-            codes, scales = quantise(hs[u][:, j * BANK : (j + tiles) * BANK], tiles * P, E5M2, f"h{first}")
+            at = [AT["square"] + 2 * K, AT["square"] + 4 * K, step(3, 4 * K), None][u]
+            codes, scales = quantise(hs[u][:, j * BANK : (j + tiles) * BANK], tiles * P, E5M2, f"h{first}", at)
             for k in range(tiles):
                 h_mx[first + k] = codes[:, k * P : (k + 1) * P], scales[:, k * P : (k + 1) * P]
 
-        def product(k, a, bank):
-            h_codes, h_scales = h_mx[k]
-            w_codes, w_scales = w_slot_mx[a]
-            b = group(k // TILES)
-            cols = slice(b * D // 2, (b + 1) * D // 2)
-            nc.tensor.matmul_mx(
-                out=bank,
-                lhsT=h_codes.bitcast(E5M2),
-                lhsT_scale=h_scales,
-                rhs=w_codes[:, cols].bitcast(E4M3),
-                rhs_scale=w_scales[:, cols],
-                start=True,
-                stop=True,
-            )
-
-        def finish(k, copy, pool, name):
+        def finish(k, copy):
             u, j = divmod(k, TILES)
-            bank = pool.tile([P, BANK], F32, name=name)
-            for a in range(2):
-                product(k, a, bank[:, a * D // 2 : (a + 1) * D // 2])
-            staged = placed([P, D], F32, f"staged{k}", AT["planes"] + 4 * D * k)
-            copy(staged[:].rearrange("n (p t) -> n p t", t=PACK), bank[:].rearrange("n (t p) -> n p t", t=PACK))
+            h_codes, h_scales = h_mx[k]
+            bank = result_banks[u]()
+            for a in reversed(range(2)):
+                w_codes, w_scales = w_slot_mx[a]
+                cols = slice(group(u) * D // 2, (group(u) + 1) * D // 2)
+                nc.tensor.matmul_mx(
+                    out=bank[:, a * D // 2 : (a + 1) * D // 2],
+                    lhsT=h_codes.bitcast(E5M2),
+                    lhsT_scale=h_scales,
+                    rhs=w_codes[:, cols].bitcast(E4M3),
+                    rhs_scale=w_scales[:, cols],
+                    start=True,
+                    stop=True,
+                )
+            if j == 0:
+                staged[u] = placed([P, TILES, D], F32, f"staged{u}", AT["planes"] + u * SLOT)
+            copy(staged[u][:, j, :].rearrange("n (p t) -> n p t", t=PACK), bank[:].rearrange("n (t p) -> n p t", t=PACK))
             first = rows_of(u).start + j * P
-            nc.sync.dma_start(out[group(u), first : first + P, :], staged[:])
+            nc.sync.dma_start(out[group(u), first : first + P, :], staged[u][:, j, :])
+
+        staged = {}
+        result_banks = [
+            lambda: product_bank(1),
+            lambda: product_bank(0),
+            lambda: prob_banks.tile([P, BANK], F32, name="turned_prob"),
+            lambda: miss_banks.tile([P, BANK], F32, name="turned_miss"),
+        ]
 
         for t in range(PACK):
             gather(t)
@@ -286,49 +297,47 @@ def tile_attend_gsl2_x_ts_kernel(tc, xT, wT, y, wt, ts, offs, out):
         weave_x(0, AT["woven0"] - SLOT // 4)
         quantise_by_feature(0, 2)
         quantise_x(0)
-        turn_plane(2)
-        turn_plane(3)
         weave_x(1)
-        sigmoids(0)
         weave_x(2)
+        sigmoids(0)
         square(0)
         quantise_x(1)
         quantise_by_feature(1, 1)
+        quantise_x(2)
         quantise_by_slot(0)
-        weigh_targets(range(TILES), nc.vector)
-        weigh_targets([TILES], nc.gpsimd, AT["y"])
+        for k in range(TILES):
+            weigh_targets(k, nc.vector)
+        weigh_targets(TILES, nc.gpsimd)
         miss(0)
         miss(1)
         sigmoids(1)
         weave_x(3)
         for u in range(UNITS):
             first = u * TILES
-            if u + 2 < UNITS:
-                quantise_x(u + 2)
-            if u < VECTOR_SLOPES:
-                slope(u)
-            if u == 0:
+            if u == 1:
+                quantise_x(3)
+            if u == 2:
                 quantise_by_slot(1)
+            if u + 1 < UNITS:
+                slope(u)
             if u:
                 quantise_h(first - TILES, TILES)
-            if u + 1 < UNITS:
-                ahead = range(first + TILES + 1, min(first + 2 * TILES + 1, ROW_TILES))
-                weigh_targets(ahead, nc.gpsimd, AT["step"] + u * STEP + SLOT // 4)
+            for k in range(first + TILES + 1, min(first + 2 * TILES + 1, ROW_TILES)):
+                weigh_targets(k, nc.gpsimd)
             gradient(first)
             gradient(first + 1)
             if u + 1 < UNITS:
                 square(u + 1)
-                if u + 1 >= VECTOR_SLOPES:
+                if u + 2 == UNITS:
                     slope(u + 1)
                 miss(first + TILES)
                 miss(first + TILES + 1)
             if u + 2 < UNITS:
                 sigmoids(u + 2)
-            if u:
-                banks = (out_banks, "result") if u + 1 < UNITS else (score_banks, "score")
-                finish(first - 2, nc.scalar.copy, *banks)
-                finish(first - 1, nc.scalar.copy, *banks)
+            if u == 0:
+                turn_plane(2)
+                turn_plane(3)
         quantise_h(ROW_TILES - 2, 1)
         quantise_h(ROW_TILES - 1, 1)
-        finish(ROW_TILES - 2, nc.scalar.copy, prob_banks, "turned_prob")
-        finish(ROW_TILES - 1, nc.vector.tensor_copy, prob_banks, "turned_prob")
+        for k in range(ROW_TILES):
+            finish(k, nc.vector.tensor_copy if k in (7,) else nc.scalar.copy)

@@ -29,7 +29,7 @@ COLS = N // 16
 X_LOADS = ((0, 1, 2), (3,), (), ())
 SLOT = 4 * PACK * ROWS
 K = 1024
-AT = {"ts": 0, "x3": 8 * K, "x2": 12 * K, "woven0": 24 * K, "square": 28 * K, "step": 36 * K, "planes": 76 * K}
+AT = {"ts": 0, "x3": 8 * K, "x2": 12 * K, "x0": 16 * K, "woven0": 26 * K, "square": 28 * K, "step": 36 * K, "planes": 76 * K, "picked": 108 * K}
 STEP = 8 * K
 
 
@@ -63,8 +63,8 @@ def tile_attend_gsl2_x_ts_kernel(tc, xT, wT, y, wt, ts, offs, out):
         offsets = keep.tile([P, B * COLS], U16, name="offsets")
         zero = keep.tile([P, 1], F32, name="zero")
         nc.vector.memset(zero[:], 0.0)
-        ts_table = placed([P, T], F32, "ts_table", AT["ts"])
-        nc.vector.memset(ts_table[:], 0.0)
+        ts_cut = placed([P, T // P], F32, "ts_cut", AT["picked"])
+        nc.sync.dma_start(ts_cut[:], ts[0].rearrange("(n j) -> n j", n=P))
         wt_rows = keep.tile([P, P], F32, name="wt_rows")
         nc.vector.memset(wt_rows[:], 0.0)
         planes = []
@@ -74,8 +74,7 @@ def tile_attend_gsl2_x_ts_kernel(tc, xT, wT, y, wt, ts, offs, out):
             planes.append(plane)
             if t == 0:
                 nc.sync.dma_start(offsets[:], offs)
-                nc.sync.dma_start(ts_table[0:1, :], ts[0:1, :])
-                nc.sync.dma_start(wt_rows[0:ROW_TILES, :], wt.rearrange("b (j n) o -> (b j) (n o)", n=P))
+                nc.sync.dma_start(wt_rows[0 : 2 * ROW_TILES : 2, :], wt.rearrange("b (j n) o -> (b j) (n o)", n=P))
         x_raw, y_raw = {}, {}
 
         def load_x(u):
@@ -99,27 +98,40 @@ def tile_attend_gsl2_x_ts_kernel(tc, xT, wT, y, wt, ts, offs, out):
             nc.vector.quantize_mx(out=codes[:].bitcast(fmt), scales=scales[:], in_=src)
             return codes, scales
 
-        ts_picked = keep.tile([P, B * N], F32, name="ts_picked")
-        for b in range(B):
-            nc.scalar.activation(
-                ts_picked[:, b * N : (b + 1) * N], ts_table[:].indirect(offsets[:, b * COLS : (b + 1) * COLS]), ACT.Copy
+        ts_table = placed([P, T], F32, "ts_table", AT["ts"])
+        for q in range(T // BANK):
+            bank = product_bank(q)
+            for j in range(LINE):
+                column = ts_cut[:, LINE * q + j : LINE * q + j + 1].to_broadcast([P, P])
+                nc.tensor.transpose(bank[:, j * P : (j + 1) * P], column, ident[:])
+            (nc.scalar.copy if q else nc.vector.tensor_copy)(
+                ts_table[:].rearrange("p (n q j) -> p q n j", n=P, j=LINE)[:, q],
+                bank[:].rearrange("p (j n) -> p n j", j=LINE),
             )
-        column_bank = prob_banks.tile([P, BANK], F32, name="turned_prob")
-        nc.tensor.transpose(column_bank[:, BANK - P :], wt_rows[:], ident[:])
-        for k in range(B * PACK):
-            b, t = divmod(k, PACK)
-            nc.tensor.transpose(column_bank[:, 2 * k : 2 * k + P], ts_picked[:, b * N + t : (b + 1) * N : PACK], ident[:])
+        ts_picked = keep.tile([P, B * N], F32, name="ts_picked")
+        nc.scalar.activation(ts_picked[:], ts_table[:].indirect(offsets[:]), ACT.Copy)
+        ts_dealt = keep.tile([P, B * N], F32, name="ts_dealt")
+        nc.scalar.copy(
+            ts_dealt[:].rearrange("p (b t q i) -> p b q t i", b=B, t=PACK, i=LINE),
+            ts_picked[:].rearrange("p (b q i t) -> p b q t i", b=B, t=PACK, i=LINE),
+        )
+        wt_scaled = placed([P, P], F32, "wt_scaled", AT["ts"] + SLOT)
+        nc.scalar.activation(wt_scaled[:], wt_rows[:], ACT.Copy, scale=4.0)
 
-        def columns(name, src, scale):
-            tile = keep.tile([P, ROW_TILES], F32, name=name)
-            nc.scalar.activation(tile[:], src, ACT.Copy, scale=scale)
-            return tile
+        def columns():
+            bank = prob_banks.tile([P, BANK], F32, name="turned_prob")
+            for k in range(B * PACK):
+                nc.tensor.transpose(bank[:, 2 * k : 2 * k + P], ts_dealt[:, k * P : (k + 1) * P], ident[:])
+            nc.tensor.transpose(bank[:, 2 * B * PACK : 2 * B * PACK + P], wt_scaled[:], ident[:])
+            count = B * PACK + ROW_TILES
+            tiles = []
+            for place, scale in enumerate((1.0, -0.25)):
+                tile = placed([P, count], F32, f"columns{place}", AT["x0"] + 64 * place)
+                nc.scalar.activation(tile[:], bank[:, 0 : 2 * count : 2], ACT.Copy, scale=scale)
+                tiles += [tile[:, : B * PACK], tile[:, B * PACK :]]
+            return tiles
 
-        ts_turned, wt_turned = column_bank[:, 0 : 2 * B * PACK : 2], column_bank[:, BANK - P : BANK - P + ROW_TILES]
-        ts_cols, ts_quarter = columns("ts_cols", ts_turned, 1.0), columns("ts_quarter", ts_turned, -0.25)
-        wt_cols, wt_minus = columns("wt_cols", wt_turned, 1.0), columns("wt_minus", wt_turned, -1.0)
-
-        picked = keep.tile([P, PACK * B * N], BF16, name="picked", align_bytes=64)
+        picked = placed([P, PACK * B * N], BF16, "picked", AT["picked"])
         by_slot, w_slot_mx, w_feature_mx, x_woven, x_mx = {}, {}, {}, {}, {}
 
         def gather(t):
@@ -150,7 +162,7 @@ def tile_attend_gsl2_x_ts_kernel(tc, xT, wT, y, wt, ts, offs, out):
             )
 
         def quantise_by_slot(a):
-            w_slot_mx[a] = quantise(by_slot[a][:], D, E4M3, f"w_slot{a}", step(2, 4 * K) if a else AT["woven0"])
+            w_slot_mx[a] = quantise(by_slot[a][:], D, E4M3, f"w_slot{a}", step(2, 4 * K) if a else AT["square"])
 
         def quantise_by_feature(b, pieces):
             by_feature = placed([P, N * PACK], BF16, f"by_feature{b}", AT["woven0"] - SLOT if b else None)
@@ -177,7 +189,7 @@ def tile_attend_gsl2_x_ts_kernel(tc, xT, wT, y, wt, ts, offs, out):
 
         probs, squares, slopes, targets, misses, hs, h_mx = {}, {}, {}, {}, {}, {}, {}
 
-        def scale_of(u, t, cols=ts_cols):
+        def scale_of(u, t, cols):
             k = group(u) * PACK + t
             return cols[:, k : k + 1]
 
@@ -199,7 +211,7 @@ def tile_attend_gsl2_x_ts_kernel(tc, xT, wT, y, wt, ts, offs, out):
                     )
                 for e in range(2):
                     t = 2 * a + e
-                    nc.scalar.activation(probs[u][:, t, :], bank[:, e * ROWS : (e + 1) * ROWS], ACT.Sigmoid, scale=scale_of(u, t))
+                    nc.scalar.activation(probs[u][:, t, :], bank[:, e * ROWS : (e + 1) * ROWS], ACT.Sigmoid, scale=scale_of(u, t, ts_cols))
 
         def square(u):
             for a in range(2):
@@ -214,15 +226,15 @@ def tile_attend_gsl2_x_ts_kernel(tc, xT, wT, y, wt, ts, offs, out):
                 dst = slopes[u][:].rearrange("p (c t i) -> p c t i", t=PACK, i=LINE)[:, :, t, :]
                 src = squares[u, t // 2][:, t % 2, :].rearrange("p (c i) -> p c i", i=LINE)
                 if on_vector:
-                    nc.vector.tensor_scalar(dst, src, -0.25, scale_of(u, t), ALU.add, ALU.mult)
+                    nc.vector.tensor_scalar(dst, src, -0.25, scale_of(u, t, ts_cols), ALU.add, ALU.mult)
                 else:
-                    nc.scalar.activation(dst, src, ACT.Identity, bias=scale_of(u, t, ts_quarter), scale=scale_of(u, t))
+                    nc.scalar.activation(dst, src, ACT.Identity, bias=scale_of(u, t, ts_quarter), scale=scale_of(u, t, ts_cols))
 
         def weigh_targets(k, engine):
             u, j = divmod(k, TILES)
             at = step(u, 4 * K - 64) if j == 0 else (step(u + 1, 6 * K) if u else None)
             targets[k] = placed([P, N], F32, f"target{k}", at)
-            engine.tensor_scalar(targets[k][:], y_raw[u][:, j, :], wt_cols[:, k : k + 1], 0.0, ALU.mult, ALU.add)
+            engine.tensor_scalar(targets[k][:], y_raw[u][:, j, :], wt_fourfold[:, k : k + 1], 0.25, ALU.mult, ALU.mult)
 
         def miss(k):
             u, j = divmod(k, TILES)
@@ -295,6 +307,7 @@ def tile_attend_gsl2_x_ts_kernel(tc, xT, wT, y, wt, ts, offs, out):
             if t < 2:
                 turn_plane(t)
         weave_x(0, AT["woven0"] - SLOT // 4)
+        ts_cols, wt_fourfold, ts_quarter, wt_minus = columns()
         quantise_by_feature(0, 2)
         quantise_x(0)
         weave_x(1)
@@ -304,7 +317,6 @@ def tile_attend_gsl2_x_ts_kernel(tc, xT, wT, y, wt, ts, offs, out):
         quantise_x(1)
         quantise_by_feature(1, 1)
         quantise_x(2)
-        quantise_by_slot(0)
         for k in range(TILES):
             weigh_targets(k, nc.vector)
         weigh_targets(TILES, nc.gpsimd)
@@ -322,6 +334,8 @@ def tile_attend_gsl2_x_ts_kernel(tc, xT, wT, y, wt, ts, offs, out):
                 slope(u)
             if u:
                 quantise_h(first - TILES, TILES)
+            else:
+                quantise_by_slot(0)
             for k in range(first + TILES + 1, min(first + 2 * TILES + 1, ROW_TILES)):
                 weigh_targets(k, nc.gpsimd)
             gradient(first)

@@ -28,8 +28,9 @@ LINE = 4
 COLS = N // 16
 X_LOADS = ((0, 1, 2), (3,), (), ())
 SLOT = 4 * PACK * ROWS
+VECTOR_SHARE = (800, 800, 800, 512)
 K = 1024
-AT = {"ts": 0, "x3": 8 * K, "x2": 12 * K, "x0": 16 * K, "woven0": 26 * K, "square": 28 * K, "step": 36 * K, "planes": 76 * K, "picked": 108 * K}
+AT = {"ts": 0, "x3": 8 * K, "x0": 16 * K, "woven0": 26 * K, "square": 28 * K, "step": 36 * K, "planes": 76 * K}
 STEP = 8 * K
 
 
@@ -61,10 +62,11 @@ def tile_attend_gsl2_x_ts_kernel(tc, xT, wT, y, wt, ts, offs, out):
             return slice(u * ROWS % R, u * ROWS % R + ROWS)
 
         offsets = keep.tile([P, B * COLS], U16, name="offsets")
+        nc.sync.dma_start(offsets[:], offs)
         zero = keep.tile([P, 1], F32, name="zero")
         nc.vector.memset(zero[:], 0.0)
-        ts_cut = placed([P, T // P], F32, "ts_cut", AT["picked"])
-        nc.sync.dma_start(ts_cut[:], ts[0].rearrange("(n j) -> n j", n=P))
+        ts_table = placed([P, T], F32, "ts_table", AT["ts"])
+        nc.vector.memset(ts_table[:], 0.0)
         wt_rows = keep.tile([P, P], F32, name="wt_rows")
         nc.vector.memset(wt_rows[:], 0.0)
         planes = []
@@ -73,7 +75,7 @@ def tile_attend_gsl2_x_ts_kernel(tc, xT, wT, y, wt, ts, offs, out):
             nc.sync.dma_start(plane[:], wT.rearrange("(p t) c -> p t c", t=PACK)[:, t, :])
             planes.append(plane)
             if t == 0:
-                nc.sync.dma_start(offsets[:], offs)
+                nc.sync.dma_start(ts_table[0:1, :], ts[0:1, :])
                 nc.sync.dma_start(wt_rows[0 : 2 * ROW_TILES : 2, :], wt.rearrange("b (j n) o -> (b j) (n o)", n=P))
         x_raw, y_raw = {}, {}
 
@@ -98,45 +100,31 @@ def tile_attend_gsl2_x_ts_kernel(tc, xT, wT, y, wt, ts, offs, out):
             nc.vector.quantize_mx(out=codes[:].bitcast(fmt), scales=scales[:], in_=src)
             return codes, scales
 
-        ts_table = placed([P, T], F32, "ts_table", AT["ts"])
-        for q in range(T // BANK):
-            bank = product_bank(q)
-            for j in range(LINE):
-                column = ts_cut[:, LINE * q + j : LINE * q + j + 1].to_broadcast([P, P])
-                nc.tensor.transpose(bank[:, j * P : (j + 1) * P], column, ident[:])
-            (nc.scalar.copy if q else nc.vector.tensor_copy)(
-                ts_table[:].rearrange("p (n q j) -> p q n j", n=P, j=LINE)[:, q],
-                bank[:].rearrange("p (j n) -> p n j", j=LINE),
-            )
         ts_picked = keep.tile([P, B * N], F32, name="ts_picked")
-        nc.scalar.activation(ts_picked[:], ts_table[:].indirect(offsets[:]), ACT.Copy)
-        ts_dealt = keep.tile([P, B * N], F32, name="ts_dealt")
-        nc.scalar.copy(
-            ts_dealt[:].rearrange("p (b t q i) -> p b q t i", b=B, t=PACK, i=LINE),
-            ts_picked[:].rearrange("p (b q i t) -> p b q t i", b=B, t=PACK, i=LINE),
-        )
-        wt_scaled = placed([P, P], F32, "wt_scaled", AT["ts"] + SLOT)
-        nc.scalar.activation(wt_scaled[:], wt_rows[:], ACT.Copy, scale=4.0)
 
         def columns():
+            wt_scaled = placed([P, P], F32, "wt_scaled", AT["planes"] + 4 * T)
+            nc.scalar.activation(wt_scaled[:], wt_rows[:], ACT.Copy, scale=4.0)
             bank = prob_banks.tile([P, BANK], F32, name="turned_prob")
+            nc.tensor.transpose(bank[:, BANK // 2 : BANK // 2 + P], wt_scaled[:], ident[:])
             for k in range(B * PACK):
-                nc.tensor.transpose(bank[:, 2 * k : 2 * k + P], ts_dealt[:, k * P : (k + 1) * P], ident[:])
-            nc.tensor.transpose(bank[:, 2 * B * PACK : 2 * B * PACK + P], wt_scaled[:], ident[:])
+                b, t = divmod(k, PACK)
+                nc.tensor.transpose(bank[:, 2 * k : 2 * k + P], ts_picked[:, b * N + t : (b + 1) * N : PACK], ident[:])
             count = B * PACK + ROW_TILES
             tiles = []
             for place, scale in enumerate((1.0, -0.25)):
                 tile = placed([P, count], F32, f"columns{place}", AT["x0"] + 64 * place)
-                nc.scalar.activation(tile[:], bank[:, 0 : 2 * count : 2], ACT.Copy, scale=scale)
+                turned = bank[:].rearrange("p (h c) -> p h c", h=2)[:, :, 0:count:2]
+                nc.scalar.activation(tile[:].rearrange("p (h c) -> p h c", h=2), turned, ACT.Copy, scale=scale)
                 tiles += [tile[:, : B * PACK], tile[:, B * PACK :]]
             return tiles
 
-        picked = placed([P, PACK * B * N], BF16, "picked", AT["picked"])
+        picked = placed([P, PACK * B * N], BF16, "picked")
         by_slot, w_slot_mx, w_feature_mx, x_woven, x_mx = {}, {}, {}, {}, {}
 
         def gather(t):
             first = t * B * N
-            cut = B * N if t < PACK - 1 else N
+            cut = VECTOR_SHARE[t]
             nc.vector.tensor_copy(picked[:, first : first + cut], planes[t][:].indirect(offsets[:, : cut // 16]))
             if cut < B * N:
                 nc.scalar.activation(
@@ -179,7 +167,7 @@ def tile_attend_gsl2_x_ts_kernel(tc, xT, wT, y, wt, ts, offs, out):
 
         def weave_x(u, at=None):
             x_woven[u] = placed([P, ROWS * PACK], BF16, f"x_woven{u}", at)
-            nc.scalar.copy(
+            (nc.vector.tensor_copy if u == 2 else nc.scalar.copy)(
                 x_woven[u][:].rearrange("p (q n t) -> p q t n", n=LINE, t=PACK),
                 x_raw[u][:].rearrange("p t (q n) -> p q t n", n=LINE),
             )
@@ -195,7 +183,7 @@ def tile_attend_gsl2_x_ts_kernel(tc, xT, wT, y, wt, ts, offs, out):
 
         def sigmoids(u):
             x_codes, x_scales = x_mx[u]
-            probs[u] = placed([P, PACK, ROWS], F32, f"prob{u}", None if u else AT["x2"])
+            probs[u] = placed([P, PACK, ROWS], F32, f"prob{u}", None)
             for a in range(2):
                 bank = product_bank(0)
                 for e in range(2):
@@ -304,6 +292,8 @@ def tile_attend_gsl2_x_ts_kernel(tc, xT, wT, y, wt, ts, offs, out):
 
         for t in range(PACK):
             gather(t)
+            if t == 0:
+                nc.scalar.activation(ts_picked[:], ts_table[:].indirect(offsets[:]), ACT.Copy)
             if t < 2:
                 turn_plane(t)
         weave_x(0, AT["woven0"] - SLOT // 4)
@@ -311,14 +301,14 @@ def tile_attend_gsl2_x_ts_kernel(tc, xT, wT, y, wt, ts, offs, out):
         quantise_by_feature(0, 2)
         quantise_x(0)
         weave_x(1)
-        weave_x(2)
         sigmoids(0)
         square(0)
         quantise_x(1)
         quantise_by_feature(1, 1)
-        quantise_x(2)
+        weave_x(2)
         for k in range(TILES):
             weigh_targets(k, nc.vector)
+        quantise_x(2)
         weigh_targets(TILES, nc.gpsimd)
         miss(0)
         miss(1)

@@ -28,7 +28,7 @@ LINE = 4
 COLS = N // 16
 X_LOADS = ((0, 1, 2), (3,), (), ())
 SLOT = 4 * PACK * ROWS
-VECTOR_SHARE = (800, 800, 800, 512)
+VECTOR_SHARE = (832, 864, 864, 512)
 K = 1024
 AT = {"ts": 0, "x3": 8 * K, "x0": 16 * K, "woven0": 26 * K, "square": 28 * K, "step": 36 * K, "planes": 76 * K}
 STEP = 8 * K

@@ -28,7 +28,7 @@ LINE = 4
 COLS = N // 16
 X_LOADS = ((0, 1, 2), (3,), (), ())
 SLOT = 4 * PACK * ROWS
-VECTOR_SHARE = (832, 864, 864, 512)
+VECTOR_SHARE = (832, 864, 864, 384)
 K = 1024
 AT = {"ts": 0, "x3": 8 * K, "x0": 16 * K, "woven0": 26 * K, "square": 28 * K, "step": 36 * K, "planes": 76 * K}
 STEP = 8 * K
@@ -62,7 +62,6 @@ def tile_attend_gsl2_x_ts_kernel(tc, xT, wT, y, wt, ts, offs, out):
             return slice(u * ROWS % R, u * ROWS % R + ROWS)
 
         offsets = keep.tile([P, B * COLS], U16, name="offsets")
-        nc.sync.dma_start(offsets[:], offs)
         zero = keep.tile([P, 1], F32, name="zero")
         nc.vector.memset(zero[:], 0.0)
         ts_table = placed([P, T], F32, "ts_table", AT["ts"])
@@ -75,6 +74,7 @@ def tile_attend_gsl2_x_ts_kernel(tc, xT, wT, y, wt, ts, offs, out):
             nc.sync.dma_start(plane[:], wT.rearrange("(p t) c -> p t c", t=PACK)[:, t, :])
             planes.append(plane)
             if t == 0:
+                nc.sync.dma_start(offsets[:], offs)
                 nc.sync.dma_start(ts_table[0:1, :], ts[0:1, :])
                 nc.sync.dma_start(wt_rows[0 : 2 * ROW_TILES : 2, :], wt.rearrange("b (j n) o -> (b j) (n o)", n=P))
         x_raw, y_raw = {}, {}
@@ -126,10 +126,11 @@ def tile_attend_gsl2_x_ts_kernel(tc, xT, wT, y, wt, ts, offs, out):
             first = t * B * N
             cut = VECTOR_SHARE[t]
             nc.vector.tensor_copy(picked[:, first : first + cut], planes[t][:].indirect(offsets[:, : cut // 16]))
-            if cut < B * N:
-                nc.scalar.activation(
-                    picked[:, first + cut : first + B * N], planes[t][:].indirect(offsets[:, cut // 16 :]), ACT.Copy
-                )
+            for lo, hi in ((cut, N), (max(cut, N), B * N)):
+                if lo < hi:
+                    nc.scalar.activation(
+                        picked[:, first + lo : first + hi], planes[t][:].indirect(offsets[:, lo // 16 : hi // 16]), ACT.Copy
+                    )
 
         def turn_plane(t):
             a, e = divmod(t, 2)
@@ -222,7 +223,14 @@ def tile_attend_gsl2_x_ts_kernel(tc, xT, wT, y, wt, ts, offs, out):
             u, j = divmod(k, TILES)
             at = step(u, 4 * K - 64) if j == 0 else (step(u + 1, 6 * K) if u else None)
             targets[k] = placed([P, N], F32, f"target{k}", at)
-            engine.tensor_scalar(targets[k][:], y_raw[u][:, j, :], wt_fourfold[:, k : k + 1], 0.25, ALU.mult, ALU.mult)
+            engine.tensor_scalar(
+                targets[k][:].rearrange("p (t q i) -> p q t i", t=PACK, i=LINE),
+                y_raw[u][:, j, :].rearrange("p (q i t) -> p q t i", t=PACK, i=LINE),
+                wt_fourfold[:, k : k + 1],
+                0.25,
+                ALU.mult,
+                ALU.mult,
+            )
 
         def miss(k):
             u, j = divmod(k, TILES)
@@ -230,14 +238,7 @@ def tile_attend_gsl2_x_ts_kernel(tc, xT, wT, y, wt, ts, offs, out):
             for t in reversed(range(PACK)):
                 nc.tensor.transpose(turned[:, t * P : (t + 1) * P], probs[u][:, t, j * P : (j + 1) * P], ident[:])
             weighted = work.tile([P, N], F32, name="weighted")
-            nc.vector.scalar_tensor_tensor(
-                weighted[:].rearrange("p (t s) -> p s t", t=PACK),
-                turned[:].rearrange("p (t s) -> p s t", t=PACK),
-                wt_minus[:, k : k + 1],
-                targets[k][:].rearrange("p (s t) -> p s t", t=PACK),
-                ALU.mult,
-                ALU.add,
-            )
+            nc.vector.scalar_tensor_tensor(weighted[:], turned[:], wt_minus[:, k : k + 1], targets[k][:], ALU.mult, ALU.add)
             misses[k] = miss_banks.tile([P, BANK], F32, name="turned_miss")
             for t in range(PACK):
                 nc.tensor.transpose(misses[k][:, t * P : (t + 1) * P], weighted[:, t * P : (t + 1) * P], ident[:])

@@ -28,7 +28,7 @@ LINE = 4
 COLS = N // 16
 X_LOADS = ((0, 1, 2), (3,), (), ())
 SLOT = 4 * PACK * ROWS
-VECTOR_SHARE = (832, 864, 864, 384)
+VECTOR_SHARE = (576, 576, 640, 384)
 K = 1024
 AT = {"ts": 0, "x3": 8 * K, "x0": 16 * K, "woven0": 26 * K, "square": 28 * K, "step": 36 * K, "planes": 76 * K}
 STEP = 8 * K
@@ -64,19 +64,18 @@ def tile_attend_gsl2_x_ts_kernel(tc, xT, wT, y, wt, ts, offs, out):
         offsets = keep.tile([P, B * COLS], U16, name="offsets")
         zero = keep.tile([P, 1], F32, name="zero")
         nc.vector.memset(zero[:], 0.0)
+        nc.sync.dma_start(offsets[:], offs)
         ts_table = placed([P, T], F32, "ts_table", AT["ts"])
-        nc.vector.memset(ts_table[:], 0.0)
+        nc.scalar.dma_start(ts_table[P - 1 :, :], ts[0:1, :])
         wt_rows = keep.tile([P, P], F32, name="wt_rows")
-        nc.vector.memset(wt_rows[:], 0.0)
+        nc.scalar.dma_start(wt_rows[P - ROW_TILES :, :], wt.rearrange("b (j n) o -> (b j) (n o)", n=P))
+        nc.vector.memset(ts_table[: P - 1, :], 0.0)
+        nc.vector.memset(wt_rows[: P - ROW_TILES, :], 0.0)
         planes = []
         for t in range(PACK):
             plane = placed([P, T], F32, f"plane{t}", AT["planes"] + 4 * T * t)
             nc.sync.dma_start(plane[:], wT.rearrange("(p t) c -> p t c", t=PACK)[:, t, :])
             planes.append(plane)
-            if t == 0:
-                nc.sync.dma_start(offsets[:], offs)
-                nc.sync.dma_start(ts_table[0:1, :], ts[0:1, :])
-                nc.sync.dma_start(wt_rows[0 : 2 * ROW_TILES : 2, :], wt.rearrange("b (j n) o -> (b j) (n o)", n=P))
         x_raw, y_raw = {}, {}
 
         def load_x(u):
@@ -100,23 +99,22 @@ def tile_attend_gsl2_x_ts_kernel(tc, xT, wT, y, wt, ts, offs, out):
             nc.vector.quantize_mx(out=codes[:].bitcast(fmt), scales=scales[:], in_=src)
             return codes, scales
 
-        ts_picked = keep.tile([P, B * N], F32, name="ts_picked")
+        ts_picked = [keep.tile([P, N], F32, name=f"ts_picked{b}") for b in range(B)]
+        nc.vector.tensor_copy(ts_picked[0][:], ts_table[:].indirect(offsets[:, :COLS]))
+        nc.scalar.activation(ts_picked[1][:], ts_table[:].indirect(offsets[:, COLS:]), ACT.Copy)
 
         def columns():
-            wt_scaled = placed([P, P], F32, "wt_scaled", AT["planes"] + 4 * T)
-            nc.scalar.activation(wt_scaled[:], wt_rows[:], ACT.Copy, scale=4.0)
             bank = prob_banks.tile([P, BANK], F32, name="turned_prob")
-            nc.tensor.transpose(bank[:, BANK // 2 : BANK // 2 + P], wt_scaled[:], ident[:])
-            for k in range(B * PACK):
+            nc.tensor.transpose(bank[:, BANK - P :], wt_rows[:], ident[:])
+            for k in reversed(range(B * PACK)):
                 b, t = divmod(k, PACK)
-                nc.tensor.transpose(bank[:, 2 * k : 2 * k + P], ts_picked[:, b * N + t : (b + 1) * N : PACK], ident[:])
-            count = B * PACK + ROW_TILES
+                nc.tensor.transpose(bank[:, 2 * k : 2 * k + P], ts_picked[b][:, t::PACK], ident[:])
             tiles = []
-            for place, scale in enumerate((1.0, -0.25)):
-                tile = placed([P, count], F32, f"columns{place}", AT["x0"] + 64 * place)
-                turned = bank[:].rearrange("p (h c) -> p h c", h=2)[:, :, 0:count:2]
-                nc.scalar.activation(tile[:].rearrange("p (h c) -> p h c", h=2), turned, ACT.Copy, scale=scale)
-                tiles += [tile[:, : B * PACK], tile[:, B * PACK :]]
+            for place, (name, scale) in enumerate((("ts", 1.0), ("wt", 1.0), ("ts", -0.25), ("wt", -1.0))):
+                tile = placed([P, ROW_TILES], F32, f"columns{place}", AT["x0"] + 64 * place)
+                turned = bank[:, P - 1 : P - 1 + 2 * B * PACK : 2] if name == "ts" else bank[:, BANK - ROW_TILES :]
+                nc.scalar.activation(tile[:], turned, ACT.Copy, scale=scale)
+                tiles.append(tile)
             return tiles
 
         picked = placed([P, PACK * B * N], BF16, "picked")
@@ -135,7 +133,7 @@ def tile_attend_gsl2_x_ts_kernel(tc, xT, wT, y, wt, ts, offs, out):
         def turn_plane(t):
             a, e = divmod(t, 2)
             if e == 0:
-                by_slot[a] = placed([P, B * 2 * P * PACK], BF16, f"by_slot{a}", AT["x3"] if a else AT["ts"])
+                by_slot[a] = placed([P, B * 2 * P * PACK], BF16, f"by_slot{a}", AT["x3"] if a else AT["planes"] + 4 * T)
             bank = product_bank(1)
             words = picked[:].bitcast(F32)
             for b in range(B):
@@ -226,10 +224,10 @@ def tile_attend_gsl2_x_ts_kernel(tc, xT, wT, y, wt, ts, offs, out):
             engine.tensor_scalar(
                 targets[k][:].rearrange("p (t q i) -> p q t i", t=PACK, i=LINE),
                 y_raw[u][:, j, :].rearrange("p (q i t) -> p q t i", t=PACK, i=LINE),
-                wt_fourfold[:, k : k + 1],
-                0.25,
+                wt_cols[:, k : k + 1],
+                0.0,
                 ALU.mult,
-                ALU.mult,
+                ALU.add,
             )
 
         def miss(k):
@@ -293,12 +291,10 @@ def tile_attend_gsl2_x_ts_kernel(tc, xT, wT, y, wt, ts, offs, out):
 
         for t in range(PACK):
             gather(t)
-            if t == 0:
-                nc.scalar.activation(ts_picked[:], ts_table[:].indirect(offsets[:]), ACT.Copy)
             if t < 2:
                 turn_plane(t)
         weave_x(0, AT["woven0"] - SLOT // 4)
-        ts_cols, wt_fourfold, ts_quarter, wt_minus = columns()
+        ts_cols, wt_cols, ts_quarter, wt_minus = columns()
         quantise_by_feature(0, 2)
         quantise_x(0)
         weave_x(1)

@@ -26,12 +26,9 @@ UNITS = B * R // ROWS
 ROW_TILES = B * R // P
 LINE = 4
 COLS = N // 16
-X_LOADS = ((0, 1, 2), (3,), (), ())
-SLOT = 4 * PACK * ROWS
-VECTOR_SHARE = (576, 576, 640, 384)
-K = 1024
-AT = {"ts": 0, "x3": 8 * K, "x0": 16 * K, "woven0": 26 * K, "square": 28 * K, "step": 36 * K, "planes": 76 * K}
-STEP = 8 * K
+VECTOR_SHARE = (576, 576, 640)
+LAST_SHARE = (288, 128)
+AT = {"plane0":0,"plane1":8256,"plane2":16512,"plane3":24768,"ts":33024,"y0":41280,"tg2":45312,"sl1":47296,"sl0":51456,"tg0":55488,"tg3":57600,"sq01":59584,"tg4":61568,"sl2":63552,"sq00":67712,"sq10":69824,"sq20":71936,"tg5":74048,"h0":76032,"tg6":78016,"h1":80128,"tg7":82112,"x3":84224,"x0":88384,"bf1":92416,"h3":96576,"bs1":84224,"bs0":8256,"ws0_scales":67712,"ws1_scales":62080,"st0":33024,"st1":37120,"st2":12352,"st3":4096,"columns0":0,"columns1":64,"columns2":128,"columns3":192,"xq3_scales":45824,"hq0_scales":69824,"hq2_scales":71936,"hq4_scales":78528}
 
 
 def tile_attend_gsl2_x_ts_kernel(tc, xT, wT, y, wt, ts, offs, out):
@@ -44,16 +41,14 @@ def tile_attend_gsl2_x_ts_kernel(tc, xT, wT, y, wt, ts, offs, out):
         prob_banks = ctx.enter_context(tc.psum_pool(name="prob_banks", bufs=2))
         miss_banks = ctx.enter_context(tc.psum_pool(name="miss_banks", bufs=2))
 
-        def placed(shape, dtype, name, at=None):
+        def placed(shape, dtype, name):
+            at = AT.get(name)
             if at is None:
                 return keep.tile(shape, dtype, name=name, align_bytes=64)
             return shared.tile(shape, dtype, name=name, offset=at, align_bytes=64)
 
         def product_bank(pair):
-            return product_banks[pair % 2].tile([P, BANK], F32, name="product")
-
-        def step(u, at):
-            return AT["step"] + u * STEP + at
+            return product_banks[pair].tile([P, BANK], F32, name="product")
 
         def group(u):
             return u * ROWS // R
@@ -65,7 +60,7 @@ def tile_attend_gsl2_x_ts_kernel(tc, xT, wT, y, wt, ts, offs, out):
         zero = keep.tile([P, 1], F32, name="zero")
         nc.vector.memset(zero[:], 0.0)
         nc.sync.dma_start(offsets[:], offs)
-        ts_table = placed([P, T], F32, "ts_table", AT["ts"])
+        ts_table = placed([P, T], F32, "ts")
         nc.scalar.dma_start(ts_table[P - 1 :, :], ts[0:1, :])
         wt_rows = keep.tile([P, P], F32, name="wt_rows")
         nc.scalar.dma_start(wt_rows[P - ROW_TILES :, :], wt.rearrange("b (j n) o -> (b j) (n o)", n=P))
@@ -73,29 +68,36 @@ def tile_attend_gsl2_x_ts_kernel(tc, xT, wT, y, wt, ts, offs, out):
         nc.vector.memset(wt_rows[: P - ROW_TILES, :], 0.0)
         planes = []
         for t in range(PACK):
-            plane = placed([P, T], F32, f"plane{t}", AT["planes"] + 4 * T * t)
+            plane = placed([P, T], F32, f"plane{t}")
             nc.sync.dma_start(plane[:], wT.rearrange("(p t) c -> p t c", t=PACK)[:, t, :])
             planes.append(plane)
         x_raw, y_raw = {}, {}
 
         def load_x(u):
-            x_raw[u] = placed([P, PACK, ROWS], F32, f"x_raw{u}", AT.get(f"x{u}"))
+            x_raw[u] = placed([P, PACK, ROWS], F32, f"x{u}")
             nc.sync.dma_start(x_raw[u][:], xT[group(u)].rearrange("(p t) r -> p t r", t=PACK)[:, :, rows_of(u)])
 
-        for u in range(UNITS):
-            for k in X_LOADS[u]:
-                load_x(k)
-            y_raw[u] = placed([P, TILES, N], F32, f"y_raw{u}", step(1, 5 * K) if u == 0 else None)
+        def load_y(u):
+            y_raw[u] = placed([P, TILES, N], F32, f"y{u}")
             nc.sync.dma_start(y_raw[u][:], y[group(u), rows_of(u), :].rearrange("(j n) i -> n j i", n=P))
+
+        load_x(0)
+        load_x(1)
+        load_x(2)
+        load_y(0)
+        load_x(3)
+        load_y(1)
+        load_y(2)
+        load_y(3)
 
         ident = keep.tile([P, P], F32, name="ident")
         make_identity(nc, ident[:])
         half = keep.tile([P, 1], F32, name="half")
         nc.scalar.activation(half[:], zero[:], ACT.Sigmoid)
 
-        def quantise(src, cols, fmt, name, at=None):
+        def quantise(src, cols, fmt, name):
             codes = placed([P, cols], U32, name + "_codes")
-            scales = placed([P, cols], U8, name + "_scales", at)
+            scales = placed([P, cols], U8, name + "_scales")
             nc.vector.quantize_mx(out=codes[:].bitcast(fmt), scales=scales[:], in_=src)
             return codes, scales
 
@@ -110,8 +112,8 @@ def tile_attend_gsl2_x_ts_kernel(tc, xT, wT, y, wt, ts, offs, out):
                 b, t = divmod(k, PACK)
                 nc.tensor.transpose(bank[:, 2 * k : 2 * k + P], ts_picked[b][:, t::PACK], ident[:])
             tiles = []
-            for place, (name, scale) in enumerate((("ts", 1.0), ("wt", 1.0), ("ts", -0.25), ("wt", -1.0))):
-                tile = placed([P, ROW_TILES], F32, f"columns{place}", AT["x0"] + 64 * place)
+            for place, (name, scale) in enumerate((("ts", 1.0), ("wt", 1.0), ("wt", -1.0), ("ts", -0.25))):
+                tile = placed([P, ROW_TILES], F32, f"columns{place}")
                 turned = bank[:, P - 1 : P - 1 + 2 * B * PACK : 2] if name == "ts" else bank[:, BANK - ROW_TILES :]
                 nc.scalar.activation(tile[:], turned, ACT.Copy, scale=scale)
                 tiles.append(tile)
@@ -120,21 +122,19 @@ def tile_attend_gsl2_x_ts_kernel(tc, xT, wT, y, wt, ts, offs, out):
         picked = placed([P, PACK * B * N], BF16, "picked")
         by_slot, w_slot_mx, w_feature_mx, x_woven, x_mx = {}, {}, {}, {}, {}
 
-        def gather(t):
-            first = t * B * N
-            cut = VECTOR_SHARE[t]
-            nc.vector.tensor_copy(picked[:, first : first + cut], planes[t][:].indirect(offsets[:, : cut // 16]))
-            for lo, hi in ((cut, N), (max(cut, N), B * N)):
-                if lo < hi:
-                    nc.scalar.activation(
-                        picked[:, first + lo : first + hi], planes[t][:].indirect(offsets[:, lo // 16 : hi // 16]), ACT.Copy
-                    )
+        def gather(t, lo, hi, on_vector):
+            dst = picked[:, t * B * N + lo : t * B * N + hi]
+            src = planes[t][:].indirect(offsets[:, lo // 16 : hi // 16])
+            if on_vector:
+                nc.vector.tensor_copy(dst, src)
+            else:
+                nc.scalar.activation(dst, src, ACT.Copy)
 
-        def turn_plane(t):
+        def turn_plane(t, new_bank, copy):
             a, e = divmod(t, 2)
             if e == 0:
-                by_slot[a] = placed([P, B * 2 * P * PACK], BF16, f"by_slot{a}", AT["x3"] if a else AT["planes"] + 4 * T)
-            bank = product_bank(1)
+                by_slot[a] = placed([P, B * 2 * P * PACK], BF16, f"bs{a}")
+            bank = new_bank()
             words = picked[:].bitcast(F32)
             for b in range(B):
                 first = (t * B + b) * N // 2
@@ -143,36 +143,43 @@ def tile_attend_gsl2_x_ts_kernel(tc, xT, wT, y, wt, ts, offs, out):
                     nc.tensor.transpose(
                         bank[:, quarter * P : (quarter + 1) * P], words[:, first + v : first + N // 2 : 2], ident[:]
                     )
-            nc.scalar.copy(
+            copy(
                 by_slot[a][:].bitcast(F32).rearrange("s (b e p v) -> s b e p v", b=B, e=2, v=2)[:, :, e, :, :],
                 bank[:].rearrange("s (b v p) -> s b p v", b=B, v=2),
             )
 
         def quantise_by_slot(a):
-            w_slot_mx[a] = quantise(by_slot[a][:], D, E4M3, f"w_slot{a}", step(2, 4 * K) if a else AT["square"])
+            w_slot_mx[a] = quantise(by_slot[a][:], D, E4M3, f"ws{a}")
 
-        def quantise_by_feature(b, pieces):
-            by_feature = placed([P, N * PACK], BF16, f"by_feature{b}", AT["woven0"] - SLOT if b else None)
-            woven = by_feature[:].rearrange("p (r q e t) -> p q r e t", r=PACK, e=2, t=PACK)
+        by_feature = {}
+
+        def weave_w(b, a):
+            if a == 0:
+                by_feature[b] = placed([P, N * PACK], BF16, f"bf{b}")
+            woven = by_feature[b][:].rearrange("p (r q e t) -> p q r e t", r=PACK, e=2, t=PACK)
             planar = picked[:].rearrange("p (t b q e r) -> p b q r e t", t=PACK, b=B, e=2, r=PACK)[:, b]
+            nc.vector.tensor_copy(woven[:, :, 2 * a : 2 * a + 2], planar[:, :, 2 * a : 2 * a + 2])
+
+        def quantise_w(b, pieces):
             tiles = PACK // pieces
             for a in range(pieces):
-                nc.vector.tensor_copy(woven[:, :, a * tiles : (a + 1) * tiles], planar[:, :, a * tiles : (a + 1) * tiles])
-            for a in range(pieces):
-                part = by_feature[:, a * tiles * P * PACK : (a + 1) * tiles * P * PACK]
-                codes, scales = quantise(part, tiles * P, E4M3, f"w_feature{b}{a}")
+                part = by_feature[b][:, a * tiles * P * PACK : (a + 1) * tiles * P * PACK]
+                codes, scales = quantise(part, tiles * P, E4M3, f"wq{b}{a}")
                 for r in range(tiles):
                     w_feature_mx[b, a * tiles + r] = codes[:, r * P : (r + 1) * P], scales[:, r * P : (r + 1) * P]
 
-        def weave_x(u, at=None):
-            x_woven[u] = placed([P, ROWS * PACK], BF16, f"x_woven{u}", at)
-            (nc.vector.tensor_copy if u == 2 else nc.scalar.copy)(
+        def weave_x(u, copy):
+            x_woven[u] = placed([P, ROWS * PACK], BF16, f"xw{u}")
+            copy(
                 x_woven[u][:].rearrange("p (q n t) -> p q t n", n=LINE, t=PACK),
                 x_raw[u][:].rearrange("p t (q n) -> p q t n", n=LINE),
             )
 
+        def copy_on_gpsimd(dst, src):
+            nc.gpsimd.tensor_scalar(dst, src, 1.0, 0.0, ALU.mult, ALU.add)
+
         def quantise_x(u):
-            x_mx[u] = quantise(x_woven[u][:], ROWS, E4M3, f"x{u}", step(1, 4 * K) if u + 1 == UNITS else None)
+            x_mx[u] = quantise(x_woven[u][:], ROWS, E4M3, f"xq{u}")
 
         probs, squares, slopes, targets, misses, hs, h_mx = {}, {}, {}, {}, {}, {}, {}
 
@@ -180,11 +187,10 @@ def tile_attend_gsl2_x_ts_kernel(tc, xT, wT, y, wt, ts, offs, out):
             k = group(u) * PACK + t
             return cols[:, k : k + 1]
 
-        def sigmoids(u):
+        def scores(u):
             x_codes, x_scales = x_mx[u]
-            probs[u] = placed([P, PACK, ROWS], F32, f"prob{u}", None)
             for a in range(2):
-                bank = product_bank(0)
+                bank = scored[u, a] = product_bank(0)
                 for e in range(2):
                     w_codes, w_scales = w_feature_mx[group(u), 2 * a + e]
                     nc.tensor.matmul_mx(
@@ -196,31 +202,33 @@ def tile_attend_gsl2_x_ts_kernel(tc, xT, wT, y, wt, ts, offs, out):
                         start=True,
                         stop=True,
                     )
+
+        def sigmoids(u):
+            probs[u] = placed([P, PACK, ROWS], F32, f"p{u}")
+            for a in range(2):
+                bank = scored[u, a]
                 for e in range(2):
                     t = 2 * a + e
                     nc.scalar.activation(probs[u][:, t, :], bank[:, e * ROWS : (e + 1) * ROWS], ACT.Sigmoid, scale=scale_of(u, t, ts_cols))
 
         def square(u):
             for a in range(2):
-                at = AT["square"] + 2 * K * u if a == 0 else (None if u else step(2, 5 * K))
-                squares[u, a] = placed([P, 2, ROWS], F32, f"square{u}{a}", at)
+                squares[u, a] = placed([P, 2, ROWS], F32, f"sq{u}{a}")
                 nc.scalar.activation(squares[u, a][:], probs[u][:, 2 * a : 2 * a + 2, :], ACT.Square, bias=half[:], scale=-1.0)
 
-        def slope(u):
-            on_vector = u + 1 < UNITS
-            slopes[u] = placed([P, PACK * ROWS], F32, f"slope{u}", step(u, 0) if on_vector else None)
+        def slope(u, engine):
+            slopes[u] = placed([P, PACK * ROWS], F32, f"sl{u}")
             for t in range(PACK):
                 dst = slopes[u][:].rearrange("p (c t i) -> p c t i", t=PACK, i=LINE)[:, :, t, :]
                 src = squares[u, t // 2][:, t % 2, :].rearrange("p (c i) -> p c i", i=LINE)
-                if on_vector:
-                    nc.vector.tensor_scalar(dst, src, -0.25, scale_of(u, t, ts_cols), ALU.add, ALU.mult)
+                if engine is not None:
+                    engine.tensor_scalar(dst, src, -0.25, scale_of(u, t, ts_cols), ALU.add, ALU.mult)
                 else:
                     nc.scalar.activation(dst, src, ACT.Identity, bias=scale_of(u, t, ts_quarter), scale=scale_of(u, t, ts_cols))
 
         def weigh_targets(k, engine):
             u, j = divmod(k, TILES)
-            at = step(u, 4 * K - 64) if j == 0 else (step(u + 1, 6 * K) if u else None)
-            targets[k] = placed([P, N], F32, f"target{k}", at)
+            targets[k] = placed([P, N], F32, f"tg{k}")
             engine.tensor_scalar(
                 targets[k][:].rearrange("p (t q i) -> p q t i", t=PACK, i=LINE),
                 y_raw[u][:, j, :].rearrange("p (q i t) -> p q t i", t=PACK, i=LINE),
@@ -230,11 +238,14 @@ def tile_attend_gsl2_x_ts_kernel(tc, xT, wT, y, wt, ts, offs, out):
                 ALU.add,
             )
 
-        def miss(k):
+        def turn_probs(k, new_bank):
             u, j = divmod(k, TILES)
-            turned = prob_banks.tile([P, BANK], F32, name="turned_prob")
+            turned = turned_probs[k] = new_bank()
             for t in reversed(range(PACK)):
                 nc.tensor.transpose(turned[:, t * P : (t + 1) * P], probs[u][:, t, j * P : (j + 1) * P], ident[:])
+
+        def miss(k):
+            turned = turned_probs[k]
             weighted = work.tile([P, N], F32, name="weighted")
             nc.vector.scalar_tensor_tensor(weighted[:], turned[:], wt_minus[:, k : k + 1], targets[k][:], ALU.mult, ALU.add)
             misses[k] = miss_banks.tile([P, BANK], F32, name="turned_miss")
@@ -244,7 +255,7 @@ def tile_attend_gsl2_x_ts_kernel(tc, xT, wT, y, wt, ts, offs, out):
         def gradient(k):
             u, j = divmod(k, TILES)
             if j == 0:
-                hs[u] = placed([P, ROWS * PACK], BF16, f"h{u}", step(u + 3, 5 * K) if u + 2 < UNITS else None)
+                hs[u] = placed([P, ROWS * PACK], BF16, f"h{u}")
             nc.vector.tensor_tensor(
                 hs[u][:, j * BANK : (j + 1) * BANK].rearrange("p (c i t) -> p c t i", t=PACK, i=LINE),
                 misses[k][:].rearrange("p (t c i) -> p c t i", t=PACK, i=LINE),
@@ -254,91 +265,71 @@ def tile_attend_gsl2_x_ts_kernel(tc, xT, wT, y, wt, ts, offs, out):
 
         def quantise_h(first, tiles):
             u, j = divmod(first, TILES)
-            at = [AT["square"] + 2 * K, AT["square"] + 4 * K, step(3, 4 * K), None][u]
-            codes, scales = quantise(hs[u][:, j * BANK : (j + tiles) * BANK], tiles * P, E5M2, f"h{first}", at)
+            codes, scales = quantise(hs[u][:, j * BANK : (j + tiles) * BANK], tiles * P, E5M2, f"hq{first}")
             for k in range(tiles):
                 h_mx[first + k] = codes[:, k * P : (k + 1) * P], scales[:, k * P : (k + 1) * P]
 
-        def finish(k, copy):
-            u, j = divmod(k, TILES)
+        def multiply(k, out_cols, a, cols):
             h_codes, h_scales = h_mx[k]
-            bank = result_banks[u]()
-            for a in reversed(range(2)):
-                w_codes, w_scales = w_slot_mx[a]
-                cols = slice(group(u) * D // 2, (group(u) + 1) * D // 2)
-                nc.tensor.matmul_mx(
-                    out=bank[:, a * D // 2 : (a + 1) * D // 2],
-                    lhsT=h_codes.bitcast(E5M2),
-                    lhsT_scale=h_scales,
-                    rhs=w_codes[:, cols].bitcast(E4M3),
-                    rhs_scale=w_scales[:, cols],
-                    start=True,
-                    stop=True,
-                )
+            w_codes, w_scales = w_slot_mx[a]
+            nc.tensor.matmul_mx(
+                out=out_cols,
+                lhsT=h_codes.bitcast(E5M2),
+                lhsT_scale=h_scales,
+                rhs=w_codes[:, cols].bitcast(E4M3),
+                rhs_scale=w_scales[:, cols],
+                start=True,
+                stop=True,
+            )
+
+        def result(k, new_bank):
+            u = k // TILES
+            bank = results[k] = new_bank()
+            for a in range(2):
+                multiply(k, bank[:, a * D // 2 : (a + 1) * D // 2], a, slice(group(u) * D // 2, (group(u) + 1) * D // 2))
+
+        def store(k, copy):
+            u, j = divmod(k, TILES)
+            bank = results[k]
             if j == 0:
-                staged[u] = placed([P, TILES, D], F32, f"staged{u}", AT["planes"] + u * SLOT)
-            copy(staged[u][:, j, :].rearrange("n (p t) -> n p t", t=PACK), bank[:].rearrange("n (t p) -> n p t", t=PACK))
+                staged[u] = placed([P, TILES, D], F32, f"st{u}")
+            copy(
+                staged[u][:, j, :].rearrange("n (p t) -> n p t", t=PACK),
+                bank[:].rearrange("n (t p) -> n p t", t=PACK),
+            )
             first = rows_of(u).start + j * P
             nc.sync.dma_start(out[group(u), first : first + P, :], staged[u][:, j, :])
 
-        staged = {}
-        result_banks = [
-            lambda: product_bank(1),
-            lambda: product_bank(0),
-            lambda: prob_banks.tile([P, BANK], F32, name="turned_prob"),
-            lambda: miss_banks.tile([P, BANK], F32, name="turned_miss"),
-        ]
+        staged, results, turned_probs, scored = {}, {}, {}, {}
+        spare = lambda: product_bank(1)
+        score = lambda: product_bank(0)
+        prob = lambda: prob_banks.tile([P, BANK], F32, name="turned_prob")
+        missb = lambda: miss_banks.tile([P, BANK], F32, name="turned_miss")
+        V, S, G = nc.vector, nc.scalar, nc.gpsimd
 
-        for t in range(PACK):
-            gather(t)
-            if t < 2:
-                turn_plane(t)
-        weave_x(0, AT["woven0"] - SLOT // 4)
-        ts_cols, wt_cols, ts_quarter, wt_minus = columns()
-        quantise_by_feature(0, 2)
-        quantise_x(0)
-        weave_x(1)
-        sigmoids(0)
-        square(0)
-        quantise_x(1)
-        quantise_by_feature(1, 1)
-        weave_x(2)
-        for k in range(TILES):
-            weigh_targets(k, nc.vector)
-        quantise_x(2)
-        weigh_targets(TILES, nc.gpsimd)
-        miss(0)
-        miss(1)
-        sigmoids(1)
-        weave_x(3)
-        for u in range(UNITS):
-            first = u * TILES
-            if u == 1:
-                quantise_x(3)
-            if u == 2:
-                quantise_by_slot(1)
-            if u + 1 < UNITS:
-                slope(u)
-            if u:
-                quantise_h(first - TILES, TILES)
-            else:
-                quantise_by_slot(0)
-            for k in range(first + TILES + 1, min(first + 2 * TILES + 1, ROW_TILES)):
-                weigh_targets(k, nc.gpsimd)
-            gradient(first)
-            gradient(first + 1)
-            if u + 1 < UNITS:
-                square(u + 1)
-                if u + 2 == UNITS:
-                    slope(u + 1)
-                miss(first + TILES)
-                miss(first + TILES + 1)
-            if u + 2 < UNITS:
-                sigmoids(u + 2)
-            if u == 0:
-                turn_plane(2)
-                turn_plane(3)
-        quantise_h(ROW_TILES - 2, 1)
-        quantise_h(ROW_TILES - 1, 1)
-        for k in range(ROW_TILES):
-            finish(k, nc.vector.tensor_copy if k in (7,) else nc.scalar.copy)
+        ts_cols, wt_cols, wt_minus, ts_quarter = columns()
+        gather(0, 0, VECTOR_SHARE[0], True); gather(0, VECTOR_SHARE[0], B * N, False); turn_plane(0, spare, S.copy)
+        gather(1, 0, VECTOR_SHARE[1], True); gather(1, VECTOR_SHARE[1], B * N, False); turn_plane(1, spare, S.copy)
+        gather(2, 0, VECTOR_SHARE[2], True); gather(2, VECTOR_SHARE[2], B * N, False)
+        gather(3, 0, LAST_SHARE[0], True); gather(3, LAST_SHARE[0], N, False); gather(3, N, N + LAST_SHARE[1], True); gather(3, N + LAST_SHARE[1], B * N, False)
+        weave_w(0, 0); weave_w(0, 1); quantise_w(0, 2)
+        weave_x(0, S.copy); quantise_x(0)
+        weave_x(1, S.copy); scores(0); sigmoids(0); square(0)
+        weave_w(1, 0); weave_w(1, 1); quantise_x(1); quantise_w(1, 1); weave_x(2, V.tensor_copy); weigh_targets(0, V); weigh_targets(1, V); quantise_x(2)
+        weigh_targets(2, G)
+        turn_probs(0, prob); miss(0); turn_probs(1, prob); miss(1); scores(1); sigmoids(1); weave_x(3, S.copy)
+        slope(0, V); quantise_by_slot(0)
+        weigh_targets(3, G); weigh_targets(4, G)
+        gradient(0); gradient(1); square(1); turn_probs(2, prob); miss(2); turn_probs(3, prob); miss(3); scores(2); sigmoids(2); turn_plane(2, spare, S.copy); turn_plane(3, spare, S.copy)
+        quantise_x(3); slope(1, V); quantise_h(0, 2)
+        weigh_targets(5, G); weigh_targets(6, G)
+        gradient(2); gradient(3); square(2); turn_probs(4, prob); miss(4); turn_probs(5, prob); miss(5); scores(3); sigmoids(3)
+        quantise_by_slot(1); slope(2, V); quantise_h(2, 2)
+        weigh_targets(7, G)
+        gradient(4); square(3); slope(3, None); turn_probs(6, prob); miss(6); gradient(5); turn_probs(7, prob); miss(7)
+        quantise_h(4, 2)
+        gradient(6); gradient(7); quantise_h(6, 1); quantise_h(7, 1)
+        result(0, spare); result(1, spare); store(0, S.copy); store(1, S.copy)
+        result(2, score); result(3, score); store(2, S.copy); store(3, S.copy)
+        result(4, prob); result(5, prob); store(4, S.copy); store(5, S.copy)
+        result(6, missb); store(6, S.copy); result(7, missb); store(7, V.tensor_copy)

@@ -85,8 +85,8 @@ def tile_attend_gsl2_x_ts_kernel(tc, xT, wT, y, wt, ts, offs, out):
         load_x(1)
         load_x(2)
         load_y(0)
-        load_x(3)
         load_y(1)
+        load_x(3)
         load_y(2)
         load_y(3)
 

@@ -28,7 +28,7 @@ LINE = 4
 COLS = N // 16
 VECTOR_SHARE = (576, 576, 640)
 LAST_SHARE = (288, 128)
-AT = {"plane0":0,"plane1":8256,"plane2":16512,"plane3":24768,"ts":33024,"y0":41280,"tg2":45312,"sl1":47296,"sl0":51456,"tg0":55488,"tg3":57600,"sq01":59584,"tg4":61568,"sl2":63552,"sq00":67712,"sq10":69824,"sq20":71936,"tg5":74048,"h0":76032,"tg6":78016,"h1":80128,"tg7":82112,"x3":84224,"x0":88384,"bf1":92416,"h3":96576,"bs1":84224,"bs0":8256,"ws0_scales":67712,"ws1_scales":62080,"st0":33024,"st1":37120,"st2":12352,"st3":4096,"columns0":0,"columns1":64,"columns2":128,"columns3":192,"xq3_scales":45824,"hq0_scales":69824,"hq2_scales":71936,"hq4_scales":78528}
+AT = {"plane0":0,"plane1":8256,"plane2":16512,"plane3":24768,"ts":33024,"y0":41280,"tg2":45312,"sl1":47296,"sl0":51456,"tg0":55488,"tg3":57600,"sq01":59584,"tg4":61568,"sl2":63552,"sq00":67712,"sq10":69824,"sq20":71936,"tg5":74048,"h0":76032,"tg6":78016,"h1":80128,"tg7":82112,"x3":84224,"x0":88384,"bf1":92416,"h3":96576,"bs1":84224,"bs0":8256,"ws0_scales":67712,"ws1_scales":62080,"st0":33024,"st1":37120,"st2":12352,"st3":4096,"columns0":89408,"columns1":89472,"columns2":89536,"columns3":89600,"xq3_scales":45824,"hq0_scales":69824,"hq2_scales":71936,"hq4_scales":78528,"minus_rows":12352}
 
 
 def tile_attend_gsl2_x_ts_kernel(tc, xT, wT, y, wt, ts, offs, out):
@@ -107,12 +107,14 @@ def tile_attend_gsl2_x_ts_kernel(tc, xT, wT, y, wt, ts, offs, out):
 
         def columns():
             bank = prob_banks.tile([P, BANK], F32, name="turned_prob")
-            nc.tensor.transpose(bank[:, BANK - P :], wt_rows[:], ident[:])
+            minus_rows = placed([P, P], F32, "minus_rows")
+            nc.scalar.activation(minus_rows[:], wt_rows[:], ACT.Copy, scale=-1.0)
+            nc.tensor.transpose(bank[:, BANK - P :], minus_rows[:], ident[:])
             for k in reversed(range(B * PACK)):
                 b, t = divmod(k, PACK)
                 nc.tensor.transpose(bank[:, 2 * k : 2 * k + P], ts_picked[b][:, t::PACK], ident[:])
             tiles = []
-            for place, (name, scale) in enumerate((("ts", 1.0), ("wt", 1.0), ("wt", -1.0), ("ts", -0.25))):
+            for place, (name, scale) in enumerate((("ts", 1.0), ("wt", -1.0), ("wt", 1.0), ("ts", -0.25))):
                 tile = placed([P, ROW_TILES], F32, f"columns{place}")
                 turned = bank[:, P - 1 : P - 1 + 2 * B * PACK : 2] if name == "ts" else bank[:, BANK - ROW_TILES :]
                 nc.scalar.activation(tile[:], turned, ACT.Copy, scale=scale)
@@ -307,13 +309,12 @@ def tile_attend_gsl2_x_ts_kernel(tc, xT, wT, y, wt, ts, offs, out):
         missb = lambda: miss_banks.tile([P, BANK], F32, name="turned_miss")
         V, S, G = nc.vector, nc.scalar, nc.gpsimd
 
-        ts_cols, wt_cols, wt_minus, ts_quarter = columns()
         gather(0, 0, VECTOR_SHARE[0], True); gather(0, VECTOR_SHARE[0], B * N, False); turn_plane(0, spare, S.copy)
         gather(1, 0, VECTOR_SHARE[1], True); gather(1, VECTOR_SHARE[1], B * N, False); turn_plane(1, spare, S.copy)
         gather(2, 0, VECTOR_SHARE[2], True); gather(2, VECTOR_SHARE[2], B * N, False)
         gather(3, 0, LAST_SHARE[0], True); gather(3, LAST_SHARE[0], N, False); gather(3, N, N + LAST_SHARE[1], True); gather(3, N + LAST_SHARE[1], B * N, False)
         weave_w(0, 0); weave_w(0, 1); quantise_w(0, 2)
-        weave_x(0, S.copy); quantise_x(0)
+        weave_x(0, S.copy); ts_cols, wt_cols, wt_minus, ts_quarter = columns(); quantise_x(0)
         weave_x(1, S.copy); scores(0); sigmoids(0); square(0)
         weave_w(1, 0); weave_w(1, 1); quantise_x(1); quantise_w(1, 1); weave_x(2, V.tensor_copy); weigh_targets(0, V); weigh_targets(1, V); quantise_x(2)
         weigh_targets(2, G)

from contextlib import ExitStack

import concourse.mybir as mybir
from concourse.masks import make_identity

B, N, T, D, R = 2, 512, 2048, 512, 512
FLOPS = 2 * 2 * B * R * N * D
BYTES = 4 * (B * D * R + D * T + B * R * N + B * R + T + B * R * D) + 2 * 128 * B * N // 16

F32 = mybir.dt.float32
BF16 = mybir.dt.bfloat16
U32 = mybir.dt.uint32
U16 = mybir.dt.uint16
U8 = mybir.dt.uint8
E4M3 = mybir.dt.float8_e4m3fn_x4
E5M2 = mybir.dt.float8_e5m2_x4
ACT = mybir.ActivationFunctionType
ALU = mybir.AluOpType

P = 128
PACK = 4
BANK = 512
ROWS = 256
TILES = ROWS // P
UNITS = B * R // ROWS
ROW_TILES = B * R // P
LINE = 4
COLS = N // 16
VECTOR_SHARE = (576, 576, 640)
LAST_SHARE = (288, 128)
AT = {"plane0":0,"plane1":8256,"plane2":16512,"plane3":24768,"ts":33024,"y0":41280,"tg2":45312,"sl1":47296,"sl0":51456,"tg0":55488,"tg3":57600,"sq01":59584,"tg4":61568,"sl2":63552,"sq00":67712,"sq10":69824,"sq20":71936,"tg5":74048,"h0":76032,"tg6":78016,"h1":80128,"tg7":82112,"x3":84224,"x0":88384,"bf1":92416,"h3":96576,"bs1":84224,"bs0":8256,"ws0_scales":67712,"ws1_scales":62080,"st0":33024,"st1":37120,"st2":12352,"st3":4096,"columns0":89408,"columns1":89472,"columns2":89536,"columns3":89600,"xq3_scales":45824,"hq0_scales":69824,"hq2_scales":71936,"hq4_scales":78528,"minus_rows":12352}


def tile_attend_gsl2_x_ts_kernel(tc, xT, wT, y, wt, ts, offs, out):
    nc = tc.nc
    with ExitStack() as ctx:
        keep = ctx.enter_context(tc.tile_pool(name="keep", bufs=1))
        shared = ctx.enter_context(tc.tile_pool(name="shared", bufs=1))
        work = ctx.enter_context(tc.tile_pool(name="work", bufs=2))
        product_banks = [ctx.enter_context(tc.psum_pool(name=f"product_banks{k}", bufs=2)) for k in range(2)]
        prob_banks = ctx.enter_context(tc.psum_pool(name="prob_banks", bufs=2))
        miss_banks = ctx.enter_context(tc.psum_pool(name="miss_banks", bufs=2))

        def placed(shape, dtype, name):
            at = AT.get(name)
            if at is None:
                return keep.tile(shape, dtype, name=name, align_bytes=64)
            return shared.tile(shape, dtype, name=name, offset=at, align_bytes=64)

        def product_bank(pair):
            return product_banks[pair].tile([P, BANK], F32, name="product")

        def group(u):
            return u * ROWS // R

        def rows_of(u):
            return slice(u * ROWS % R, u * ROWS % R + ROWS)

        offsets = keep.tile([P, B * COLS], U16, name="offsets")
        zero = keep.tile([P, 1], F32, name="zero")
        nc.vector.memset(zero[:], 0.0)
        nc.sync.dma_start(offsets[:], offs)
        ts_table = placed([P, T], F32, "ts")
        nc.scalar.dma_start(ts_table[P - 1 :, :], ts[0:1, :])
        wt_rows = keep.tile([P, P], F32, name="wt_rows")
        nc.scalar.dma_start(wt_rows[P - ROW_TILES :, :], wt.rearrange("b (j n) o -> (b j) (n o)", n=P))
        nc.vector.memset(ts_table[: P - 1, :], 0.0)
        nc.vector.memset(wt_rows[: P - ROW_TILES, :], 0.0)
        planes = []
        for t in range(PACK):
            plane = placed([P, T], F32, f"plane{t}")
            nc.sync.dma_start(plane[:], wT.rearrange("(p t) c -> p t c", t=PACK)[:, t, :])
            planes.append(plane)
        x_raw, y_raw = {}, {}

        def load_x(u):
            x_raw[u] = placed([P, PACK, ROWS], F32, f"x{u}")
            nc.sync.dma_start(x_raw[u][:], xT[group(u)].rearrange("(p t) r -> p t r", t=PACK)[:, :, rows_of(u)])

        def load_y(u):
            y_raw[u] = placed([P, TILES, N], F32, f"y{u}")
            nc.sync.dma_start(y_raw[u][:], y[group(u), rows_of(u), :].rearrange("(j n) i -> n j i", n=P))

        load_x(0)
        load_x(1)
        load_x(2)
        load_y(0)
        load_y(1)
        load_x(3)
        load_y(2)
        load_y(3)

        ident = keep.tile([P, P], F32, name="ident")
        make_identity(nc, ident[:])
        half = keep.tile([P, 1], F32, name="half")
        nc.scalar.activation(half[:], zero[:], ACT.Sigmoid)

        def quantise(src, cols, fmt, name):
            codes = placed([P, cols], U32, name + "_codes")
            scales = placed([P, cols], U8, name + "_scales")
            nc.vector.quantize_mx(out=codes[:].bitcast(fmt), scales=scales[:], in_=src)
            return codes, scales

        ts_picked = [keep.tile([P, N], F32, name=f"ts_picked{b}") for b in range(B)]
        nc.vector.tensor_copy(ts_picked[0][:], ts_table[:].indirect(offsets[:, :COLS]))
        nc.scalar.activation(ts_picked[1][:], ts_table[:].indirect(offsets[:, COLS:]), ACT.Copy)

        def columns():
            bank = prob_banks.tile([P, BANK], F32, name="turned_prob")
            minus_rows = placed([P, P], F32, "minus_rows")
            nc.scalar.activation(minus_rows[:], wt_rows[:], ACT.Copy, scale=-1.0)
            nc.tensor.transpose(bank[:, BANK - P :], minus_rows[:], ident[:])
            for k in reversed(range(B * PACK)):
                b, t = divmod(k, PACK)
                nc.tensor.transpose(bank[:, 2 * k : 2 * k + P], ts_picked[b][:, t::PACK], ident[:])
            tiles = []
            for place, (name, scale) in enumerate((("ts", 1.0), ("wt", -1.0), ("wt", 1.0), ("ts", -0.25))):
                tile = placed([P, ROW_TILES], F32, f"columns{place}")
                turned = bank[:, P - 1 : P - 1 + 2 * B * PACK : 2] if name == "ts" else bank[:, BANK - ROW_TILES :]
                nc.scalar.activation(tile[:], turned, ACT.Copy, scale=scale)
                tiles.append(tile)
            return tiles

        picked = placed([P, PACK * B * N], BF16, "picked")
        by_slot, w_slot_mx, w_feature_mx, x_woven, x_mx = {}, {}, {}, {}, {}

        def gather(t, lo, hi, on_vector):
            dst = picked[:, t * B * N + lo : t * B * N + hi]
            src = planes[t][:].indirect(offsets[:, lo // 16 : hi // 16])
            if on_vector:
                nc.vector.tensor_copy(dst, src)
            else:
                nc.scalar.activation(dst, src, ACT.Copy)

        def turn_plane(t, new_bank, copy):
            a, e = divmod(t, 2)
            if e == 0:
                by_slot[a] = placed([P, B * 2 * P * PACK], BF16, f"bs{a}")
            bank = new_bank()
            words = picked[:].bitcast(F32)
            for b in range(B):
                first = (t * B + b) * N // 2
                for v in range(2):
                    quarter = 2 * b + v
                    nc.tensor.transpose(
                        bank[:, quarter * P : (quarter + 1) * P], words[:, first + v : first + N // 2 : 2], ident[:]
                    )
            copy(
                by_slot[a][:].bitcast(F32).rearrange("s (b e p v) -> s b e p v", b=B, e=2, v=2)[:, :, e, :, :],
                bank[:].rearrange("s (b v p) -> s b p v", b=B, v=2),
            )

        def quantise_by_slot(a):
            w_slot_mx[a] = quantise(by_slot[a][:], D, E4M3, f"ws{a}")

        by_feature = {}

        def weave_w(b, a):
            if a == 0:
                by_feature[b] = placed([P, N * PACK], BF16, f"bf{b}")
            woven = by_feature[b][:].rearrange("p (r q e t) -> p q r e t", r=PACK, e=2, t=PACK)
            planar = picked[:].rearrange("p (t b q e r) -> p b q r e t", t=PACK, b=B, e=2, r=PACK)[:, b]
            nc.vector.tensor_copy(woven[:, :, 2 * a : 2 * a + 2], planar[:, :, 2 * a : 2 * a + 2])

        def quantise_w(b, pieces):
            tiles = PACK // pieces
            for a in range(pieces):
                part = by_feature[b][:, a * tiles * P * PACK : (a + 1) * tiles * P * PACK]
                codes, scales = quantise(part, tiles * P, E4M3, f"wq{b}{a}")
                for r in range(tiles):
                    w_feature_mx[b, a * tiles + r] = codes[:, r * P : (r + 1) * P], scales[:, r * P : (r + 1) * P]

        def weave_x(u, copy):
            x_woven[u] = placed([P, ROWS * PACK], BF16, f"xw{u}")
            copy(
                x_woven[u][:].rearrange("p (q n t) -> p q t n", n=LINE, t=PACK),
                x_raw[u][:].rearrange("p t (q n) -> p q t n", n=LINE),
            )

        def copy_on_gpsimd(dst, src):
            nc.gpsimd.tensor_scalar(dst, src, 1.0, 0.0, ALU.mult, ALU.add)

        def quantise_x(u):
            x_mx[u] = quantise(x_woven[u][:], ROWS, E4M3, f"xq{u}")

        probs, squares, slopes, targets, misses, hs, h_mx = {}, {}, {}, {}, {}, {}, {}

        def scale_of(u, t, cols):
            k = group(u) * PACK + t
            return cols[:, k : k + 1]

        def scores(u):
            x_codes, x_scales = x_mx[u]
            for a in range(2):
                bank = scored[u, a] = product_bank(0)
                for e in range(2):
                    w_codes, w_scales = w_feature_mx[group(u), 2 * a + e]
                    nc.tensor.matmul_mx(
                        out=bank[:, e * ROWS : (e + 1) * ROWS],
                        lhsT=w_codes.bitcast(E4M3),
                        lhsT_scale=w_scales,
                        rhs=x_codes[:].bitcast(E4M3),
                        rhs_scale=x_scales[:],
                        start=True,
                        stop=True,
                    )

        def sigmoids(u):
            probs[u] = placed([P, PACK, ROWS], F32, f"p{u}")
            for a in range(2):
                bank = scored[u, a]
                for e in range(2):
                    t = 2 * a + e
                    nc.scalar.activation(probs[u][:, t, :], bank[:, e * ROWS : (e + 1) * ROWS], ACT.Sigmoid, scale=scale_of(u, t, ts_cols))

        def square(u):
            for a in range(2):
                squares[u, a] = placed([P, 2, ROWS], F32, f"sq{u}{a}")
                nc.scalar.activation(squares[u, a][:], probs[u][:, 2 * a : 2 * a + 2, :], ACT.Square, bias=half[:], scale=-1.0)

        def slope(u, engine):
            slopes[u] = placed([P, PACK * ROWS], F32, f"sl{u}")
            for t in range(PACK):
                dst = slopes[u][:].rearrange("p (c t i) -> p c t i", t=PACK, i=LINE)[:, :, t, :]
                src = squares[u, t // 2][:, t % 2, :].rearrange("p (c i) -> p c i", i=LINE)
                if engine is not None:
                    engine.tensor_scalar(dst, src, -0.25, scale_of(u, t, ts_cols), ALU.add, ALU.mult)
                else:
                    nc.scalar.activation(dst, src, ACT.Identity, bias=scale_of(u, t, ts_quarter), scale=scale_of(u, t, ts_cols))

        def weigh_targets(k, engine):
            u, j = divmod(k, TILES)
            targets[k] = placed([P, N], F32, f"tg{k}")
            engine.tensor_scalar(
                targets[k][:].rearrange("p (t q i) -> p q t i", t=PACK, i=LINE),
                y_raw[u][:, j, :].rearrange("p (q i t) -> p q t i", t=PACK, i=LINE),
                wt_cols[:, k : k + 1],
                0.0,
                ALU.mult,
                ALU.add,
            )

        def turn_probs(k, new_bank):
            u, j = divmod(k, TILES)
            turned = turned_probs[k] = new_bank()
            for t in reversed(range(PACK)):
                nc.tensor.transpose(turned[:, t * P : (t + 1) * P], probs[u][:, t, j * P : (j + 1) * P], ident[:])

        def miss(k):
            turned = turned_probs[k]
            weighted = work.tile([P, N], F32, name="weighted")
            nc.vector.scalar_tensor_tensor(weighted[:], turned[:], wt_minus[:, k : k + 1], targets[k][:], ALU.mult, ALU.add)
            misses[k] = miss_banks.tile([P, BANK], F32, name="turned_miss")
            for t in range(PACK):
                nc.tensor.transpose(misses[k][:, t * P : (t + 1) * P], weighted[:, t * P : (t + 1) * P], ident[:])

        def gradient(k):
            u, j = divmod(k, TILES)
            if j == 0:
                hs[u] = placed([P, ROWS * PACK], BF16, f"h{u}")
            nc.vector.tensor_tensor(
                hs[u][:, j * BANK : (j + 1) * BANK].rearrange("p (c i t) -> p c t i", t=PACK, i=LINE),
                misses[k][:].rearrange("p (t c i) -> p c t i", t=PACK, i=LINE),
                slopes[u][:, j * BANK : (j + 1) * BANK].rearrange("p (c t i) -> p c t i", t=PACK, i=LINE),
                ALU.mult,
            )

        def quantise_h(first, tiles):
            u, j = divmod(first, TILES)
            codes, scales = quantise(hs[u][:, j * BANK : (j + tiles) * BANK], tiles * P, E5M2, f"hq{first}")
            for k in range(tiles):
                h_mx[first + k] = codes[:, k * P : (k + 1) * P], scales[:, k * P : (k + 1) * P]

        def multiply(k, out_cols, a, cols):
            h_codes, h_scales = h_mx[k]
            w_codes, w_scales = w_slot_mx[a]
            nc.tensor.matmul_mx(
                out=out_cols,
                lhsT=h_codes.bitcast(E5M2),
                lhsT_scale=h_scales,
                rhs=w_codes[:, cols].bitcast(E4M3),
                rhs_scale=w_scales[:, cols],
                start=True,
                stop=True,
            )

        def result(k, new_bank):
            u = k // TILES
            bank = results[k] = new_bank()
            for a in range(2):
                multiply(k, bank[:, a * D // 2 : (a + 1) * D // 2], a, slice(group(u) * D // 2, (group(u) + 1) * D // 2))

        def store(k, copy):
            u, j = divmod(k, TILES)
            bank = results[k]
            if j == 0:
                staged[u] = placed([P, TILES, D], F32, f"st{u}")
            copy(
                staged[u][:, j, :].rearrange("n (p t) -> n p t", t=PACK),
                bank[:].rearrange("n (t p) -> n p t", t=PACK),
            )
            first = rows_of(u).start + j * P
            nc.sync.dma_start(out[group(u), first : first + P, :], staged[u][:, j, :])

        staged, results, turned_probs, scored = {}, {}, {}, {}
        spare = lambda: product_bank(1)
        score = lambda: product_bank(0)
        prob = lambda: prob_banks.tile([P, BANK], F32, name="turned_prob")
        missb = lambda: miss_banks.tile([P, BANK], F32, name="turned_miss")
        V, S, G = nc.vector, nc.scalar, nc.gpsimd

        gather(0, 0, VECTOR_SHARE[0], True); gather(0, VECTOR_SHARE[0], B * N, False); turn_plane(0, spare, S.copy)
        gather(1, 0, VECTOR_SHARE[1], True); gather(1, VECTOR_SHARE[1], B * N, False); turn_plane(1, spare, S.copy)
        gather(2, 0, VECTOR_SHARE[2], True); gather(2, VECTOR_SHARE[2], B * N, False)
        gather(3, 0, LAST_SHARE[0], True); gather(3, LAST_SHARE[0], N, False); gather(3, N, N + LAST_SHARE[1], True); gather(3, N + LAST_SHARE[1], B * N, False)
        weave_w(0, 0); weave_w(0, 1); quantise_w(0, 2)
        weave_x(0, S.copy); ts_cols, wt_cols, wt_minus, ts_quarter = columns(); quantise_x(0)
        weave_x(1, S.copy); scores(0); sigmoids(0); square(0)
        weave_w(1, 0); weave_w(1, 1); quantise_x(1); quantise_w(1, 1); weave_x(2, V.tensor_copy); weigh_targets(0, V); weigh_targets(1, V); quantise_x(2)
        weigh_targets(2, G)
        turn_probs(0, prob); miss(0); turn_probs(1, prob); miss(1); scores(1); sigmoids(1); weave_x(3, S.copy)
        slope(0, V); quantise_by_slot(0)
        weigh_targets(3, G); weigh_targets(4, G)
        gradient(0); gradient(1); square(1); turn_probs(2, prob); miss(2); turn_probs(3, prob); miss(3); scores(2); sigmoids(2); turn_plane(2, spare, S.copy); turn_plane(3, spare, S.copy)
        quantise_x(3); slope(1, V); quantise_h(0, 2)
        weigh_targets(5, G); weigh_targets(6, G)
        gradient(2); gradient(3); square(2); turn_probs(4, prob); miss(4); turn_probs(5, prob); miss(5); scores(3); sigmoids(3)
        quantise_by_slot(1); slope(2, V); quantise_h(2, 2)
        weigh_targets(7, G)
        gradient(4); square(3); slope(3, None); turn_probs(6, prob); miss(6); gradient(5); turn_probs(7, prob); miss(7)
        quantise_h(4, 2)
        gradient(6); gradient(7); quantise_h(6, 1); quantise_h(7, 1)
        result(0, spare); result(1, spare); store(0, S.copy); store(1, S.copy)
        result(2, score); result(3, score); store(2, S.copy); store(3, S.copy)
        result(4, prob); result(5, prob); store(4, S.copy); store(5, S.copy)
        result(6, missb); store(6, S.copy); result(7, missb); store(7, V.tensor_copy)
